import numpy as np, ml_dtypes
CORES = [10,34,74,98]
N = 4
BF = ml_dtypes.bfloat16
W, C, H, CAP, RO = 4096, 1024, 1024, 64, 4
L = C >> 2
S16 = np.arange(16)
def owner(m):
    mb = np.zeros((8, W + 1), np.int32); mb[np.arange(8)[:, None, None], m] = np.arange(C)[None, :, None]
    return mb[:, :W]
def tight(m):
    return np.take_along_axis(m, np.argsort(m >= W, axis=-1, kind="stable"), -1)
def pick(a, j):
    return np.take_along_axis(a, j[:, :, None], 2)[:, :, 0]
def fill(n, order, s):
    s = np.minimum(s, 16 - n[order]); c = np.add.accumulate(s); left = W - np.add.reduce(n); n = n.copy()
    n[order] = n[order] + np.clip(left - (c - s), 0, s)
    return n
def sizes(rng):
    a = (W // C) * rng.choice(np.array([0.5, 1.0, 1.5]))
    n = fill(np.zeros(C, np.int64), rng.permutation(C), 1 + rng.poisson(a, C))
    return fill(n, rng.permutation(C), np.full(C, 16))
def seat(rng, n):
    m = np.full((C, 16), W, np.int64); m[S16 < n[:, None]] = rng.permutation(W)
    return m
def seats(rng):
    return np.stack([np.stack([seat(rng, sizes(rng)) for g in range(8)]) for q in range(N)])
def people(rng, m):
    typ = rng.integers(0, 16, (8, 24, 16)); own = np.take_along_axis(rng.integers(0, 24, (8, C)), owner(m), 1)
    ty = np.where(rng.random((8, W)) < rng.choice(np.array([0.3, 0.7, 0.95]), (8, 1)), own, rng.integers(0, 24, (8, W)))
    v = typ[np.arange(8)[:, None], ty]
    return np.clip(v + rng.integers(-3, 4, (8, W, 16)), 0, 15)
def wrap(x, a, m, li, w):
    def turn(v): return np.ascontiguousarray(v.transpose(0, 1, 3, 2)).reshape(N, 128, -1)
    return {"x0": turn(x).astype(np.float32).astype(BF), "ac": turn(a).astype(np.int32), "ml": turn(m).astype(np.int32),
            "lims": np.repeat(li, 16, axis=1).astype(np.int32), "wt": w.reshape(N, 128, 1).astype(np.int32)}
def setup_inputs(rng):
    m = seats(rng); x = np.stack([people(rng, b) for b in m])
    li = np.stack([rng.integers(30, 130, (N, 8)), rng.integers(20, 110, (N, 8))], axis=2)
    return wrap(x, rng.integers(0, W, (N, 8, H, 16)), m, li, rng.integers(0, 256, (N, 8, 16)))
def setup_inputs_ends(rng):
    ms, xs, as_, ls = [], [], [], []
    for q in range(N):
        m = []
        for g in range(8):
            n = np.zeros(C, np.int64); n[:4] = 16; n[C - 4:] = 16; o = 4 + rng.permutation(C - 8)
            n = fill(n, o, rng.choice(np.array([1, 1, 1, 16, 16, 8]), C - 8)); n = fill(n, o, np.full(C - 8, 16)); b = seat(rng, n)
            c = C - 4 + (g + q) % 4
            for v, k in ((0, 0), (W - 1, 15)):
                at = np.argwhere(b == v)[0]; b[at[0], at[1]] = b[c, k]; b[c, k] = v
            m.append(b)
        m = np.stack(m); ty = rng.integers(0, 5, (8, C, 1, 1)); ty[:, :4] = 4; ty[:, C - 4:] = 4
        edge = ((S16 != 2) & (S16 != 15))[None, None, :, None]
        val = np.where(ty == 0, True, np.where(ty == 1, False, np.where(ty == 2, rng.random((8, C, 16, 1)) < 0.5, np.where(ty == 3, rng.random((8, C, 16, 16)) < 0.5, edge))))
        x = np.zeros((8, W + 1, 16), np.int64); x[np.arange(8)[:, None, None], m] = 15 * val
        far = rng.random((8, H, 16)) < np.where(rng.random((8, H, 1)) < 0.4, 1.1, 0.55)
        ms.append(m); xs.append(x[:, :W]); as_.append(np.where(far, (W - 1) * rng.integers(0, 2, (8, H, 16)), rng.integers(0, W, (8, H, 16))))
        ls.append(np.array([[0, 0], [0, 240], [240, 0], [240, 240]])[(np.arange(8) // 2 + q) % 4])
    w = 255 * rng.integers(0, 2, (N, 8, 16)); w[:, 3::4] = 255; w[:, 1] = 0
    return wrap(np.stack(xs), np.stack(as_), np.stack(ms), np.stack(ls), w)
def setup_inputs_corners(rng):
    ms, xs, as_, ls = [], [], [], []
    for q in range(N):
        m = []; l = []; x = rng.integers(0, 16, (8, W, 16))
        for g in range(8):
            k = (g + q) & 7; n = np.zeros(C, np.int64); o = rng.permutation(C); z = 4 * rng.permutation(L); u = o[(o & 3) != 0]
            if k < 2:
                n[z[:CAP + k]] = 16; n = fill(n, u, rng.choice(np.array([1, 4, 8, 16]), len(u))); n = fill(n, u, np.full(len(u), 16))
            elif k == 2: n[:] = W // C
            elif k == 3:
                n[:] = W // C; n[o[:3]] = 0; n[o[3:6]] = 2 * (W // C)
            elif k == 4:
                n[z[:L // 2]] = 8; n = fill(n, u, rng.choice(np.array([8, 9]), len(u)))
            elif k == 5: n = fill(n, o, np.full(C, 16))
            elif k == 6:
                n[z] = 1; n = fill(n, u, rng.choice(np.array([15, 16]), len(u)))
            else:
                n = sizes(rng); x[g] = rng.integers(0, 2, (W, 16))
            m.append(seat(rng, n)); l.append(((0, 240), (0, 240), (240, 0), (0, 0), (240, 240), (240, 0), (240, 0), (int(rng.integers(2, 14)), int(rng.integers(2, 9))))[k])
        m = np.stack(m); mb = owner(m); mode = rng.integers(0, 6, (8, H, 1)); a = rng.integers(0, W, (8, H, 16)); zero = []
        for g in range(8):
            c0 = np.nonzero((mb[g] & 3) == 0)[0]
            if len(c0) == 0: c0 = np.arange(W)
            zero.append(c0[rng.integers(0, len(c0), (H, 16))])
        a = np.where(mode == 1, a[:, :, :1], np.where(mode == 2, (W - 1) * rng.integers(0, 2, (8, H, 16)), np.where(mode == 3, np.arange(H)[None, :, None] + H * rng.integers(0, W // H, (8, H, 16)),
            np.where(mode == 4, np.stack(zero), np.where(mode == 5, a[:, :, S16 & 1], a)))))
        ms.append(m); xs.append(x); as_.append(a); ls.append(np.array(l))
    w = np.where(rng.random((N, 8, 16)) < 0.5, rng.integers(0, 256, (N, 8, 16)), rng.choice(np.array([0, 1, 255]), (N, 8, 16)))
    return wrap(np.stack(xs), np.stack(as_), np.stack(ms), np.stack(ls), w)
def setup_inputs_brim(rng):
    ms, xs, as_, ls = [], [], [], []
    for q in range(N):
        m = []; l = []; x = rng.integers(0, 16, (8, W, 16)); a = rng.integers(0, W, (8, H, 16))
        for g in range(8):
            k = (g + q) & 3; n = np.zeros(C, np.int64); o = rng.permutation(C); z = 4 * rng.permutation(L); u = o[(o & 3) != 0][:L]
            if k == 1:
                n[z] = 1; n[u] = 2; n = fill(n, o, rng.choice(np.array([0, 2, 4, 6]), C)); n = fill(n, o, 8 - n[o])
            else:
                n[z] = 4; n = fill(n, rng.permutation(np.concatenate([z, u])), rng.choice(np.array([0, 1, 4, 8, 12]), 2 * L)); n = fill(n, rng.permutation(z), np.full(L, 12))
            b = seat(rng, n)
            if k == 1:
                old = b[z, rng.integers(0, n[z])]; h = rng.permutation(H)[:L]; new = h + H * rng.integers(0, W // H, L); p = np.full(W + 1, W)
                p[old] = new; p[np.setdiff1d(np.arange(W), old)] = rng.permutation(np.setdiff1d(np.arange(W), new)); b = p[b]
                x[g] = rng.integers(1, 16, (W, 16)); x[g, new] = 0
                x[g, b[u, 0]] = np.where(S16 == rng.integers(0, 16, (L, 1)), 0, 12); x[g, b[u, 1]] = np.where(S16 == rng.integers(0, 16, (L, 1)), 1, 12)
                a[g, h] = np.where((rng.random((L, 16)) < 0.25) & (S16 > 1), new[rng.integers(0, L, (L, 16))], np.where((S16 & 1) == 1, b[u, 0][:, None], b[np.roll(u, -1), 1][:, None]))
            elif k == 2:
                p = np.argsort(rng.random((L, 16)), axis=1); j = np.argsort(rng.random((L, 4)), axis=1); x[g] = rng.integers(1, 10, (W, 16))
                x[g, b[z, j[:, 0]]] = 0; x[g, b[z, j[:, 1]]] = np.where(p < 10, 15, np.where(p == 10, 1, 0)); x[g, b[z, j[:, 2]]] = np.where(p >= 6, 15, np.where(p < 2, 1, 0))
            elif k == 3:
                ty = rng.integers(0, 3, (W, 1)); x[g] = np.where(ty == 0, 15, np.where((ty == 1) & (S16 == rng.integers(0, 16, (W, 1))), 1, 0))
            m.append(b); l.append(((0, 0), (240, 0), (0, 0), (0, 239 + (g >> 2)))[k])
        ms.append(np.stack(m)); xs.append(x); as_.append(a); ls.append(np.array(l))
    return wrap(np.stack(xs), np.stack(as_), np.stack(ms), np.stack(ls), rng.integers(0, 256, (N, 8, 16)))
def setup_inputs_ties(rng):
    m = seats(rng); two = np.array([[0, 1], [7, 8], [0, 15], [3, 6]])[(np.arange(8)[None, :] + np.arange(N)[:, None]) & 3]
    pool = rng.integers(0, 2, (N, 8, 12, 16)); pool = np.where(pool == 1, two[:, :, None, 1:], two[:, :, None, :1])
    kind = rng.integers(0, 12, (N, 8, W)); x = pool[np.arange(N)[:, None, None], np.arange(8)[None, :, None], kind]
    step = two[:, :, 1] - two[:, :, 0]; li = np.stack([step * rng.integers(5, 14, (N, 8)), step * rng.integers(3, 11, (N, 8))], axis=2)
    known = rng.integers(0, W, (N, 8, 40)); k = rng.integers(0, 40, (N, 8, H * 16))
    a = np.where(rng.random((N, 8, H, 1)) < 0.5, np.take_along_axis(known, k, 2).reshape(N, 8, H, 16), rng.integers(0, W, (N, 8, H, 16)))
    return wrap(x, a, m, np.minimum(li, 240), rng.integers(0, 256, (N, 8, 16)))
def setup_inputs_spread(rng):
    x = rng.integers(0, 2 ** rng.integers(0, 5, (N, 8, W, 1)), (N, 8, W, 16)); m = []
    for q in range(N):
        for g in range(8):
            n = fill(np.zeros(C, np.int64), rng.permutation(C), rng.choice(np.array([0, 1, 1, 2, 3, 5, 16]), C)); m.append(seat(rng, fill(n, rng.permutation(C), np.full(C, 16))))
    a = np.minimum((W * rng.random((N, 8, H, 16)) ** 3).astype(np.int64), W - 1); w = np.minimum((np.exp2(8 * rng.random((N, 8, 16))) - 1).astype(np.int64), 255)
    return wrap(x, a, np.stack(m).reshape(N, 8, C, 16), rng.integers(0, 241, (N, 8, 2)), w)
def check_inputs(d):
    bad = []
    for k, lo, hi in (("x0", 0, 15), ("ac", 0, W - 1), ("ml", 0, W), ("lims", 0, 240), ("wt", 0, 255)):
        a = np.asarray(d[k]).astype(np.float64)
        if not (np.min(a) >= lo and np.max(a) <= hi): bad.append("range of " + k)
    a = np.asarray(d["x0"]).astype(np.float64)
    if np.any(a != np.floor(a)): bad.append("whole numbers in x0")
    m = np.asarray(d["ml"]).astype(np.int64).reshape(N, 8, 16, C)
    if np.any(np.sort(m.reshape(N, 8, 16 * C), axis=-1) != np.minimum(np.arange(16 * C), W)): bad.append("every agent once in ml")
    if np.any((m[:, :, 1:] < W) & (m[:, :, :-1] >= W)): bad.append("members before empty slots in ml")
    l = np.asarray(d["lims"]).reshape(N, 8, 16, 2)
    if np.any(l != l[:, :, :1]): bad.append("lims alike in a group")
    return bad
def reference(x0, ac, ml, lims, wt):
    X = np.zeros((N, 8, W + 1, 16), np.int32)
    X[:, :, :W] = x0.astype(np.float32).astype(np.int32).reshape(N, 8, 16, W).transpose(0, 1, 3, 2)
    A = ac.reshape(N, 8, 16, H).transpose(0, 1, 3, 2); M = np.array(ml.reshape(N, 8, 16, C).transpose(0, 1, 3, 2))
    lim = lims.reshape(N, 8, 16, 2)[:, :, 0].astype(np.int64); wv = wt.reshape(N, 8, 16).astype(np.int64)
    G = np.arange(8)[:, None]; G3 = G[:, :, None]; low = np.tri(L, L, -1, dtype=bool); z = np.zeros(N, np.int64)
    for t in range(RO):
        cl = t & 3; lane = 4 * np.arange(L) + cl; M2 = M.copy(); X2 = X.copy(); z2 = np.zeros(N, np.int64); go = []
        for r in range(N):
            x, m, mb = X[r], M[r], owner(M[r])
            own = m[:, lane]; here = own < W; live = here[:, :, 0]; tx = x[G3, own]; U = np.max(tx, axis=2)
            gr = np.where(here, np.sum(U[:, :, None] - tx, axis=3), -1); s = pick(own, np.argmax(gr, axis=2)); xs = x[G, s]
            ds = np.where(here, np.sum((tx - xs[:, :, None]) ** 2, axis=3), -1)
            an = A[r][G, s & (H - 1)]; ad = mb[G3, an]; fit = live[:, :, None] & ((ad & 3) != cl); has = np.any(fit, axis=2)
            d = pick(ad, np.argmin(np.where(fit, np.sum((x[G3, an] - xs[:, :, None]) ** 2, axis=3), 2 ** 20), axis=2))
            first = ~np.any((d[:, :, None] == d[:, None, :]) & has[:, None, :] & low, axis=2)
            dm = m[G, d]; dh = dm < W; td = x[G3, dm]; V = np.maximum(U, np.max(td, axis=2))[:, :, None]
            worst = np.maximum(np.max(np.where(here, np.sum(V - tx, axis=3), 0), axis=2), np.max(np.where(dh, np.sum(V - td, axis=3), 0), axis=2))
            mer = has & first & (np.sum(here, axis=2) + np.sum(dh, axis=2) <= 16) & (worst <= lim[r, :, :1] + (z[r] & 15))
            want = live & ~mer & (np.max(gr, axis=2) > lim[r, :, 1:])
            xg = x[G, pick(own, np.argmax(ds, axis=2))]; away = here & (np.sum((tx - xg[:, :, None]) ** 2, axis=3) < ds)
            vacant = m[:, :, 0] >= W; free = np.argsort(~vacant, axis=1, kind="stable")
            k = np.add.accumulate(want.astype(np.int64), axis=1) - want.astype(np.int64)
            spl = want & (k < np.sum(vacant, axis=1)[:, None]); e = np.take_along_axis(free, k, 1)
            both = tight(np.concatenate([own, dm], axis=2))[:, :, :16]
            M2[r][:, lane] = np.where(mer[:, :, None], both, np.where(spl[:, :, None], tight(np.where(away, W, own)), own))
            a, b = np.nonzero(mer); M2[r][a, d[a, b]] = W
            a, b = np.nonzero(spl); M2[r][a, e[a, b]] = tight(np.where(away, own, W))[a, b]
            idle = live & ~mer & ~spl; a, b = np.nonzero(idle & (np.add.accumulate(idle.astype(np.int64), axis=1) <= CAP))
            go.append((a, s[a, b], xs[a, b])); z2[r] = np.sum(mer)
        for r in range(N):
            q = (r + 1 + t % (N - 1)) % N; a, sa, xa = go[r]
            v = np.sum(wv[q][a] * xa, axis=1) & (W - 1); mm = M2[q][a, owner(M2[q])[a, v]]; y = X[q][a[:, None], mm]
            j = np.argmin(np.where(mm < W, np.sum((y - xa[:, None]) ** 2, axis=2), 2 ** 20), axis=1)
            X2[r][a, sa] = (xa + y[np.arange(len(a)), j]) >> 1
        X, M, z = X2, M2, z2
    return {"ym": np.ascontiguousarray(M.transpose(0, 1, 3, 2)).reshape(N, 128, C).astype(np.float32),
            "yx": np.ascontiguousarray(X[:, :, :W].transpose(0, 1, 3, 2)).reshape(N, 128, W).astype(np.float32).astype(BF)}

@@ -1,0 +1,734 @@
+from concourse.mybir import AluOpType as A, ActivationFunctionType as F, AxisListType
+AX = AxisListType.X
+
+NX = 4368
+NO = 8576
+NE = 2064
+D0 = 4352
+BIG = float(2 ** 20)
+
+
+def _sb(spec):
+    d = {}
+    for dtype, names in spec.items():
+        for x in names.split():
+            k, w = x.split(":")
+            d[k] = ("sbuf", [128] + [int(v) for v in w.split("x")], dtype)
+    return d
+
+
+SCRATCH = _sb({
+    "bfloat16": "X:4368 TB:3344 TX:4096 US:4096 XE:4096 SQO:4096 SQ:4096 XA:4096 OWG:4096 RM:4096 ONEB:128 IDB:128 NID:128 "
+                "IDV:128 BO:128 G16:8 G64:8 GM1:8 GS0:8 GC:64 BM:256 ROW:1792 WQ:2048 WT:2048 TRI:128 TRJ:128 RW1:512 RW2:512 "
+                "IND:1024 XS:256 SB:64 OCB:64 CF:768 XB:256 VM:256 TG:256 PRS:512 E2:512 THB:512 "
+                "VS:336 XVE:1024 XVS:1024 VD:1024 OVG:64 RET:64",
+    "float32": "OW:8576 ML:1280 VAL:4096 ONE:128 IDF:128 IDK:128 GS0F:8 QM:1024 RB:8 IXA:8x32 IXB:8x32 DUM:256 CO:256 CI:64 "
+               "LMF:8 LIM:64 K1:256 KM:256 KB:256 KD:256 E1:1024 EM:1024 EX:256 EQ:256 DS:256 SM:1024 TH:512 MD:256 W:16x32 "
+               "H3:16x32 F1:16x16 F2:16x16",
+    "int32": "AC:4368 MI:1024 QI:1280 LMI:2 WTI:1 SI:256",
+    "uint16": "OFO:256 ACO:256 OFD:256 MVO:256 LST:512 HL:64"})
+for _t in range(4):
+    SCRATCH["XV%d" % _t] = ("sbuf", [128, 64], "bfloat16")
+    SCRATCH["ME%d" % _t] = ("sbuf", [128, 336], "bfloat16")
+for _b in range(8):
+    SCRATCH["B%d" % _b] = ("psum", [128, 512], "float32")
+SHARE = {"SQB": "SQ", "XSE": "SQ", "THC": "CF", "NX1": "VM", "INDD": "TG", "TD": "XA", "UD": "OWG", "FS": "TH", "KA": "K1", "MSD": "KM", "L2": "MD", "ZI": "QI", "SQV": "XVE"}
+WIDTH = {k: v[1][1] for k, v in SCRATCH.items()}
+WIDTH.update({"SQB": 4096, "XSE": 4096, "THC": 512, "NX1": 256, "INDD": 256, "TD": 4096, "UD": 4096, "FS": 512, "KA": 256, "MSD": 256, "L2": 256, "ZI": 512, "SQV": 1024})
+SEMAPHORES = ["v", "s", "p", "gg", "dx", "da", "dm", "dl", "dw", "oy", "ox"] + ["%s%d" % (a, b) for a in ("va", "vl", "ra", "rl") for b in range(4)]
+PSUM = ["B%d" % b for b in range(8)]
+SIZE = {"float32": 4, "int32": 4, "bfloat16": 2, "uint16": 2}
+
+
+def rank_program(g, core, T, topo):
+    rank = T.rank_of(core)
+    if rank is None:
+        return
+    n = len(T.cores)
+    queue = {"v": g.vector, "s": g.scalar, "p": g.tensor, "gg": g, "y": g.sync}
+    count = {}
+    known = {q: {} for q in queue}
+    clock = {}
+    log = {}
+
+    def R(b, lo=0, hi=None, st=1, p0=0, p1=128):
+        hi = WIDTH[b] if hi is None else min(hi, WIDTH[b])
+        b = SHARE.get(b, b)
+        full = p0 == 0 and p1 == 128
+        ap = T[b][:, lo:hi:st] if full else T[b][p0:p1, lo:hi:st]
+        return (ap, [(b, lo, hi, st)])
+
+    def R3(b, a0, a1, k0, k1):
+        s = SCRATCH[b][1][2]
+        return (T[b][:, a0:a1, k0:k1], [(b, a0 * s, a1 * s, 1)])
+
+    def I(b, lo, hi, ob, o0, o1):
+        b, ob = SHARE.get(b, b), SHARE.get(ob, ob)
+        return (T[b][:, lo:hi].indirect(T[ob][:, o0:o1]), [(b, lo, hi, 1), (ob, o0, o1, 1)])
+
+    def need(q, reads, writes, dma=False):
+        out = []
+        for regs, w in ((reads, False), (writes, True)):
+            for (b, lo, hi, st) in regs:
+                ps = b in PSUM
+                if dma and w:
+                    al = 16 // SIZE[SCRATCH[b][2]]
+                    lo, hi, st = lo // al * al, -(-hi // al) * al, 1
+                for (l2, h2, s2, w2, e, c, d2) in log.get(b, []):
+                    if ps:
+                        if e == q and (q == "p" or not (w or w2) or lo >= h2 or l2 >= hi):
+                            continue
+                    else:
+                        if not (w or w2):
+                            continue
+                        if d2 and w2 and w:
+                            al = 16 // SIZE[SCRATCH[b][2]]
+                            l2, h2, s2 = l2 // al * al, -(-h2 // al) * al, 1
+                        if lo >= h2 or l2 >= hi or (st == s2 and st > 1 and (lo - l2) % st):
+                            continue
+                    out.append((e, c))
+        best = {}
+        for e, c in out:
+            best[e] = max(best.get(e, 0), c)
+        for e, c in sorted(best.items(), key=lambda x: -x[1]):
+            if known[q].get(e, 0) < c:
+                queue[q].wait_ge(T.sem[e], c)
+                for k, v in clock[(e, c)].items():
+                    known[q][k] = max(known[q].get(k, 0), v)
+
+    def done(q, e, inc, reads, writes, dma=False):
+        count[e] = count.get(e, 0) + inc
+        c = count[e]
+        ck = dict(known[q])
+        ck[e] = c
+        clock[(e, c)] = ck
+        for (b, lo, hi, st) in writes:
+            keep = [r for r in log.get(b, []) if not (b not in PSUM and st == 1 and lo <= r[0] and r[1] <= hi)]
+            log[b] = keep + [(lo, hi, st, True, e, c, dma)]
+        for (b, lo, hi, st) in reads:
+            l = log.setdefault(b, [])
+            l[:] = [r for r in l if not (r[:4] == (lo, hi, st, False) and r[4] == e)]
+            l.append((lo, hi, st, False, e, c, dma))
+        for b in set(x[0] for x in reads + writes if x[0] in PSUM):
+            if len(log[b]) > 60:
+                m = {}
+                for r in log[b]:
+                    k = (r[4], r[3])
+                    o = m.get(k)
+                    m[k] = r if o is None else (min(o[0], r[0]), max(o[1], r[1]), 1, r[3], r[4], max(o[5], r[5]), r[6])
+                log[b] = list(m.values())
+
+    def op(q, f, out, ins):
+        rd = [x for i in ins if isinstance(i, tuple) for x in i[1]]
+        wr = list(out[1])
+        if len(wr) > 1:
+            rd = rd + wr[1:]
+            wr = wr[:1]
+        need(q, rd, wr)
+        f().then_inc(T.sem[q], 1)
+        done(q, q, 1, rd, wr)
+
+    def ap(x):
+        return x[0] if isinstance(x, tuple) else x
+
+    def tc(o, i):
+        op("v", lambda: g.vector.tensor_copy(o[0], i[0]), o, [i])
+
+    def tt(o, a, b, f):
+        op("v", lambda: g.vector.tensor_tensor(o[0], a[0], b[0], f), o, [a, b])
+
+    def ts(o, a, s1, f1, s2=None, f2=None):
+        if f2 is None:
+            op("v", lambda: g.vector.tensor_scalar(o[0], a[0], ap(s1), None, f1), o, [a, s1])
+        else:
+            op("v", lambda: g.vector.tensor_scalar(o[0], a[0], ap(s1), ap(s2), f1, f2), o, [a, s1, s2])
+
+    def ms(o, c):
+        op("v", lambda: g.vector.memset(o[0], c), o, [])
+
+    def scan(o, d0, d1, f0, f1):
+        op("v", lambda: g.vector.tensor_tensor_scan(o[0], d0[0], d1[0], 0.0, f0, f1), o, [d0, d1])
+
+    def addup(o, i):
+        op("v", lambda: g.vector.tensor_reduce(o[0], i[0], AX, A.add), o, [i])
+
+    def act(o, i, f):
+        op("s", lambda: g.scalar.activation(o[0], i[0], f), o, [i])
+
+    def mm(o, l, r, a, z):
+        op("p", lambda: g.tensor.matmul(o[0], l[0], r[0], a, z), o, [l, r])
+
+    def aff(o, i, pat, cmp, fill, base, cm):
+        op("gg", lambda: g.affine_select(o[0], i[0], pat, cmp, fill, base, cm), o, [i])
+
+    def iota(o, pat, base, cm):
+        fl = SCRATCH[o[1][0][0]][2] != "int32"
+        op("gg", lambda: g.iota(o[0], pat, base, cm, allow_small_or_imprecise_dtypes=fl), o, [])
+
+    def dma(sem, o_ap, i_ap, reads, writes):
+        need("y", reads, writes, True)
+        g.sync.dma_start(o_ap, i_ap).then_inc(T.sem[sem], 16)
+        done("y", sem, 16, reads, writes, True)
+
+    def send(dst, ob, ib, rs, ls):
+        eng = topo.engines(core, T.cores[dst])[:4]
+        mask = sum(1 << e for e in eng)
+        rid, pid, _se = topo.addr(T.cores[dst])
+        i = R(ib, 0, 64)
+        need("gg", i[1], [])
+        g.remote_dma(T[ob][:, 0:64], i[0], T.sem[rs], T.sem[ls], pid, rid, mask)
+        done("gg", ls, len(eng), i[1], [])
+
+    def arrive(sem, b):
+        count[sem] = 4
+        clock[(sem, 4)] = {sem: 4}
+        log.setdefault(b, []).append((0, 64, 1, True, sem, 4, True))
+
+    def bounded(o, pat, base, cm, width):
+        aff(o, o, pat, A.is_ge, 0.0, base, cm)
+        aff(o, o, [[-s, k] for s, k in pat], A.is_ge, 0.0, width - 1 - base, -cm)
+
+    q_ = lambda k: R("QM", k, k + 1)
+    C = lambda a: R("CO", 16 * a, 16 * a + 16)
+    S = lambda a, w=16: R("SM", 16 * a, 16 * a + w)
+    g8 = R("BO", 0, 128, 16)
+    row = lambda a, w: R("ROW", a, a + w, 1, 0, 1)
+    lone = R("ONEB", 0, 128, 1, 0, 1)
+    one = R("ONE")
+    w2 = lambda: (T.W[:, :, :], [("W", 0, 512, 1)])
+
+    def wrap(cols, bank, ps, keep=None):
+        w = 16 * cols
+        x = keep if keep is not None else R(ps, 0, w)
+        scan(x, R("RM", 0, w), R("E1", 0, w), A.mult, A.add)
+        tt(R("EM", 0, w), x, R("QM", 0, w), A.mult)
+        for h in range(cols // 8):
+            mm(R(bank, 8 * h, 8 * h + 8), R("EM", 128 * h, 128 * h + 128), R("RB"), True, True)
+        return R(bank, 0, cols)
+
+    def wide(bank, lo, order):
+        scan(R("B3"), R("RM", 0, 512), R("E1", 0, 512), A.mult, A.add)
+        scan(R("B7"), R("RM", 0, 512), R("E1", 512, 1024), A.mult, A.add)
+        tt(R("EM", 512, 1024), R("B7"), R("QM", 0, 512), A.mult)
+        tt(R("EM", 0, 512), R("B3"), R("QM", 0, 512), A.mult)
+        for b in order:
+            mm(R(bank, lo + 8 * b, lo + 8 * b + 8), R("EM", 128 * b, 128 * b + 128), R("RB"), True, True)
+        return R(bank, lo, lo + 64)
+
+    def moved(ids, b):
+        ts(R("B1", 0, 256), ids, 0.0, A.is_equal)
+        tt(R("EQ"), R("B1", 0, 256), R("DUM"), A.mult)
+        tt(R("EQ"), R("EQ"), ids, A.add)
+        tc(R(b), R("EQ"))
+
+    def owners(b):
+        mv = ("MVO", "OFD")[b % 2]
+        moved(R("ML", 256 * b, 256 * b + 256), mv)
+        tc(R("XE", 0, 4096, 16), R("TB", NE + 256 * b, NE + 256 * b + 256))
+        settle(mv)
+
+    def settle(mv):
+        for h in range(2):
+            v = R("VAL", 2048 * h, 2048 * h + 2048)
+            scan(v, R("RM", 0, 2048), R("XE", 2048 * h, 2048 * h + 2048), A.mult, A.add)
+            act(I("OW", 0, NO, mv, 128 * h, 128 * h + 128), v, F.Silu)
+
+    mi = R("MI")
+    dma("dm", T.MI[:, :], T.ml[:, :], [], mi[1])
+    ms(R("X", 0, 16), -16.0)
+    ms(R("X", 4096, NX), 0.0)
+    ms(R("AC", 0, 8), 0)
+    ms(R("AC", 4096, NX), 0)
+    dma("dx", T.X[:, 1:4097], T.x0[:, :], [], R("X", 1, 4097)[1])
+    for j in range(4):
+        dma("da", T.AC[:, 1 + 1024 * j:1025 + 1024 * j], T.ac[:, :], [], R("AC", 1 + 1024 * j, 1025 + 1024 * j)[1])
+    log["AC"] = [r[:5] + (64,) + r[6:] if r[4] == "da" else r for r in log["AC"]]
+    dma("dl", T.LMI[:], T.lims[:, :], [], R("LMI")[1])
+    dma("dw", T.WTI[:], T.wt[:, :], [], R("WTI")[1])
+    iota(R("QI", 0, 1024), [[0, 64], [-1, 16]], 1024, 1)
+    iota(R("QI", 1024, 1280), [[1, 256]], 0, 0)
+    iota(R("DUM"), [[16, 256]], D0, 1)
+    ms(R("XE"), 0.0)
+    ms(R("RM"), 1.0)
+    ms(R("RM", 0, 4096, 16), 0.0)
+    ms(R("OW", 0, 16), 128.0)
+    ms(one, 1.0)
+    ts(R("QI", 0, 1024), R("QI", 0, 1024), 15, A.bitwise_and)
+    ts(R("QM"), R("QI", 0, 1024), 0, A.is_equal)
+    ms(R("SM", 4, 6), 0.0)
+    for u in range(4):
+        ts(R("SM", 6, 7), q_(2 + u), float(u), A.mult)
+        tt(R("SM", 4, 5), R("SM", 4, 5), R("SM", 6, 7), A.add)
+        tt(R("SM", 5, 6), R("SM", 5, 6), q_(2 + u), A.add)
+    ci, cj = R("QI", 1024, 1280), R("SI")
+    ts(cj, ci, 7, A.logical_shift_right)
+    ts(R("K1"), cj, q_(0), A.mult, 128.0, A.add)
+    ts(cj, ci, 127, A.bitwise_and)
+    ts(R("KM"), cj, q_(1), A.mult)
+    tt(R("K1"), R("K1"), R("KM"), A.add)
+    ts(cj, ci, 3, A.bitwise_and)
+    ts(R("KM"), cj, R("SM", 4, 5), A.is_equal, R("SM", 5, 6), A.mult)
+    tt(R("TB", NE, NE + 256), R("K1"), R("KM"), A.add)
+    ml = R("ML", 0, 1024)
+    ts(ml, mi, 4096, A.is_equal, -4097, A.mult)
+    tt(ml, ml, mi, A.add)
+    ts(ml, ml, 1, A.add)
+    owners(0)
+    for b in range(1, 5):
+        ts(R("SM", 7, 8), q_(0), 2.0 * b, A.mult)
+        ts(R("TB", NE + 256 * b, NE + 256 * b + 256), R("TB", NE, NE + 256), R("SM", 7, 8), A.add)
+    ms(R("ML", 1024, 1280), 0.0)
+    act(R("IND"), ml, F.Sign)
+    aff(R("IDF"), one, [[-1, 128]], A.is_equal, 0.0, 0, 1)
+    ms(R("TH"), 1.0)
+    for o, w, p in ((0, 128, ([[-16, 8], [0, 16]], 0, 1, 16)), (128, 8, ([[-16, 8]], 0, 1, 16)), (256, 128, ([[1, 128]], -1, -1, 200)),
+                    (384, 128, ([[1, 128]], 0, -1, 200))):
+        bounded(R("TH", o, o + w), *p)
+    tc(R("BO"), R("TH", 0, 128))
+    tc(R("RB"), R("TH", 128, 136))
+    tc(R("TRI"), R("TH", 256, 384))
+    tc(R("TRJ"), R("TH", 384, 512))
+    tc(R("ONEB"), one)
+    tc(R("IDB"), R("IDF"))
+    ts(R("NID"), R("IDF"), -1.0, A.mult)
+    ts(R("IDK"), R("IDF"), 1024.0, A.mult)
+    ts(R("IDV"), R("IDF"), float(2 ** 18), A.mult)
+    for b, c in (("G16", 16.0), ("G64", 65536.0), ("GM1", -1.0)):
+        ts(R(b), g8, c, A.mult)
+    ts(R("GS0"), g8, q_(0), A.mult)
+    ts(R("GS0F"), g8, q_(0), A.mult)
+    for o, pat, base in ((0, [[0, 8], [4096, 16]], 0), (128, [[0, 8], [1, 16]], 0), (256, [[0, 8], [-1, 16]], 15), (512, [[-1, 256]], 0)):
+        w = pat[0][1] * (pat[1][1] if len(pat) > 1 else 1)
+        iota(R("EM", o, o + w), pat, base, 0)
+    tc(R("ROW", 0, 384), R("EM", 0, 384))
+    ms(R("ROW", 384, 512), -1.0)
+    tc(R("ROW", 512, 768), R("EM", 512, 768))
+    ms(w2(), 0.0)
+    ms(R3("W", 0, 16, 16, 32), -1.0)
+    tc(R("ROW", 768, 1280), w2())
+    ms(R("ROW", 1280, 1792), 0.0)
+    for h in range(2):
+        tc(R("ROW", 1280 + 256 * h, 1408 + 256 * h), R("EM", 128, 256))
+    ms(R("BM"), 0.0)
+    ms(R("BM", 0, 256, 16), float(2 ** 25))
+    wc = R("SM", 0, 1)
+    ts(wc, q_(0), 128.0, A.mult)
+    tt(wc, wc, q_(1), A.add)
+    ts(R("SM", 1, 2), q_(6), -129.0, A.mult)
+    tt(wc, wc, R("SM", 1, 2), A.add)
+    for u in range(4):
+        tt(R("SM", 2, 3), q_(2 + u), q_(6), A.subtract)
+        ts(R("GC", 16 * u + 8, 16 * u + 16), g8, wc, A.mult)
+        ts(R("GC", 16 * u, 16 * u + 8), g8, R("SM", 2, 3), A.mult, float(2 ** 17), A.mult)
+    lanes = lambda a, base, s: iota(C(a), [[128 * s, 2], [0, 8]], base, s)
+    lanes(0, 4097, 1)
+    lanes(1, 15, 16)
+    lanes(2, 4096, -1)
+    lanes(3, NE + 1024, 1)
+    lanes(4, 64, 1)
+    iota(C(5), [[0, 16]], 0, 16)
+    for t in range(4):
+        lanes(6 + t, t, 4)
+        lanes(10 + t, t + NE, 4)
+    iota(R("CI"), [[128, 8], [0, 8]], 0, 1)
+    iota(R("SI", 0, 1), [[0, 1]], 0, 1)
+    ms(R("E1"), 0.0)
+    ms(R("WQ"), 1.0)
+    aff(R("WQ"), R("WQ"), [[1, 16], [0, 8], [-1, 16]], A.is_equal, 0.0, 0, 0)
+    bounded(R("WQ"), [[0, 16], [-16, 8], [0, 16]], 0, 1, 16)
+    owners(1)
+
+    def rest():
+        ms(R("TB", 0, NE), 128.0)
+        for b, s in (("RW1", 128), ("RW2", 256)):
+            ms(R(b), 1.0)
+            ms(R(b, 0, 512, s), 0.0)
+        ms(R3("IXA", 0, 8, 16, 32), 0.0)
+        ms(R3("IXB", 0, 8, 0, 16), 0.0)
+        ts(R3("IXA", 0, 8, 0, 16), R("IDF"), 2.0 ** -10, A.mult)
+        ts(R3("IXB", 0, 8, 16, 32), R("IDF"), 2.0 ** -10, A.mult)
+        for k in range(11):
+            ms(R("SM", 16 + k, 17 + k), float(2 ** (10 - k)))
+        ms(R("SM", 27, 32), 0.0)
+        tt(R("SM", 16, 32), R("SM", 16, 32), R("QM", 0, 16), A.mult)
+        addup(R("LMF", 0, 1), R("SM", 16, 32))
+        ts(R("LMF", 2, 3), R("LMF", 1, 2), -1.0, A.mult, 1.0, A.add)
+        for a in (0, 1):
+            ts(R("LMF", 3 + 2 * a, 4 + 2 * a), R("LMF", 1 + a, 2 + a), 1 / 32, A.mult)
+            ts(R("LMF", 4 + 2 * a, 5 + 2 * a), R("LMF", 1 + a, 2 + a), -16.0, A.mult)
+        tc(R("SM", 8, 10), R("LMI"))
+        for j in range(2):
+            ts(R("VM", 0, 128), one, R("SM", 8 + j, 9 + j), A.mult)
+            for h in range(2):
+                mm(R("B2", 16 * j + 8 * h, 16 * j + 8 * h + 8), R("VM", 0, 128), R("GS0"), True, True)
+        tc(R("LIM", 0, 32), R("B2", 0, 32))
+        tc(R("LIM", 32, 48), R("LIM", 0, 16))
+        for b in ("VS", "XVS", "E2"):
+            ms(R(b), 0.0)
+        for u in range(4):
+            ms(R("ME%d" % u, 64, 336), 0.0)
+        tc(R("SM", 3, 4), R("WTI"))
+        ts(R("WT"), R("WQ"), R("SM", 3, 4), A.mult)
+        ts(R("WQ"), R("WQ"), wc, A.mult)
+
+    ts(R("SI", 0, 1), R("SI", 0, 1), 16, A.bitwise_and)
+    ts(R("LMF", 1, 2), R("SI", 0, 1), 16.0, A.is_equal)
+    NN, LIVE, HAS, FM, DD, MS, GR, WAN, SPL, RK, IDL, VIS, T1, T2, RV = range(4, 19)
+    SUU, S1, NV, NM, AA = 20, 21, 22, 23, 24
+
+    def empties():
+        for b in range(8):
+            mm(R("B2", 64 + 8 * b, 72 + 8 * b), R("IND", 128 * b, 128 * b + 128), R("GS0"), True, True)
+        tc(R("OCB"), R("B2", 64, 128))
+        mm(R("B2", 128, 192), R("TRJ"), R("OCB"), True, False)
+        for j in range(1, 8):
+            mm(R("B2", 128 + 8 * j, 192), R("ONEB"), R("OCB", 0, 64 - 8 * j), False, j == 7)
+        for h in range(2):
+            for j in range(8):
+                mm(R("B2", 192 + 8 * h, 200 + 8 * h), R("ONEB"), R("OCB", 8 * j, 8 * j + 8), j == 0, j == 7)
+        u, y = R("SM", 512, 576), R("SM", 576, 640)
+        tt(u, R("CI"), R("B2", 128, 192), A.subtract)
+        ts(S(NV), R("B2", 192, 208), -1.0, A.mult, 1024.0, A.add)
+        tt(y, R("B2", 128, 192), u, A.subtract)
+        ts(y, y, 1024.0, A.add)
+        tt(y, y, R("OCB"), A.mult)
+        tt(R("E1", 0, 1024, 16), y, u, A.add)
+        tc(R("LST", 64, 128), wide("B2", 256, range(8)))
+        tc(I("TB", 0, NE, "LST", 64, 128), R("TB", NE, NE + 1024))
+
+    for t in range(4):
+        cl = t & 3
+        own = lambda h, b="ML": R(b, cl + 512 * h, cl + 512 * h + 512, 4)
+        half = lambda b, h: R(b, 2048 * h, 2048 * h + 2048)
+
+        def squares(out, win, w, bank, kk):
+            for j in range(2):
+                o = R(bank, 256 * j, 256 * j + 256)
+                mm(o, R("IDB"), R(win, 2 * kk + j, 4096, 16), True, False)
+                mm(o, R("NID"), w, False, True)
+            act(R(out, 512 * kk, 512 * kk + 512), R(bank), F.Square)
+        if t == 0:
+            tc(R("OFO"), R("ML", 0, 1024, 4))
+        tc(half("TX", 0), I("X", 0, NX, "OFO", 0, 128))
+        if t == 0:
+            tc(half("TX", 1), I("X", 0, NX, "OFO", 128, 256))
+        else:
+            act(half("TX", 1), I("X", 0, NX, "OFO", 128, 256), F.Copy)
+        for h in range(2):
+            o = R("B0", 128 * h, 128 * h + 128)
+            mm(o, own(h), R("IDF"), True, False)
+            mm(o, lone, row(0, 128), False, False)
+            mm(o, lone, row(384, 128), False, False)
+            for k in range(16):
+                mm(R("B0", 128 * h + k, 128 * h + 128, 16), R("TX", 2048 * h + k, 2048 * h + 2048, 16), R("G64"), False, k == 15)
+        act(R("K1"), R("B0", 0, 256), F.Abs)
+        for h in range(2):
+            mm(R("B2", 8 * h, 8 * h + 8), own(h, "IND"), g8, True, True)
+        scan(half("US", 0), half("RM", 0), half("TX", 0), A.mult, A.max)
+        tc(S(NN), R("B2", 0, 16))
+        ts(S(LIVE), S(NN), 0.0, A.is_gt)
+        scan(R("KM"), R("BM"), R("K1"), A.max, A.min)
+        tc(R("SI", 0, 16), R("KM", 15, 256, 16))
+        ts(R("SI", 16, 32), R("SI", 0, 16), 4095, A.bitwise_and)
+        ts(S(T1), R("SI", 16, 32), 1.0, A.add)
+        tt(S(T1), S(T1), C(0), A.subtract)
+        tt(S(T1), S(T1), S(LIVE), A.mult)
+        tt(R("E1", 0, 256, 16), S(T1), C(0), A.add)
+        w = wrap(16, "B2", "B3")
+        tc(R("LST", 0, 16), w)
+        ts(R("ACO"), I("AC", 0, NX, "LST", 0, 16), 1, A.add)
+        xs = R("XS")
+        tc(xs, I("X", 0, NX, "LST", 0, 16))
+        if t == 0:
+            owners(2)
+        tc(R("XE", 0, 4096, 16), xs)
+        scan(R("XSE"), R("RM"), R("XE"), A.mult, A.add)
+        if t == 0:
+            owners(3)
+        for h in range(2):
+            act(half("OWG", h), I("OW", 0, NO, "ACO", 128 * h, 128 * h + 128), F.Copy)
+        for h in range(2):
+            tt(half("XA", h), I("X", 0, NX, "ACO", 128 * h, 128 * h + 128), half("XSE", h), A.subtract)
+            act(half("XA", h), half("XA", h), F.Square)
+        if t == 0:
+            rest()
+            empties()
+        ts(R("SI", 32, 48), R("SI", 0, 16), 16, A.logical_shift_right)
+        scan(half("US", 1), half("RM", 1), half("TX", 1), A.mult, A.max)
+        for h in range(2):
+            mm(R("B2", 16 + 8 * h, 24 + 8 * h), R("US", 2048 * h + 15, 2048 * h + 2048, 16), g8, True, True)
+        tc(S(SUU), R("B2", 16, 32))
+        mm(R("B0"), lone, row(1280, 512), True, False)
+        for h in range(2):
+            for k in range(16):
+                mm(R("B0", 256 * h + k, 256 * h + 256, 16), R("OWG", 2048 * h + k, 2048 * h + 2048, 16), R("GC", 16 * cl, 16 * cl + 16), False, False)
+        for h in range(2):
+            for k in range(16):
+                mm(R("B0", 256 * h + k, 256 * h + 128, 16), R("XA", 2048 * h + k, 2048 * h + 2048, 16), R("G16"), False, h == 1 and k == 15)
+        for kk in range(5):
+            squares("SQO", "TX", xs, ("B4", "B5")[kk % 2], kk)
+        hv = lambda b, h: R(b, 128 * h, 128 * h + 128)
+        for h in range(2):
+            scan(hv("KD", h), R("BM", 0, 128), R("B0", 256 * h, 256 * h + 128), A.max, A.min)
+        tc(R("E1", 0, 256, 16), R("KD", 15, 256, 16))
+        scan(R("EX"), R("RM", 0, 256), R("E1", 0, 256), A.mult, A.add)
+        for h in range(2):
+            tt(hv("EQ", h), hv("EX", h), R("B0", 256 * h, 256 * h + 128), A.is_equal)
+        for h in range(2):
+            tt(hv("EQ", h), hv("EQ", h), R("B0", 256 * h + 128, 256 * h + 256), A.mult)
+        scan(R("DS"), R("RM", 0, 256), R("EQ"), A.mult, A.add)
+        ts(S(HAS), R("KD", 15, 256, 16), float(2 ** 17), A.is_lt)
+        tt(S(HAS), S(HAS), S(LIVE), A.mult)
+        ts(S(T1), R("DS", 15, 256, 16), float(-cl), A.add)
+        tt(S(T1), S(T1), S(HAS), A.mult)
+        ts(S(DD), S(T1), float(cl), A.add)
+        tc(R("E1", 0, 256, 16), S(DD))
+        w = wrap(16, "B2", "B3", R("EX"))
+        for h in range(2):
+            mm(R("B1", 128 * h, 128 * h + 128), R("EX", 128 * h, 128 * h + 128), R("IDF"), True, True)
+        for kk in range(5, 8):
+            squares("SQO", "TX", xs, ("B4", "B5")[kk % 2], kk)
+        tc(R("LST", 32, 48), w)
+        tc(R("MD"), I("ML", 0, 1280, "LST", 32, 48))
+        tc(R("OFD"), R("MD"))
+        for h in range(2):
+            act(half("TD", h), I("X", 0, NX, "OFD", 128 * h, 128 * h + 128), F.Copy)
+        act(R("INDD"), R("MD"), F.Sign)
+        ts(R("ZI", 0, 256), R("B1", 0, 256), R("LMF", 0, 1), A.mult)
+        ts(R("ZI", 0, 256), R("ZI", 0, 256), 1024, A.bitwise_and)
+        ts(R("CF", 0, 256), R("ZI", 0, 256), 1 / 32, A.mult, -16.0, A.add)
+        ts(R("CF", 256, 512), R("ZI", 0, 256), R("LMF", 5, 6), A.mult, R("LMF", 6, 7), A.add)
+        ts(R("CF", 512, 768), R("ZI", 0, 256), R("LMF", 3, 4), A.mult, R("LMF", 4, 5), A.add)
+        for h in range(2):
+            o = R("B0", 128 * h, 128 * h + 128)
+            mm(o, own(h, "IND"), R("IDV"), True, False)
+            mm(o, lone, row(256, 128), False, False)
+            for k in range(16):
+                mm(R("B0", 128 * h + k, 128 * h + 128, 16), R("SQO", 256 * k + 128 * h, 256 * k + 128 * h + 128), R("G16"), False, k == 15)
+
+        def leave(h, sq, signs, stop):
+            for k in range(16):
+                for f in range(2):
+                    mm(R("B6", 256 * h + 16 * f + k, 256 * h + 256, 32), R(sq, 256 * k + 128 * h, 256 * k + 128 * h + 128), signs[f], False,
+                       stop and h == 1 and k == 15 and f == 1)
+        mm(R("B6"), lone, row(768, 512), True, False)
+        for h in range(2):
+            leave(h, "SQO", (R("GM1"), g8), False)
+
+        def firsts(i, b):
+            if i < 2:
+                h, gs, wd, rw = 0, range(4 * i, 4 * i + 4), 128, "RW1"
+            else:
+                h, gs, wd, rw = 1, range(2 * (i - 2), 2 * (i - 2) + 2), 256, "RW2"
+            for j, gg in enumerate(gs):
+                p0 = 32 * (gg // 2)
+                o = R(b, wd * j, wd * j + wd)
+                if j and p0 != 32 * (gs[j - 1] // 2):
+                    queue["p"].wait_ge(T.sem["p"], count["p"])
+                    known["p"]["p"] = count["p"]
+                mm(o, R("ONEB", 0, 128, 1, p0, p0 + 1), R("ROW", 512, 512 + wd, 1, p0, p0 + 1), True, False)
+                c = 256 + 256 * (gg % 2) + 128 * h
+                mm(o, R("CF", c, c + 128, 1, p0, p0 + 32), R("CF", 0, wd, 1, p0, p0 + 32), False, True)
+            return gs, wd, rw, h, b
+
+        def firsts2(r):
+            gs, wd, rw, h, b = r
+            scan(R("FS"), R(rw), R(b), A.mult, A.max)
+            tc(R("SM", 16 * FM + 8 * h + gs[0], 16 * FM + 8 * h + gs[0] + len(gs)), R("FS", wd - 1, 512, wd))
+        rr = [firsts(i, ("B3", "B7")[i]) for i in range(2)]
+        scan(R("KB"), R("RM", 0, 256), R("B0", 0, 256), A.mult, A.max)
+        tc(R("SI", 48, 64), R("KB", 15, 256, 16))
+        ts(R("SI", 48, 64), R("SI", 48, 64), 15, A.bitwise_and)
+        tt(R("E1", 0, 256, 16), C(1), R("SI", 48, 64), A.subtract)
+        w = wrap(16, "B2", "B1")
+        tc(R("LST", 16, 32), w)
+        tc(R("XB"), I("TX", 0, 4096, "LST", 16, 32))
+        xb = R("XB")
+        for i in range(2):
+            firsts2(rr[i])
+            rr.append(firsts(i + 2, ("B3", "B7")[i]))
+        for i in range(2):
+            firsts2(rr[i + 2])
+            rr.append(firsts(i + 4, ("B3", "B7")[i]))
+        for h in range(2):
+            for k in range(16):
+                mm(R("B0", 128 * h + k, 128 * h + 128, 16), R("TD", 2048 * h + k, 2048 * h + 2048, 16), g8, True, True)
+            mm(R("B1", 8 * h, 8 * h + 8), R("INDD", 128 * h, 128 * h + 128), g8, True, False)
+            mm(R("B1", 8 * h, 8 * h + 8), own(h, "IND"), g8, False, True)
+        act(R("KA"), R("B0", 0, 256), F.Abs)
+
+        for i in range(2):
+            firsts2(rr[i + 4])
+        for h in range(2):
+            scan(half("UD", h), half("RM", h), half("TD", h), A.mult, A.max)
+        tt(R("VM"), R("US", 15, 4096, 16), R("UD", 15, 4096, 16), A.max)
+        for kk in range(2):
+            squares("SQB", "TX", xb, ("B4", "B5")[kk], kk)
+        for h in range(2):
+            mm(R("B1", 16 + 8 * h, 24 + 8 * h), R("VM", 128 * h, 128 * h + 128), g8, True, True)
+        for kk in range(2, 8):
+            squares("SQB", "TX", xb, ("B4", "B5")[kk % 2], kk)
+        scan(R("MSD"), R("BM"), R("KA"), A.max, A.min)
+        tt(S(GR), S(SUU), R("SI", 32, 48), A.subtract)
+        tt(S(GR), S(GR), R("LIM", 16, 32), A.is_gt)
+        tt(S(FM), S(FM), C(2), A.is_equal)
+        tt(S(MS), R("SI", 32, 48), R("MSD", 15, 256, 16), A.min)
+        tt(S(FM), S(FM), S(HAS), A.mult)
+        tt(S(MS), S(MS), R("LIM", 32, 48), A.add)
+        ts(S(T1), R("B1", 0, 16), 16.0, A.is_le)
+        tt(S(T2), R("B1", 16, 32), S(MS), A.is_le)
+        tt(S(FM), S(FM), S(T1), A.mult)
+        mer = R("SB", 0, 16)
+        tt(mer, S(FM), S(T2), A.mult)
+        ts(S(NM), mer, -1.0, A.mult, 1.0, A.add)
+        tt(S(NM), S(NM), S(LIVE), A.mult)
+        want = R("SB", 16, 32)
+        tt(want, S(GR), S(NM), A.mult)
+
+        def ranks(bank, s):
+            mm(R(bank, 0, 8), R("TRI"), R("SB", s, s + 8), True, True)
+            mm(R(bank, 8, 16), R("TRI"), R("SB", s + 8, s + 16), True, False)
+            mm(R(bank, 8, 16), R("ONEB"), R("SB", s, s + 8), False, True)
+        ranks("B1", 16)
+        mm(R("B1", 32, 48), R("ONEB"), mer, True, True)
+        ts(S(T1), S(DD), float(NE), A.add)
+        tt(S(T2), S(DD), C(6 + t), A.subtract)
+        tt(S(T1), S(T1), C(3), A.subtract)
+        tt(S(T2), S(T2), mer, A.mult)
+        tt(S(T1), S(T1), mer, A.mult)
+        tt(R("E1", 512, 768, 16), S(T2), C(6 + t), A.add)
+        tc(S(RK), R("B1", 0, 16))
+        tt(S(SPL), S(RK), S(NV), A.is_lt)
+        tt(S(SPL), S(SPL), want, A.mult)
+        tt(R("SB", 32, 48), S(NM), S(SPL), A.subtract)
+        ranks("B0", 32)
+        for h in range(2):
+            leave(h, "SQB", (g8, R("GM1")), True)
+        tt(S(T2), S(RK), C(3), A.subtract)
+        tt(S(RV), S(RK), C(10 + t), A.subtract)
+        tt(S(T2), S(T2), S(SPL), A.mult)
+        tt(S(RV), S(RV), S(SPL), A.mult)
+        tt(S(T1), S(T1), S(T2), A.add)
+        tt(R("E1", 256, 512, 16), S(RV), C(10 + t), A.add)
+        tt(R("E1", 0, 256, 16), S(T1), C(3), A.add)
+        ts(S(VIS), R("B0", 0, 16), 64.0, A.is_lt)
+        tt(S(T2), R("B0", 0, 16), C(4), A.subtract)
+        tt(S(VIS), S(VIS), R("SB", 32, 48), A.mult)
+        tt(S(T2), S(T2), S(VIS), A.mult)
+        tt(R("E1", 768, 1024, 16), S(T2), C(4), A.add)
+        tc(R("LST", 128, 192), wide("B2", 0, (6, 7, 4, 5, 0, 1, 2, 3)))
+        dst = (rank + 1 + t % (n - 1)) % n
+        src = (rank - 1 - t % (n - 1)) % n
+        tc(I("VS", 0, 336, "LST", 176, 192), xs)
+        send(dst, "XV%d" % t, "VS", "va%d" % t, "vl%d" % t)
+        tc(R("MD"), I("ML", 0, 1280, "LST", 160, 176))
+        for h in range(2):
+            o = R("B7", 256 * h, 256 * h + 256)
+            mm(o, own(h), R3("IXA", 0, 8, 0, 32), True, False)
+            mm(o, R("MD", 128 * h, 128 * h + 128), R3("IXB", 0, 8, 0, 32), False, True)
+        ts(S(T1), mer, -2.0, A.mult, 1.0, A.add)
+        ts(R("E2", 0, 512, 32), S(SPL), -1.0, A.add, BIG, A.mult)
+        tt(S(T1), S(T1), S(SPL), A.subtract)
+        ts(S(AA), S(NN), -1.0, A.mult, 16.0, A.add)
+        ts(R("E2", 16, 512, 32), S(T1), BIG, A.mult)
+        tt(S(AA), S(AA), mer, A.mult)
+        scan(R("THB"), R("RM", 0, 512), R("E2"), A.mult, A.add)
+        tt(R("PRS"), R("B6"), R("THB"), A.is_ge)
+        ts(R("THC"), R("PRS"), -1.0, A.mult, 1.0, A.add)
+        tt(R("THC", 16, 512, 32), R("THC", 16, 512, 32), S(AA), A.add)
+        scan(R("THB"), R("RM", 0, 512), R("THC"), A.mult, A.add)
+        ts(R("ZI"), R("THB"), 4369.0, A.mult)
+        ts(R("ZI"), R("ZI"), 4680, A.bitwise_and)
+        tt(R("B3"), R("ZI"), R("B7"), A.add)
+        tt(w2(), R("B3"), R("PRS"), A.mult)
+        tc(R3("F2", 0, 16, 0, 16), R3("W", 0, 16, 16, 32))
+        for h in range(2):
+            mm(R("B0", 128 * h, 128 * h + 128), R3("F2", 8 * h, 8 * h + 8, 0, 16), R("IDK"), True, True)
+        tc(R("XE", 0, 4096, 16), I("TB", 0, NE + 1280, "LST", 144, 160))
+        tc(R("TG"), I("TB", 0, NE + 1280, "LST", 128, 144))
+        for q in range(16):
+            mm(R("B4", 0, 16), R("WQ", 128 * q, 128 * q + 128), R("TG", q, 256, 16), q == 0, q == 15)
+        if t < 3:
+            addup(R("SM", 400, 401), R("B1", 32, 48))
+        tc(R("SI", 0, 256), R("B0", 0, 256))
+        ts(R("SI", 0, 256), R("SI", 0, 256), 8191, A.bitwise_and)
+        moved(R("SI", 0, 256), "MVO")
+        settle("MVO")
+        tc(R("LST", 48, 64), R("B4", 0, 16))
+        for th, s in ((4096.0, 1), (512.0, 2), (64.0, 4)):
+            ts(R("B5"), w2(), -th, A.mult, th * th, A.add)
+            ts(R("B3"), w2(), -th, A.add, 0.0, A.max)
+            tt(R("TH"), w2(), R("B5"), A.min)
+            ts(R3("W", 15, 16, 24, 32), R("TH", 504, 512), 0.0, A.max)
+            tt(R3("W", 0, 15, 0, 32), R("TH", 0, 480), R("B3", s, 480 + s), A.max)
+            tt(R3("W", 15, 16, 0, 32 - s), R("TH", 480, 512 - s), R("B3", 480 + s, 512), A.max)
+        h3 = lambda a, b: R3("H3", 0, 16, a, b)
+        ts(R("B5"), w2(), -8.0, A.mult, 64.0, A.add)
+        ts(h3(0, 32), w2(), -8.0, A.add, 0.0, A.max)
+        tt(w2(), w2(), R("B5"), A.min)
+        tt(R3("F2", 0, 16, 0, 8), R3("W", 0, 16, 16, 24), h3(24, 32), A.max)
+        ts(R3("F2", 0, 16, 8, 16), R3("W", 0, 16, 24, 32), 0.0, A.max)
+        tt(R3("F1", 0, 16, 0, 16), R3("W", 0, 16, 0, 16), h3(8, 24), A.max)
+        for j, f in ((256, "F2"), (0, "F1")):
+            for h in range(2):
+                mm(R("B7", j + 128 * h, j + 128 * h + 128), R3(f, 8 * h, 8 * h + 8, 0, 16), R("IDK"), True, True)
+        tc(R("L2"), R("B7", 256, 512))
+        tc(R("ML", cl, 1024, 4), R("B7", 0, 256))
+        tc(I("ML", 0, 1280, "LST", 48, 64), R("L2"))
+        if t < 3:
+            act(R("IND"), ml, F.Sign)
+            tc(R("SI", 240, 241), R("SM", 400, 401))
+            ts(R("SI", 240, 241), R("SI", 240, 241), 15, A.bitwise_and)
+            tc(R("SM", 400, 401), R("SI", 240, 241))
+            ts(R("LIM", 32, 48), R("LIM", 0, 16), R("SM", 400, 401), A.add)
+        else:
+            ts(R("E1"), ml, 0.0, A.is_equal, 4097.0, A.mult)
+            tt(R("E1"), R("E1"), ml, A.add)
+            ts(R("E1"), R("E1"), -1.0, A.add)
+            dma("oy", T.ym[:, :], T.E1[:, :], R("E1")[1], [])
+            ms(R("KB"), 0.0)
+        ev = R("E1", 0, 128, 16, 0, 64) if t < 3 else R("KB", 0, 128, 16, 0, 64)
+        ew = R("E1", 0, 128, 1, 0, 64) if t < 3 else R("KB", 0, 128, 1, 0, 64)
+        xv = "XV%d" % t
+        arrive("va%d" % t, xv)
+        for q in range(16):
+            mm(R("B2", 64, 68), R("WT", 128 * q, 128 * q + 128), R(xv, q, 64, 16), q == 0, q == 15)
+        tc(R("SI", 0, 4), R("B2", 64, 68))
+        ts(R("SI", 0, 4), R("SI", 0, 4), 4095, A.bitwise_and)
+        ts(R("LST", 192, 196), R("SI", 0, 4), 1, A.add)
+        tc(R("XVS", 0, 1024, 16), R(xv))
+        scan(R("XVE"), R("RM", 0, 1024), R("XVS"), A.mult, A.add)
+        tc(R("OVG"), I("OW", 0, NO, "LST", 192, 196))
+        for q in range(16):
+            mm(R("B2", 64, 68), R("WQ", 128 * q, 128 * q + 128), R("OVG", q, 64, 16), q == 0, q == 15)
+        tc(R("LST", 200, 204), R("B2", 64, 68))
+        tc(R("HL"), I("ML", 0, 1280, "LST", 200, 204))
+        tt(R("VD"), I("X", 0, NX, "HL", 0, 64), R("XVE"), A.subtract)
+        act(R("SQV"), R("VD"), F.Square)
+        mm(R("B0", 0, 128, 1, 0, 64), R("ONEB", 0, 64, 1, 0, 1), row(128, 128), True, False)
+        for k in range(16):
+            mm(R("B0", k, 128, 16, 0, 64), R("SQV", k, 1024, 16), R("G16"), False, k == 15)
+        scan(R("KD", 0, 128, 1, 0, 64), R("BM", 0, 128, 1, 0, 64), R("B0", 0, 128, 1, 0, 64), A.max, A.min)
+        tc(R("SI", 0, 8, 1, 0, 64), R("KD", 15, 128, 16, 0, 64))
+        ts(R("SI", 0, 8, 1, 0, 64), R("SI", 0, 8, 1, 0, 64), 15, A.bitwise_and)
+        tt(ev, R("SI", 0, 8, 1, 0, 64), R("CO", 80, 88, 1, 0, 64), A.add)
+        scan(R("B3", 0, 128, 1, 0, 64), R("RM", 0, 128, 1, 0, 64), ew, A.mult, A.add)
+        tt(R("EM", 0, 128, 1, 0, 64), R("B3", 0, 128, 1, 0, 64), R("QM", 0, 128, 1, 0, 64), A.mult)
+        mm(R("B2", 64, 68), R("EM", 0, 128, 1, 0, 64), R("RB", 0, 4, 1, 0, 64), True, True)
+        tc(R("LST", 208, 212), R("B2", 64, 68))
+        tc(R("SI", 64, 128), I("VD", 0, 1024, "LST", 208, 212))
+        ts(R("SI", 64, 128), R("SI", 64, 128), 1, A.arith_shift_right)
+        tc(R("RET"), R("SI", 64, 128))
+        send(src, "ME%d" % t, "RET", "ra%d" % t, "rl%d" % t)
+        if t < 3:
+            tc(R("OFO"), R("ML", cl + 1, 1024, 4))
+            empties()
+        arrive("ra%d" % t, "ME%d" % t)
+        tt(R("NX1"), I("ME%d" % t, 0, 336, "LST", 176, 192), xs, A.add)
+        tc(I("X", 0, NX, "LST", 0, 16), R("NX1"))
+    dma("ox", T.yx[:, :], T.X[:, 1:4097], R("X", 1, 4097)[1], [])
+    for k in ("dm", "dx", "da", "dl", "dw", "ox", "oy", "v", "s", "p", "gg"):
+        g.sync.wait_ge(T.sem[k], count[k])
+    for t in range(4):
+        for k in ("vl", "rl"):
+            g.wait_ge(T.sem["%s%d" % (k, t)], count["%s%d" % (k, t)])

@@ -5,7 +5,6 @@ NX = 4368
 NO = 8576
 NE = 2064
 D0 = 4352
-BIG = float(2 ** 20)
 
 
 def _sb(spec):
@@ -18,26 +17,89 @@ def _sb(spec):
 
 
 SCRATCH = _sb({
-    "bfloat16": "X:4368 TB:3344 TX:4096 US:4096 XE:4096 SQO:4096 SQ:4096 XA:4096 OWG:4096 RM:4096 ONEB:128 IDB:128 NID:128 "
-                "IDV:128 BO:128 G16:8 G64:8 GM1:8 GS0:8 GC:64 BM:256 ROW:1792 WQ:2048 WT:2048 TRI:128 TRJ:128 RW1:512 RW2:512 "
-                "IND:1024 XS:256 SB:64 OCB:64 CF:768 XB:256 VM:256 TG:256 PRS:512 E2:512 THB:512 "
-                "VS:336 XVE:1024 XVS:1024 VD:1024 OVG:64 RET:64",
-    "float32": "OW:8576 ML:1280 VAL:4096 ONE:128 IDF:128 IDK:128 GS0F:8 QM:1024 RB:8 IXA:8x32 IXB:8x32 DUM:256 CO:256 CI:64 "
-               "LMF:8 LIM:64 K1:256 KM:256 KB:256 KD:256 E1:1024 EM:1024 EX:256 EQ:256 DS:256 SM:1024 TH:512 MD:256 W:16x32 "
-               "H3:16x32 F1:16x16 F2:16x16",
-    "int32": "AC:4368 MI:1024 QI:1280 LMI:2 WTI:1 SI:256",
-    "uint16": "OFO:256 ACO:256 OFD:256 MVO:256 LST:512 HL:64"})
+    "bfloat16": "X:4368 TB:3344 TX:4096 XE:4096 SQ:4096 XSE:4096 XA:4096 OWG:4096 RM:2048 QM:768 BM:512 ROW:1152 WQ:2048 WT:2048 "
+                "WE:2048 RW1:512 RW2:512 IND:1024 CF:768 MM:512 TH2:512 KC:512 ALT:1024 VS:336 XVE:1024 XVS:1024 VD:1024 RET:64",
+    "float32": "OW:8576 ML:1280 VAL:4096 KD:512 EMW:1280 SM:1024 W:512 MVA:528 MVB:272 W0:768 W1:768 W2:768",
+    "int32": "AC:4368 MI:1024 LMI:2 WTI:1 SJ:128 SK:2x16 SL:2x16",
+    "uint16": "OFO:256 ACO:256 OFD:256 MVO:256 MV2:256 LST:256 HL:64 SOF:80 SRP:4"})
+WIDTH = {k: v[1][1] * (v[1][2] if len(v[1]) > 2 else 1) for k, v in SCRATCH.items()}
+PLACE = {k: (k, 0) for k in SCRATCH}
+for _pool, _dt, _names in (
+        ("PB", "bfloat16", "ONEB:128 IDB:128 NID:128 IDV:128 BO:128 G16:8 G512:16 G64:8 GS0:8 GC:64 WB:128 TRI:128 TSB:128 XS0:256 XS1:256 "
+                           "SB:64 OCB:64 NVB:8 CN:256 XB:256 UC:256 VM:256 TG:256 INDD:256 FIT:256 NX1:256 OVG:64 AVG:64 EQV:64"),
+        ("PF", "float32", "QF:16 ONE:128 IDF:128 IDK:128 IXS:128 RB:8 DUM:256 CO:128 BAS:256 CIW:128 LMF:8 LIM:64 K1:256 KM:256 KBC:256 KV:128 "
+                          "EMA:256 EMB:256 EMV:128 EX:256 EQ:256 EQ2:256 MD:256 WM:256 ENX:256 HL1:64 HL2:64 VF:64")):
+    _at = 0
+    for _x in _names.split():
+        _k, _w = _x.split(":")
+        PLACE[_k], WIDTH[_k] = (_pool, _at), int(_w)
+        _at += -(-int(_w) // 16) * 16
+    SCRATCH[_pool] = ("sbuf", [128, _at], _dt)
 for _t in range(4):
-    SCRATCH["XV%d" % _t] = ("sbuf", [128, 64], "bfloat16")
-    SCRATCH["ME%d" % _t] = ("sbuf", [128, 336], "bfloat16")
+    for _k, _w in (("XV%d" % _t, 64), ("ME%d" % _t, 336)):
+        SCRATCH[_k] = ("sbuf", [128, _w], "bfloat16")
+        PLACE[_k], WIDTH[_k] = (_k, 0), _w
 for _b in range(8):
     SCRATCH["B%d" % _b] = ("psum", [128, 512], "float32")
-SHARE = {"SQB": "SQ", "XSE": "SQ", "THC": "CF", "NX1": "VM", "INDD": "TG", "TD": "XA", "UD": "OWG", "FS": "TH", "KA": "K1", "MSD": "KM", "L2": "MD", "ZI": "QI", "SQV": "XVE"}
-WIDTH = {k: v[1][1] for k, v in SCRATCH.items()}
-WIDTH.update({"SQB": 4096, "XSE": 4096, "THC": 512, "NX1": 256, "INDD": 256, "TD": 4096, "UD": 4096, "FS": 512, "KA": 256, "MSD": 256, "L2": 256, "ZI": 512, "SQV": 1024})
+    PLACE["B%d" % _b], WIDTH["B%d" % _b] = ("B%d" % _b, 0), 512
+for _k, _v, _at, _w in (("US", "OWG", 0, 4096), ("UD", "OWG", 0, 4096), ("TD", "XA", 0, 4096), ("XE2", "XE", 0, 4096), ("QI", "AC", 16, 768),
+                        ("YM", "VAL", 0, 1024), ("FS", "KD", 0, 512), ("SQV", "XVE", 0, 1024), ("KA", "K1", 0, 256), ("MSD", "KM", 0, 256),
+                        ("KB", "KM", 0, 256), ("L2", "MD", 0, 256), ("ZI", "MI", 0, 512), ("ZC", "MI", 512, 256), ("SI", "MI", 768, 256),
+                        ("ZA", "AC", 1024, 320)):
+    PLACE[_k], WIDTH[_k] = (PLACE[_v][0], PLACE[_v][1] + _at), _w
 SEMAPHORES = ["v", "s", "p", "gg", "dx", "da", "dm", "dl", "dw", "oy", "ox"] + ["%s%d" % (a, b) for a in ("va", "vl", "ra", "rl") for b in range(4)]
 PSUM = ["B%d" % b for b in range(8)]
 SIZE = {"float32": 4, "int32": 4, "bfloat16": 2, "uint16": 2}
+COST = {"cy": 0.9, "gat": 1.5, "sca": 3.0, "pe": 0.65, "wake": 80.0, "far": 3000.0, "dma": 3000.0, "look": 400.0}
+PLAN = {}
+
+
+def plan(calls):
+    n = len(calls)
+    wake = COST["wake"]
+    after = [[] for _ in calls]
+    for i, c in enumerate(calls):
+        for j in c["dep"]:
+            after[j].append(i)
+    rank = [0.0] * n
+    for i in range(n - 1, -1, -1):
+        c = calls[i]
+        rank[i] = min(c["ns"].values()) + c["lat"] + max([rank[j] + wake for j in after[i]] + [0.0])
+    left = [len(c["dep"]) for c in calls]
+    ready = [0.0] * n
+    where = [None] * n
+    free = {q: 0.0 for q in ("v", "s", "p", "gg", "y", "x")}
+    pool = {q: set() for q in free}
+    order = []
+
+    def enter(i):
+        for q in calls[i]["ns"]:
+            pool[q].add(i)
+    for i in range(n):
+        if not left[i]:
+            enter(i)
+    while len(order) < n:
+        q = min((q for q in free if pool[q]), key=lambda q: max(free[q], min(ready[i] for i in pool[q])))
+        now = max(free[q], min(ready[i] for i in pool[q]))
+        i = max((i for i in pool[q] if ready[i] <= now + COST["look"]), key=lambda i: (rank[i], -i))
+        if ready[i] > now:
+            fit = [j for j in pool[q] if max(now, ready[j]) + calls[j]["ns"][q] <= ready[i]]
+            if fit:
+                i = max(fit, key=lambda i: (rank[i], -i))
+        start = max(now, ready[i])
+        c = calls[i]
+        free[q] = start + c["ns"][q]
+        where[i] = q
+        order.append(i)
+        for k in c["ns"]:
+            pool[k].discard(i)
+        for j in after[i]:
+            inline = c["dep"] is not None and calls[j]["dep"][i]
+            ready[j] = max(ready[j], free[q] + (0.0 if inline else c["lat"] + wake))
+            left[j] -= 1
+            if not left[j]:
+                enter(j)
+    return [(i, where[i]) for i in order]
 
 
 def rank_program(g, core, T, topo):
@@ -46,687 +108,694 @@ def rank_program(g, core, T, topo):
         return
     n = len(T.cores)
     queue = {"v": g.vector, "s": g.scalar, "p": g.tensor, "gg": g, "y": g.sync}
-    count = {}
-    known = {q: {} for q in queue}
-    clock = {}
+    calls = []
     log = {}
+    turn = {}
 
     def R(b, lo=0, hi=None, st=1, p0=0, p1=128):
         hi = WIDTH[b] if hi is None else min(hi, WIDTH[b])
-        b = SHARE.get(b, b)
+        b, at = PLACE[b]
+        lo, hi = lo + at, hi + at
         full = p0 == 0 and p1 == 128
         ap = T[b][:, lo:hi:st] if full else T[b][p0:p1, lo:hi:st]
-        return (ap, [(b, lo, hi, st)])
+        return (ap, [(b, lo, hi, st)], -(-(hi - lo) // st))
 
     def R3(b, a0, a1, k0, k1):
         s = SCRATCH[b][1][2]
-        return (T[b][:, a0:a1, k0:k1], [(b, a0 * s, a1 * s, 1)])
+        return (T[b][:, a0:a1, k0:k1], [(b, a0 * s, a1 * s, 1)], (a1 - a0) * (k1 - k0))
 
     def I(b, lo, hi, ob, o0, o1):
-        b, ob = SHARE.get(b, b), SHARE.get(ob, ob)
-        return (T[b][:, lo:hi].indirect(T[ob][:, o0:o1]), [(b, lo, hi, 1), (ob, o0, o1, 1)])
+        b, at = PLACE[b]
+        lo, hi = lo + at, hi + at
+        return (T[b][:, lo:hi].indirect(T[ob][:, o0:o1]), [(b, lo, hi, 1), (ob, o0, o1, 1)], 16 * (o1 - o0))
 
-    def need(q, reads, writes, dma=False):
-        out = []
+    def call(ways, reads, writes, sem=None, inc=1, lat=0.0, dma=False, fence=False, more=()):
+        me = len(calls)
+        q = list(ways)[0] if len(ways) == 1 else None
+        dep = {j: False for j in more}
+        for b in set(x[0] for x in reads + writes if x[0] in PSUM):
+            holder, before, now = turn.get(b, (None, [], []))
+            if q is None or q != holder:
+                before, now = now, []
+                log[b] = []
+            if q == "p" and now:
+                dep[now[-1]] = not fence
+                now = []
+            else:
+                dep.update({j: False for j in before})
+            turn[b] = (q, before, now + [me])
         for regs, w in ((reads, False), (writes, True)):
             for (b, lo, hi, st) in regs:
-                ps = b in PSUM
+                if q == "p" and b in PSUM:
+                    continue
                 if dma and w:
                     al = 16 // SIZE[SCRATCH[b][2]]
                     lo, hi, st = lo // al * al, -(-hi // al) * al, 1
-                for (l2, h2, s2, w2, e, c, d2) in log.get(b, []):
-                    if ps:
-                        if e == q and (q == "p" or not (w or w2) or lo >= h2 or l2 >= hi):
-                            continue
-                    else:
-                        if not (w or w2):
-                            continue
-                        if d2 and w2 and w:
-                            al = 16 // SIZE[SCRATCH[b][2]]
-                            l2, h2, s2 = l2 // al * al, -(-h2 // al) * al, 1
-                        if lo >= h2 or l2 >= hi or (st == s2 and st > 1 and (lo - l2) % st):
-                            continue
-                    out.append((e, c))
-        best = {}
-        for e, c in out:
-            best[e] = max(best.get(e, 0), c)
-        for e, c in sorted(best.items(), key=lambda x: -x[1]):
-            if known[q].get(e, 0) < c:
-                queue[q].wait_ge(T.sem[e], c)
-                for k, v in clock[(e, c)].items():
-                    known[q][k] = max(known[q].get(k, 0), v)
-
-    def done(q, e, inc, reads, writes, dma=False):
-        count[e] = count.get(e, 0) + inc
-        c = count[e]
-        ck = dict(known[q])
-        ck[e] = c
-        clock[(e, c)] = ck
+                for (l2, h2, s2, w2, e, j, d2) in log.get(b, []):
+                    if not (w or w2):
+                        continue
+                    if d2 and w2 and w:
+                        al = 16 // SIZE[SCRATCH[b][2]]
+                        l2, h2, s2 = l2 // al * al, -(-h2 // al) * al, 1
+                    if lo >= h2 or l2 >= hi or (st == s2 and st > 1 and (lo - l2) % st):
+                        continue
+                    dep[j] = False
+        calls.append({"f": {k: v[0] for k, v in ways.items()}, "ns": {k: v[1] for k, v in ways.items()}, "dep": dep, "sem": sem,
+                      "inc": inc, "lat": lat})
         for (b, lo, hi, st) in writes:
-            keep = [r for r in log.get(b, []) if not (b not in PSUM and st == 1 and lo <= r[0] and r[1] <= hi)]
-            log[b] = keep + [(lo, hi, st, True, e, c, dma)]
+            keep = [r for r in log.get(b, []) if not (st == 1 and lo <= r[0] and r[1] <= hi)]
+            log[b] = keep + [(lo, hi, st, True, q, me, dma)]
         for (b, lo, hi, st) in reads:
-            l = log.setdefault(b, [])
-            l[:] = [r for r in l if not (r[:4] == (lo, hi, st, False) and r[4] == e)]
-            l.append((lo, hi, st, False, e, c, dma))
-        for b in set(x[0] for x in reads + writes if x[0] in PSUM):
-            if len(log[b]) > 60:
-                m = {}
-                for r in log[b]:
-                    k = (r[4], r[3])
-                    o = m.get(k)
-                    m[k] = r if o is None else (min(o[0], r[0]), max(o[1], r[1]), 1, r[3], r[4], max(o[5], r[5]), r[6])
-                log[b] = list(m.values())
+            log.setdefault(b, []).append((lo, hi, st, False, q, me, dma))
+        return me
 
-    def op(q, f, out, ins):
+    def sides(out, ins):
         rd = [x for i in ins if isinstance(i, tuple) for x in i[1]]
-        wr = list(out[1])
-        if len(wr) > 1:
-            rd = rd + wr[1:]
-            wr = wr[:1]
-        need(q, rd, wr)
-        f().then_inc(T.sem[q], 1)
-        done(q, q, 1, rd, wr)
+        return rd + out[1][1:], out[1][:1]
+
+    def ns(q, out, ins, two=False):
+        m = out[2]
+        if len(out[1]) > 1:
+            return 60 + m * COST["sca"] * COST["cy"]
+        if ins and len(ins[0][1]) > 1:
+            return 60 + m * COST["gat"] * COST["cy"]
+        bufs = [x[1][0][0] for x in [out] + ins if isinstance(x, tuple)]
+        if two:
+            m *= 1 if any(b in PSUM for b in bufs[1:]) else 2
+        elif q == "v" and all(SIZE[SCRATCH[b][2]] == 2 for b in bufs):
+            m *= 0.5
+        if q == "v" and not two and len(ins) == 1 and ins[0][2] > m * 2:
+            m = ins[0][2]
+        return 20 + max(m, 64) * COST["cy"]
+
+    def vop(f, out, ins, two=False, other=None):
+        rd, wr = sides(out, ins)
+        ways = {"v": (f, ns("v", out, ins, two))}
+        if other is not None:
+            ways["s"] = (other, ns("s", out, ins))
+        call(ways, rd, wr)
 
     def ap(x):
         return x[0] if isinstance(x, tuple) else x
 
     def tc(o, i):
-        op("v", lambda: g.vector.tensor_copy(o[0], i[0]), o, [i])
+        vop(lambda: g.vector.tensor_copy(o[0], i[0]), o, [i])
+
+    def cp(o, i):
+        vop(lambda: g.vector.tensor_copy(o[0], i[0]), o, [i], other=lambda: g.scalar.activation(o[0], i[0], F.Copy))
 
     def tt(o, a, b, f):
-        op("v", lambda: g.vector.tensor_tensor(o[0], a[0], b[0], f), o, [a, b])
+        vop(lambda: g.vector.tensor_tensor(o[0], a[0], b[0], f), o, [a, b], True)
 
-    def ts(o, a, s1, f1, s2=None, f2=None):
+    def ts(o, a, s1, f1, s2=None, f2=None, other=None):
         if f2 is None:
-            op("v", lambda: g.vector.tensor_scalar(o[0], a[0], ap(s1), None, f1), o, [a, s1])
+            vop(lambda: g.vector.tensor_scalar(o[0], a[0], ap(s1), None, f1), o, [a, s1], other=other)
         else:
-            op("v", lambda: g.vector.tensor_scalar(o[0], a[0], ap(s1), ap(s2), f1, f2), o, [a, s1, s2])
+            vop(lambda: g.vector.tensor_scalar(o[0], a[0], ap(s1), ap(s2), f1, f2), o, [a, s1, s2], other=other)
+
+    def lin(o, a, mul, add):
+        ts(o, a, mul, A.mult, add, A.add, lambda: g.scalar.activation(o[0], a[0], F.Identity, bias=add, scale=mul))
+
+    def relu(o, a, add):
+        ts(o, a, add, A.add, 0.0, A.max, lambda: g.scalar.activation(o[0], a[0], F.Relu, bias=add))
+
+    def sign(o, a):
+        ts(o, a, 0.0, A.is_gt, other=lambda: g.scalar.activation(o[0], a[0], F.Sign))
+
+    def none(o, a):
+        ts(o, a, 0.0, A.is_equal, other=lambda: g.scalar.activation(o[0], a[0], F.Relu, bias=1.0, scale=-1.0))
 
     def ms(o, c):
-        op("v", lambda: g.vector.memset(o[0], c), o, [])
+        vop(lambda: g.vector.memset(o[0], c), o, [])
 
     def scan(o, d0, d1, f0, f1):
-        op("v", lambda: g.vector.tensor_tensor_scan(o[0], d0[0], d1[0], 0.0, f0, f1), o, [d0, d1])
+        vop(lambda: g.vector.tensor_tensor_scan(o[0], d0[0], d1[0], 0.0, f0, f1), o, [d0, d1])
 
     def addup(o, i):
-        op("v", lambda: g.vector.tensor_reduce(o[0], i[0], AX, A.add), o, [i])
+        vop(lambda: g.vector.tensor_reduce(o[0], i[0], AX, A.add), o, [i])
 
     def act(o, i, f):
-        op("s", lambda: g.scalar.activation(o[0], i[0], f), o, [i])
+        rd, wr = sides(o, [i])
+        call({"s": (lambda: g.scalar.activation(o[0], i[0], f), ns("s", o, [i]))}, rd, wr)
 
-    def mm(o, l, r, a, z):
-        op("p", lambda: g.tensor.matmul(o[0], l[0], r[0], a, z), o, [l, r])
+    def mm(o, l, r, a, z, fence=False):
+        t = max(min(64, l[2]), r[2]) * (4 if SIZE[SCRATCH[l[1][0][0]][2]] == 4 else 1) * COST["pe"]
+        call({"p": (lambda: g.tensor.matmul(o[0], l[0], r[0], a, z), t)}, l[1] + r[1], o[1], lat=100.0, fence=fence)
 
     def aff(o, i, pat, cmp, fill, base, cm):
-        op("gg", lambda: g.affine_select(o[0], i[0], pat, cmp, fill, base, cm), o, [i])
+        call({"gg": (lambda: g.affine_select(o[0], i[0], pat, cmp, fill, base, cm), 170 + 2 * o[2] * COST["cy"])}, i[1], o[1])
 
     def iota(o, pat, base, cm):
         fl = SCRATCH[o[1][0][0]][2] != "int32"
-        op("gg", lambda: g.iota(o[0], pat, base, cm, allow_small_or_imprecise_dtypes=fl), o, [])
+        call({"gg": (lambda: g.iota(o[0], pat, base, cm, allow_small_or_imprecise_dtypes=fl), 130 + 2 * o[2] * COST["cy"])}, [], o[1])
 
-    def dma(sem, o_ap, i_ap, reads, writes):
-        need("y", reads, writes, True)
-        g.sync.dma_start(o_ap, i_ap).then_inc(T.sem[sem], 16)
-        done("y", sem, 16, reads, writes, True)
+    def dma(sem, pairs, reads, writes):
+        def f():
+            for o, i in pairs[:-1]:
+                g.sync.dma_start(o, i).then_inc(T.sem[sem], 16)
+            return g.sync.dma_start(*pairs[-1])
+        call({"y": (f, 100.0 * len(pairs))}, reads, writes, sem, 16 * len(pairs), COST["dma"] + 1000.0 * len(pairs), True)
 
     def send(dst, ob, ib, rs, ls):
         eng = topo.engines(core, T.cores[dst])[:4]
         mask = sum(1 << e for e in eng)
         rid, pid, _se = topo.addr(T.cores[dst])
         i = R(ib, 0, 64)
-        need("gg", i[1], [])
-        g.remote_dma(T[ob][:, 0:64], i[0], T.sem[rs], T.sem[ls], pid, rid, mask)
-        done("gg", ls, len(eng), i[1], [])
-
-    def arrive(sem, b):
-        count[sem] = 4
-        clock[(sem, 4)] = {sem: 4}
-        log.setdefault(b, []).append((0, 64, 1, True, sem, 4, True))
+        me = call({"gg": (lambda: g.remote_dma(T[ob][:, 0:64], i[0], T.sem[rs], T.sem[ls], pid, rid, mask), 100.0)}, i[1], [], ls, -len(eng), COST["far"])
+        call({"x": (None, 0.0)}, [], R(ob, 0, 64)[1], rs, -len(eng), 0.0, True, more=[me])
 
     def bounded(o, pat, base, cm, width):
         aff(o, o, pat, A.is_ge, 0.0, base, cm)
         aff(o, o, [[-s, k] for s, k in pat], A.is_ge, 0.0, width - 1 - base, -cm)
 
-    q_ = lambda k: R("QM", k, k + 1)
+    q_ = lambda k: R("QF", k, k + 1)
     C = lambda a: R("CO", 16 * a, 16 * a + 16)
     S = lambda a, w=16: R("SM", 16 * a, 16 * a + w)
     g8 = R("BO", 0, 128, 16)
     row = lambda a, w: R("ROW", a, a + w, 1, 0, 1)
     lone = R("ONEB", 0, 128, 1, 0, 1)
     one = R("ONE")
-    w2 = lambda: (T.W[:, :, :], [("W", 0, 512, 1)])
+    half = lambda b, h: R(b, 2048 * h, 2048 * h + 2048)
+    hv = lambda b, h, o=0: R(b, o + 128 * h, o + 128 * h + 128)
+    wide = lambda b, lo, w: I(b, lo, lo + w, "SOF", 0, w)
+    again = lambda b, lo, k: I(b, lo, lo + 16, "SRP", 0, k)
 
-    def wrap(cols, bank, ps, keep=None):
-        w = 16 * cols
-        x = keep if keep is not None else R(ps, 0, w)
-        scan(x, R("RM", 0, w), R("E1", 0, w), A.mult, A.add)
-        tt(R("EM", 0, w), x, R("QM", 0, w), A.mult)
+    def wrap(a, cols, em, eo, bank, lo):
+        tt(R(em, eo, eo + 16 * cols), wide("SM", 16 * a, cols), R("QM", 0, 16 * cols), A.mult)
         for h in range(cols // 8):
-            mm(R(bank, 8 * h, 8 * h + 8), R("EM", 128 * h, 128 * h + 128), R("RB"), True, True)
-        return R(bank, 0, cols)
+            mm(R(bank, lo + 8 * h, lo + 8 * h + 8), R(em, eo + 128 * h, eo + 128 * h + 128), R("RB"), True, True)
+        return R(bank, lo, lo + cols)
 
-    def wide(bank, lo, order):
-        scan(R("B3"), R("RM", 0, 512), R("E1", 0, 512), A.mult, A.add)
-        scan(R("B7"), R("RM", 0, 512), R("E1", 512, 1024), A.mult, A.add)
-        tt(R("EM", 512, 1024), R("B7"), R("QM", 0, 512), A.mult)
-        tt(R("EM", 0, 512), R("B3"), R("QM", 0, 512), A.mult)
-        for b in order:
-            mm(R(bank, lo + 8 * b, lo + 8 * b + 8), R("EM", 128 * b, 128 * b + 128), R("RB"), True, True)
-        return R(bank, lo, lo + 64)
-
-    def moved(ids, b):
-        ts(R("B1", 0, 256), ids, 0.0, A.is_equal)
-        tt(R("EQ"), R("B1", 0, 256), R("DUM"), A.mult)
-        tt(R("EQ"), R("EQ"), ids, A.add)
-        tc(R(b), R("EQ"))
-
-    def owners(b):
-        mv = ("MVO", "OFD")[b % 2]
-        moved(R("ML", 256 * b, 256 * b + 256), mv)
-        tc(R("XE", 0, 4096, 16), R("TB", NE + 256 * b, NE + 256 * b + 256))
-        settle(mv)
+    def moved(o, ids, e, x):
+        none(e, ids)
+        tt(x, e, R("DUM"), A.mult)
+        tt(o, x, ids, A.add)
 
     def settle(mv):
         for h in range(2):
-            v = R("VAL", 2048 * h, 2048 * h + 2048)
-            scan(v, R("RM", 0, 2048), R("XE", 2048 * h, 2048 * h + 2048), A.mult, A.add)
-            act(I("OW", 0, NO, mv, 128 * h, 128 * h + 128), v, F.Silu)
+            scan(half("VAL", h), R("RM"), half("XE2", h), A.mult, A.add)
+            act(I("OW", 0, NO, mv, 128 * h, 128 * h + 128), half("VAL", h), F.Silu)
+
+    def owners(u):
+        mv = ("MVO", "MV2")[u % 2]
+        moved(R("EQ2"), R("ML", u, 1024, 4), R("B3", 0, 256), R("EQ2"))
+        tc(R(mv), R("EQ2"))
+        tc(R("XE2", 0, 4096, 16), R("TB", NE + u, NE + 1024, 4))
+        settle(mv)
+
+    def shifts(w, width, mv, bank, sg):
+        p = R(bank, 0, width)
+        for th, s in ((4096.0, 1), (512.0, 2), (64.0, 4), (8.0, 8)):
+            lin(p, w, -th, th * th)
+            relu(R(mv, 8, 8 + width), w, -th)
+            tt(p, w, p, A.min)
+            tt(w, R(mv, 8 + sg * s, 8 + sg * s + width), p, A.max)
+
+    def numbers(bank, lo, src, cols, wq="WQ"):
+        for q in range(16):
+            mm(R(bank, lo, lo + cols), R(wq, 128 * q, 128 * q + 128), R(src, q, 16 * cols, 16), q == 0, q == 15)
+        return R(bank, lo, lo + cols)
 
     mi = R("MI")
-    dma("dm", T.MI[:, :], T.ml[:, :], [], mi[1])
+    qi = R("SJ", 112, 128)
+    iota(qi, [[-1, 16]], 1024, 1)
+    ts(qi, qi, 15, A.bitwise_and)
+    ts(R("QF"), qi, 0, A.is_equal)
+    ts(R("QM", 0, 16), qi, 0, A.is_equal)
+    for w in (16, 32, 64, 128, 256, 512):
+        tc(R("QM", w, 2 * w), R("QM", 0, min(w, 768 - w)))
+    dma("dm", [(T.MI[:, :], T.ml[:, :])], [], mi[1])
     ms(R("X", 0, 16), -16.0)
     ms(R("X", 4096, NX), 0.0)
-    ms(R("AC", 0, 8), 0)
-    ms(R("AC", 4096, NX), 0)
-    dma("dx", T.X[:, 1:4097], T.x0[:, :], [], R("X", 1, 4097)[1])
-    for j in range(4):
-        dma("da", T.AC[:, 1 + 1024 * j:1025 + 1024 * j], T.ac[:, :], [], R("AC", 1 + 1024 * j, 1025 + 1024 * j)[1])
-    log["AC"] = [r[:5] + (64,) + r[6:] if r[4] == "da" else r for r in log["AC"]]
-    dma("dl", T.LMI[:], T.lims[:, :], [], R("LMI")[1])
-    dma("dw", T.WTI[:], T.wt[:, :], [], R("WTI")[1])
-    iota(R("QI", 0, 1024), [[0, 64], [-1, 16]], 1024, 1)
-    iota(R("QI", 1024, 1280), [[1, 256]], 0, 0)
+    ms(R("AC", 0, 8), -1)
+    ms(R("AC", 4096, NX), -1)
+    dma("dx", [(T.X[:, 1:4097], T.x0[:, :])], [], R("X", 1, 4097)[1])
+    dma("da", [(T.AC[:, 1 + 1024 * j:1025 + 1024 * j], T.ac[:, :]) for j in range(4)], [], R("AC", 1, 4097)[1])
+    dma("dl", [(T.LMI[:], T.lims[:, :])], [], R("LMI")[1])
+    dma("dw", [(T.WTI[:], T.wt[:, :])], [], R("WTI")[1])
     iota(R("DUM"), [[16, 256]], D0, 1)
+    iota(R("OW", 0, 4112), [[0, 4112]], 128, 0)
     ms(R("XE"), 0.0)
     ms(R("RM"), 1.0)
-    ms(R("RM", 0, 4096, 16), 0.0)
-    ms(R("OW", 0, 16), 128.0)
+    ms(R("RM", 0, 2048, 16), 0.0)
     ms(one, 1.0)
-    ts(R("QI", 0, 1024), R("QI", 0, 1024), 15, A.bitwise_and)
-    ts(R("QM"), R("QI", 0, 1024), 0, A.is_equal)
-    ms(R("SM", 4, 6), 0.0)
+    pl, cj = R("W0", 0, 320), R("W0", 320, 640)
+    iota(pl, [[1, 40], [0, 8]], 0, 0)
+    iota(cj, [[0, 40], [1, 8]], 0, 0)
+    ts(cj, cj, q_(1), A.mult, 128.0, A.add)
+    ts(pl, pl, q_(0), A.mult)
+    tt(pl, pl, cj, A.add)
+    tt(R("SM", 4, 5), q_(2), q_(3), A.add)
+    tt(R("SM", 5, 6), q_(4), q_(5), A.add)
+    tt(R("SM", 4, 5), R("SM", 4, 5), R("SM", 5, 6), A.add)
     for u in range(4):
-        ts(R("SM", 6, 7), q_(2 + u), float(u), A.mult)
-        tt(R("SM", 4, 5), R("SM", 4, 5), R("SM", 6, 7), A.add)
-        tt(R("SM", 5, 6), R("SM", 5, 6), q_(2 + u), A.add)
-    ci, cj = R("QI", 1024, 1280), R("SI")
-    ts(cj, ci, 7, A.logical_shift_right)
-    ts(R("K1"), cj, q_(0), A.mult, 128.0, A.add)
-    ts(cj, ci, 127, A.bitwise_and)
-    ts(R("KM"), cj, q_(1), A.mult)
-    tt(R("K1"), R("K1"), R("KM"), A.add)
-    ts(cj, ci, 3, A.bitwise_and)
-    ts(R("KM"), cj, R("SM", 4, 5), A.is_equal, R("SM", 5, 6), A.mult)
-    tt(R("TB", NE, NE + 256), R("K1"), R("KM"), A.add)
+        tt(R("SM", 8 + u, 9 + u), q_(2 + u), R("SM", 4, 5), A.subtract)
+        ts(R("SM", 8 + u, 9 + u), R("SM", 8 + u, 9 + u), 128.0, A.mult)
+        ts(R("TB", NE + u, NE + 1280, 4), pl, R("SM", 8 + u, 9 + u), A.add)
     ml = R("ML", 0, 1024)
     ts(ml, mi, 4096, A.is_equal, -4097, A.mult)
     tt(ml, ml, mi, A.add)
     ts(ml, ml, 1, A.add)
-    owners(0)
-    for b in range(1, 5):
-        ts(R("SM", 7, 8), q_(0), 2.0 * b, A.mult)
-        ts(R("TB", NE + 256 * b, NE + 256 * b + 256), R("TB", NE, NE + 256), R("SM", 7, 8), A.add)
     ms(R("ML", 1024, 1280), 0.0)
-    act(R("IND"), ml, F.Sign)
+    sign(R("IND"), ml)
+    for u in range(1, 4):
+        owners(u)
     aff(R("IDF"), one, [[-1, 128]], A.is_equal, 0.0, 0, 1)
-    ms(R("TH"), 1.0)
-    for o, w, p in ((0, 128, ([[-16, 8], [0, 16]], 0, 1, 16)), (128, 8, ([[-16, 8]], 0, 1, 16)), (256, 128, ([[1, 128]], -1, -1, 200)),
-                    (384, 128, ([[1, 128]], 0, -1, 200))):
-        bounded(R("TH", o, o + w), *p)
-    tc(R("BO"), R("TH", 0, 128))
-    tc(R("RB"), R("TH", 128, 136))
-    tc(R("TRI"), R("TH", 256, 384))
-    tc(R("TRJ"), R("TH", 384, 512))
+    ms(R("KD"), 1.0)
+    for o, w, p in ((0, 128, ([[-16, 8], [0, 16]], 0, 1, 16)), (128, 8, ([[-16, 8]], 0, 1, 16)), (256, 128, ([[1, 128]], -1, -1, 200))):
+        bounded(R("KD", o, o + w), *p)
+    tc(R("BO"), R("KD", 0, 128))
+    tc(R("RB"), R("KD", 128, 136))
+    tc(R("TRI"), R("KD", 256, 384))
+    ts(R("KD", 384, 512), R("KD", 256, 384), -1.0, A.add)
+    tt(R("TSB"), R("KD", 384, 512), R("KD", 0, 128), A.mult)
+    ts(R("TSB"), R("TSB"), -1.0, A.mult)
     tc(R("ONEB"), one)
     tc(R("IDB"), R("IDF"))
     ts(R("NID"), R("IDF"), -1.0, A.mult)
     ts(R("IDK"), R("IDF"), 1024.0, A.mult)
+    ts(R("IXS"), R("IDF"), 2.0 ** -10, A.mult)
     ts(R("IDV"), R("IDF"), float(2 ** 18), A.mult)
-    for b, c in (("G16", 16.0), ("G64", 65536.0), ("GM1", -1.0)):
-        ts(R(b), g8, c, A.mult)
+    for b, c in ((R("G16"), 16.0), (R("G64"), 65536.0), (R("G512", 0, 8), 512.0), (R("G512", 8, 16), 512.0)):
+        ts(b, g8, c, A.mult)
     ts(R("GS0"), g8, q_(0), A.mult)
-    ts(R("GS0F"), g8, q_(0), A.mult)
-    for o, pat, base in ((0, [[0, 8], [4096, 16]], 0), (128, [[0, 8], [1, 16]], 0), (256, [[0, 8], [-1, 16]], 15), (512, [[-1, 256]], 0)):
-        w = pat[0][1] * (pat[1][1] if len(pat) > 1 else 1)
-        iota(R("EM", o, o + w), pat, base, 0)
-    tc(R("ROW", 0, 384), R("EM", 0, 384))
-    ms(R("ROW", 384, 512), -1.0)
-    tc(R("ROW", 512, 768), R("EM", 512, 768))
-    ms(w2(), 0.0)
-    ms(R3("W", 0, 16, 16, 32), -1.0)
-    tc(R("ROW", 768, 1280), w2())
-    ms(R("ROW", 1280, 1792), 0.0)
-    for h in range(2):
-        tc(R("ROW", 1280 + 256 * h, 1408 + 256 * h), R("EM", 128, 256))
+    for o, pat, base in ((0, [[0, 8], [4096, 16]], 0), (128, [[0, 8], [1, 16]], 0), (256, [[0, 16], [-1, 16]], 15), (512, [[0, 128]], -1),
+                         (640, [[0, 2], [-384, 2], [0, 8]], 0)):
+        w = 1
+        for x in pat:
+            w *= x[1]
+        iota(R("W1", o, o + w), pat, base, 0)
+    tc(R("ROW", 0, 640), R("W1", 0, 640))
+    iota(R("KD"), [[0, 32], [32, 16]], -128, 0)
+    iota(R("KC"), [[1, 2], [0, 16], [1, 16]], 0, 0)
+    iota(R("SJ", 0, 80), [[1, 80]], 0, 0)
+    tc(R("SOF"), R("SJ", 0, 80))
+    iota(R("SJ", 96, 100), [[0, 4]], 0, 1)
+    ts(R("SJ", 96, 100), R("SJ", 96, 100), 15, A.bitwise_and)
+    tc(R("SRP"), R("SJ", 96, 100))
+    tt(R("ROW", 640, 1152), wide("W1", 640, 32), R("KD"), A.add)
     ms(R("BM"), 0.0)
-    ms(R("BM", 0, 256, 16), float(2 ** 25))
-    wc = R("SM", 0, 1)
-    ts(wc, q_(0), 128.0, A.mult)
-    tt(wc, wc, q_(1), A.add)
-    ts(R("SM", 1, 2), q_(6), -129.0, A.mult)
-    tt(wc, wc, R("SM", 1, 2), A.add)
+    ms(R("BM", 0, 512, 16), float(2 ** 25))
+    wc, wl = R("SM", 0, 1), R("SM", 1, 2)
+    ts(wl, q_(1), 4.0, A.mult)
+    for u in range(1, 4):
+        ts(R("SM", 2, 3), q_(2 + u), u / 128, A.mult)
+        tt(wl, wl, R("SM", 2, 3), A.add)
+    ts(wc, q_(0), 32.0, A.mult)
+    tt(wc, wc, wl, A.add)
+    ts(R("SM", 2, 3), q_(6), -36.0, A.mult)
+    tt(wc, wc, R("SM", 2, 3), A.add)
     for u in range(4):
-        tt(R("SM", 2, 3), q_(2 + u), q_(6), A.subtract)
-        ts(R("GC", 16 * u + 8, 16 * u + 16), g8, wc, A.mult)
-        ts(R("GC", 16 * u, 16 * u + 8), g8, R("SM", 2, 3), A.mult, float(2 ** 17), A.mult)
-    lanes = lambda a, base, s: iota(C(a), [[128 * s, 2], [0, 8]], base, s)
-    lanes(0, 4097, 1)
-    lanes(1, 15, 16)
-    lanes(2, 4096, -1)
-    lanes(3, NE + 1024, 1)
-    lanes(4, 64, 1)
+        ts(R("SM", 2, 3), q_(2 + u), float(2 ** 15), A.mult)
+        tt(R("SM", 3, 4), R("SM", 2, 3), q_(0), A.add)
+        tt(R("SM", 2, 3), R("SM", 2, 3), wl, A.max)
+        ts(R("GC", 16 * u, 16 * u + 8), g8, R("SM", 3, 4), A.mult)
+        ts(R("GC", 16 * u + 8, 16 * u + 16), g8, R("SM", 2, 3), A.mult)
+    lanes = lambda o, base, s: iota(o, [[128 * s, 2], [0, 8]], base, s)
+    lanes(C(0), 4097, 1)
+    lanes(C(1), 15, 16)
+    lanes(C(2), 11 * 2 ** 18, -1)
+    lanes(C(3), 1024, 1)
+    lanes(C(4), 64, 1)
     iota(C(5), [[0, 16]], 0, 16)
     for t in range(4):
-        lanes(6 + t, t, 4)
-        lanes(10 + t, t + NE, 4)
-    iota(R("CI"), [[128, 8], [0, 8]], 0, 1)
-    iota(R("SI", 0, 1), [[0, 1]], 0, 1)
-    ms(R("E1"), 0.0)
+        for j, (base, s) in enumerate(((512, 1), (t, 4), (NE + t, 4), (NE + 1024, 1))):
+            lanes(R("BAS", 64 * t + 16 * j, 64 * t + 16 * j + 16), base, s)
+    iota(R("CIW", 0, 64), [[16, 64]], 0, 0)
+    tc(R("SM", 6, 7), R("SJ", 96, 97))
+    ts(R("CIW", 0, 64), R("CIW", 0, 64), R("SM", 6, 7), A.add)
+    ts(R("CIW", 64, 128), R("CIW", 0, 64), 1024.0, A.add)
     ms(R("WQ"), 1.0)
     aff(R("WQ"), R("WQ"), [[1, 16], [0, 8], [-1, 16]], A.is_equal, 0.0, 0, 0)
     bounded(R("WQ"), [[0, 16], [-16, 8], [0, 16]], 0, 1, 16)
-    owners(1)
-
-    def rest():
-        ms(R("TB", 0, NE), 128.0)
-        for b, s in (("RW1", 128), ("RW2", 256)):
-            ms(R(b), 1.0)
-            ms(R(b, 0, 512, s), 0.0)
-        ms(R3("IXA", 0, 8, 16, 32), 0.0)
-        ms(R3("IXB", 0, 8, 0, 16), 0.0)
-        ts(R3("IXA", 0, 8, 0, 16), R("IDF"), 2.0 ** -10, A.mult)
-        ts(R3("IXB", 0, 8, 16, 32), R("IDF"), 2.0 ** -10, A.mult)
-        for k in range(11):
-            ms(R("SM", 16 + k, 17 + k), float(2 ** (10 - k)))
-        ms(R("SM", 27, 32), 0.0)
-        tt(R("SM", 16, 32), R("SM", 16, 32), R("QM", 0, 16), A.mult)
-        addup(R("LMF", 0, 1), R("SM", 16, 32))
-        ts(R("LMF", 2, 3), R("LMF", 1, 2), -1.0, A.mult, 1.0, A.add)
-        for a in (0, 1):
-            ts(R("LMF", 3 + 2 * a, 4 + 2 * a), R("LMF", 1 + a, 2 + a), 1 / 32, A.mult)
-            ts(R("LMF", 4 + 2 * a, 5 + 2 * a), R("LMF", 1 + a, 2 + a), -16.0, A.mult)
-        tc(R("SM", 8, 10), R("LMI"))
-        for j in range(2):
-            ts(R("VM", 0, 128), one, R("SM", 8 + j, 9 + j), A.mult)
-            for h in range(2):
-                mm(R("B2", 16 * j + 8 * h, 16 * j + 8 * h + 8), R("VM", 0, 128), R("GS0"), True, True)
-        tc(R("LIM", 0, 32), R("B2", 0, 32))
-        tc(R("LIM", 32, 48), R("LIM", 0, 16))
-        for b in ("VS", "XVS", "E2"):
-            ms(R(b), 0.0)
-        for u in range(4):
-            ms(R("ME%d" % u, 64, 336), 0.0)
-        tc(R("SM", 3, 4), R("WTI"))
-        ts(R("WT"), R("WQ"), R("SM", 3, 4), A.mult)
-        ts(R("WQ"), R("WQ"), wc, A.mult)
-
+    ms(R("TB", 0, NE), 128.0)
+    for b, s in (("RW1", 128), ("RW2", 256)):
+        ms(R(b), 1.0)
+        ms(R(b, 0, 512, s), 0.0)
+    for k in range(11):
+        ms(R("SM", 16 + k, 17 + k), float(2 ** (10 - k)))
+    ms(R("SM", 27, 32), 0.0)
+    tt(R("SM", 16, 32), R("SM", 16, 32), R("QM", 0, 16), A.mult)
+    addup(R("LMF", 0, 1), R("SM", 16, 32))
+    iota(R("SI", 0, 1), [[0, 1]], 0, 1)
     ts(R("SI", 0, 1), R("SI", 0, 1), 16, A.bitwise_and)
     ts(R("LMF", 1, 2), R("SI", 0, 1), 16.0, A.is_equal)
-    NN, LIVE, HAS, FM, DD, MS, GR, WAN, SPL, RK, IDL, VIS, T1, T2, RV = range(4, 19)
-    SUU, S1, NV, NM, AA = 20, 21, 22, 23, 24
+    ts(R("LMF", 2, 3), R("LMF", 1, 2), -1.0, A.mult, 1.0, A.add)
+    ts(R("LMF", 5, 6), R("LMF", 0, 1), 0.0, A.is_gt, -512.0, A.mult)
+    tt(R("LMF", 6, 7), R("LMF", 5, 6), q_(15), A.add)
+    for a in (0, 1):
+        tt(R("LMF", 3 + a, 4 + a), R("LMF", 1 + a, 2 + a), R("LMF", 6, 7), A.mult)
+    iota(R("K1"), [[-1, 256]], 0, 0)
+    ts(R("CN"), R("K1"), q_(15), A.mult, R("LMF", 5, 6), A.add)
+    tc(R("SM", 12, 14), R("LMI"))
+    for j in range(2):
+        ts(R("VM", 128 * j, 128 * j + 128), one, R("SM", 12 + j, 13 + j), A.mult)
+        for h in range(2):
+            mm(R("B2", 16 * j + 8 * h, 16 * j + 8 * h + 8), R("VM", 128 * j, 128 * j + 128), R("GS0"), True, True)
+    tc(R("LIM", 0, 32), R("B2", 0, 32))
+    tc(R("LIM", 32, 48), R("LIM", 0, 16))
+    for b in ("VS", "XVS", "MVA", "MVB", "W1"):
+        ms(R(b), 0.0)
+    for u in range(4):
+        ms(R("ME%d" % u, 64, 336), 0.0)
+    cp(R("W2", 512, 768), R("DUM"))
+    cp(R("ALT"), R("TB", NE, NE + 1024))
+    tc(R("SM", 14, 15), R("WTI"))
+    ts(R("WT"), R("WQ"), R("SM", 14, 15), A.mult)
+    ts(R("WB"), R("BO"), R("SM", 14, 15), A.mult)
+    ts(R("WE"), R("WQ"), q_(0), A.mult)
+    ts(R("WQ"), R("WQ"), wc, A.mult)
+    (NN, LIVE, LS, LB, SUU, GRL, N16, HAS, FM, DD, T1, T2, T3, OK, SPL, RK, NV, MN, RK2, IDL, VIS, T4, LV, E1, E2, E3) = range(2, 28)
+    AV, BV, TA, TB2, LL = 32, 36, 40, 44, 48
+    EU = 56
+    ms(R("SM", 16 * LV, 16 * LV + 16), 0.0)
+    ms(S(AV, 128), 0.0)
+    ms(S(AV), -512.0)
+    ms(S(BV), -256.0)
 
     def empties():
-        for b in range(8):
-            mm(R("B2", 64 + 8 * b, 72 + 8 * b), R("IND", 128 * b, 128 * b + 128), R("GS0"), True, True)
-        tc(R("OCB"), R("B2", 64, 128))
-        mm(R("B2", 128, 192), R("TRJ"), R("OCB"), True, False)
-        for j in range(1, 8):
-            mm(R("B2", 128 + 8 * j, 192), R("ONEB"), R("OCB", 0, 64 - 8 * j), False, j == 7)
+        tc(R("OCB"), numbers("B7", 0, "IND", 64, "WE"))
+        mm(R("B7", 64, 128), R("BO"), R("OCB"), True, True)
+        mm(R("B7", 128, 192), R("TSB"), R("OCB"), True, True)
+        u, y = S(EU, 64), S(EU + 4, 64)
+        scan(u, R("ONE", 0, 64), R("B7", 64, 128), A.mult, A.add)
+        ts(S(E1, 1), R("SM", 16 * EU + 63, 16 * EU + 64), -1.0, A.mult, 1024.0, A.add)
+        ts(R("NVB"), R("GS0"), S(E1, 1), A.mult)
+        tt(u, R("CIW", 0, 64), u, A.subtract)
+        tt(u, u, R("B7", 128, 192), A.add)
+        tt(y, R("CIW", 64, 128), R("OCB"), A.mult)
+        tt(u, u, y, A.max)
+        tc(R("LST", 64, 128), u)
         for h in range(2):
-            for j in range(8):
-                mm(R("B2", 192 + 8 * h, 200 + 8 * h), R("ONEB"), R("OCB", 8 * j, 8 * j + 8), j == 0, j == 7)
-        u, y = R("SM", 512, 576), R("SM", 576, 640)
-        tt(u, R("CI"), R("B2", 128, 192), A.subtract)
-        ts(S(NV), R("B2", 192, 208), -1.0, A.mult, 1024.0, A.add)
-        tt(y, R("B2", 128, 192), u, A.subtract)
-        ts(y, y, 1024.0, A.add)
-        tt(y, y, R("OCB"), A.mult)
-        tt(R("E1", 0, 1024, 16), y, u, A.add)
-        tc(R("LST", 64, 128), wide("B2", 256, range(8)))
+            mm(R("B7", 192 + 8 * h, 200 + 8 * h), R("ONEB"), R("NVB"), True, True)
+        tc(S(NV), R("B7", 192, 208))
         tc(I("TB", 0, NE, "LST", 64, 128), R("TB", NE, NE + 1024))
 
-    for t in range(4):
-        cl = t & 3
-        own = lambda h, b="ML": R(b, cl + 512 * h, cl + 512 * h + 512, 4)
-        half = lambda b, h: R(b, 2048 * h, 2048 * h + 2048)
+    def squares(w, bank, kk):
+        for j in range(2):
+            o = R(bank, 256 * j, 256 * j + 256)
+            mm(o, R("IDB"), R("TX", 2 * kk + j, 4096, 16), True, False)
+            mm(o, R("NID"), w, False, True)
+        act(R("SQ", 512 * kk, 512 * kk + 512), R(bank), F.Square)
 
-        def squares(out, win, w, bank, kk):
-            for j in range(2):
-                o = R(bank, 256 * j, 256 * j + 256)
-                mm(o, R("IDB"), R(win, 2 * kk + j, 4096, 16), True, False)
-                mm(o, R("NID"), w, False, True)
-            act(R(out, 512 * kk, 512 * kk + 512), R(bank), F.Square)
-        if t == 0:
-            tc(R("OFO"), R("ML", 0, 1024, 4))
-        tc(half("TX", 0), I("X", 0, NX, "OFO", 0, 128))
-        if t == 0:
-            tc(half("TX", 1), I("X", 0, NX, "OFO", 128, 256))
-        else:
-            act(half("TX", 1), I("X", 0, NX, "OFO", 128, 256), F.Copy)
+    def members(t):
+        own = lambda h, b="ML": R(b, t + 512 * h, t + 512 * h + 512, 4)
+        xs, ls = R("XS%d" % (t % 2)), 16 * (t % 2)
+        tc(R("OFO"), R("ML", t, 1024, 4))
+        for j in range(4):
+            cp(R("TX", 1024 * j, 1024 * j + 1024), I("X", 0, NX, "OFO", 64 * j, 64 * j + 64))
         for h in range(2):
-            o = R("B0", 128 * h, 128 * h + 128)
+            o = hv("B0", h)
             mm(o, own(h), R("IDF"), True, False)
             mm(o, lone, row(0, 128), False, False)
-            mm(o, lone, row(384, 128), False, False)
+            mm(o, lone, row(512, 128), False, False)
             for k in range(16):
                 mm(R("B0", 128 * h + k, 128 * h + 128, 16), R("TX", 2048 * h + k, 2048 * h + 2048, 16), R("G64"), False, k == 15)
         act(R("K1"), R("B0", 0, 256), F.Abs)
         for h in range(2):
             mm(R("B2", 8 * h, 8 * h + 8), own(h, "IND"), g8, True, True)
-        scan(half("US", 0), half("RM", 0), half("TX", 0), A.mult, A.max)
         tc(S(NN), R("B2", 0, 16))
         ts(S(LIVE), S(NN), 0.0, A.is_gt)
-        scan(R("KM"), R("BM"), R("K1"), A.max, A.min)
+        scan(R("KM"), R("BM", 0, 256), R("K1"), A.max, A.min)
         tc(R("SI", 0, 16), R("KM", 15, 256, 16))
         ts(R("SI", 16, 32), R("SI", 0, 16), 4095, A.bitwise_and)
-        ts(S(T1), R("SI", 16, 32), 1.0, A.add)
-        tt(S(T1), S(T1), C(0), A.subtract)
-        tt(S(T1), S(T1), S(LIVE), A.mult)
-        tt(R("E1", 0, 256, 16), S(T1), C(0), A.add)
-        w = wrap(16, "B2", "B3")
-        tc(R("LST", 0, 16), w)
-        ts(R("ACO"), I("AC", 0, NX, "LST", 0, 16), 1, A.add)
-        xs = R("XS")
-        tc(xs, I("X", 0, NX, "LST", 0, 16))
-        if t == 0:
-            owners(2)
+        ts(S(LS), R("SI", 16, 32), 1.0, A.add)
+        tt(S(LS), S(LS), C(0), A.subtract)
+        tt(S(LS), S(LS), S(LIVE), A.mult)
+        tt(S(LS), S(LS), C(0), A.add)
+        tc(R("LST", ls, ls + 16), wrap(LS, 16, "EMA", 0, "B0", 256))
+        tc(xs, I("X", 0, NX, "LST", ls, ls + 16))
+        ts(R("ACO"), I("AC", 0, NX, "LST", ls, ls + 16), 1, A.add)
         tc(R("XE", 0, 4096, 16), xs)
-        scan(R("XSE"), R("RM"), R("XE"), A.mult, A.add)
-        if t == 0:
-            owners(3)
         for h in range(2):
-            act(half("OWG", h), I("OW", 0, NO, "ACO", 128 * h, 128 * h + 128), F.Copy)
-        for h in range(2):
-            tt(half("XA", h), I("X", 0, NX, "ACO", 128 * h, 128 * h + 128), half("XSE", h), A.subtract)
-            act(half("XA", h), half("XA", h), F.Square)
-        if t == 0:
-            rest()
-            empties()
+            scan(half("XSE", h), R("RM"), half("XE", h), A.mult, A.add)
         ts(R("SI", 32, 48), R("SI", 0, 16), 16, A.logical_shift_right)
-        scan(half("US", 1), half("RM", 1), half("TX", 1), A.mult, A.max)
         for h in range(2):
-            mm(R("B2", 16 + 8 * h, 24 + 8 * h), R("US", 2048 * h + 15, 2048 * h + 2048, 16), g8, True, True)
-        tc(S(SUU), R("B2", 16, 32))
-        mm(R("B0"), lone, row(1280, 512), True, False)
+            scan(half("US", h), R("RM"), half("TX", h), A.mult, A.max)
+        tc(R("UC"), R("US", 15, 4096, 16))
         for h in range(2):
-            for k in range(16):
-                mm(R("B0", 256 * h + k, 256 * h + 256, 16), R("OWG", 2048 * h + k, 2048 * h + 2048, 16), R("GC", 16 * cl, 16 * cl + 16), False, False)
+            mm(R("B2", 16 + 8 * h, 24 + 8 * h), hv("UC", h), g8, True, True)
+        tt(S(GRL), R("B2", 16, 32), R("SI", 32, 48), A.subtract)
+        tt(S(GRL), S(GRL), R("LIM", 16, 32), A.is_gt)
+        tt(S(GRL), S(GRL), S(LIVE), A.mult)
+        for kk in range(8):
+            squares(xs, ("B4", "B5")[kk % 2], kk)
         for h in range(2):
-            for k in range(16):
-                mm(R("B0", 256 * h + k, 256 * h + 128, 16), R("XA", 2048 * h + k, 2048 * h + 2048, 16), R("G16"), False, h == 1 and k == 15)
-        for kk in range(5):
-            squares("SQO", "TX", xs, ("B4", "B5")[kk % 2], kk)
-        hv = lambda b, h: R(b, 128 * h, 128 * h + 128)
-        for h in range(2):
-            scan(hv("KD", h), R("BM", 0, 128), R("B0", 256 * h, 256 * h + 128), A.max, A.min)
-        tc(R("E1", 0, 256, 16), R("KD", 15, 256, 16))
-        scan(R("EX"), R("RM", 0, 256), R("E1", 0, 256), A.mult, A.add)
-        for h in range(2):
-            tt(hv("EQ", h), hv("EX", h), R("B0", 256 * h, 256 * h + 128), A.is_equal)
-        for h in range(2):
-            tt(hv("EQ", h), hv("EQ", h), R("B0", 256 * h + 128, 256 * h + 256), A.mult)
-        scan(R("DS"), R("RM", 0, 256), R("EQ"), A.mult, A.add)
-        ts(S(HAS), R("KD", 15, 256, 16), float(2 ** 17), A.is_lt)
-        tt(S(HAS), S(HAS), S(LIVE), A.mult)
-        ts(S(T1), R("DS", 15, 256, 16), float(-cl), A.add)
-        tt(S(T1), S(T1), S(HAS), A.mult)
-        ts(S(DD), S(T1), float(cl), A.add)
-        tc(R("E1", 0, 256, 16), S(DD))
-        w = wrap(16, "B2", "B3", R("EX"))
-        for h in range(2):
-            mm(R("B1", 128 * h, 128 * h + 128), R("EX", 128 * h, 128 * h + 128), R("IDF"), True, True)
-        for kk in range(5, 8):
-            squares("SQO", "TX", xs, ("B4", "B5")[kk % 2], kk)
-        tc(R("LST", 32, 48), w)
-        tc(R("MD"), I("ML", 0, 1280, "LST", 32, 48))
-        tc(R("OFD"), R("MD"))
-        for h in range(2):
-            act(half("TD", h), I("X", 0, NX, "OFD", 128 * h, 128 * h + 128), F.Copy)
-        act(R("INDD"), R("MD"), F.Sign)
-        ts(R("ZI", 0, 256), R("B1", 0, 256), R("LMF", 0, 1), A.mult)
-        ts(R("ZI", 0, 256), R("ZI", 0, 256), 1024, A.bitwise_and)
-        ts(R("CF", 0, 256), R("ZI", 0, 256), 1 / 32, A.mult, -16.0, A.add)
-        ts(R("CF", 256, 512), R("ZI", 0, 256), R("LMF", 5, 6), A.mult, R("LMF", 6, 7), A.add)
-        ts(R("CF", 512, 768), R("ZI", 0, 256), R("LMF", 3, 4), A.mult, R("LMF", 4, 5), A.add)
-        for h in range(2):
-            o = R("B0", 128 * h, 128 * h + 128)
+            o = hv("B0", h, 256)
             mm(o, own(h, "IND"), R("IDV"), True, False)
             mm(o, lone, row(256, 128), False, False)
             for k in range(16):
-                mm(R("B0", 128 * h + k, 128 * h + 128, 16), R("SQO", 256 * k + 128 * h, 256 * k + 128 * h + 128), R("G16"), False, k == 15)
-
-        def leave(h, sq, signs, stop):
-            for k in range(16):
-                for f in range(2):
-                    mm(R("B6", 256 * h + 16 * f + k, 256 * h + 256, 32), R(sq, 256 * k + 128 * h, 256 * k + 128 * h + 128), signs[f], False,
-                       stop and h == 1 and k == 15 and f == 1)
-        mm(R("B6"), lone, row(768, 512), True, False)
+                mm(R("B0", 256 + 128 * h + k, 384 + 128 * h, 16), R("SQ", 256 * k + 128 * h, 256 * k + 128 * h + 128), R("G16"), False, k == 15)
+        scan(R("KB"), R("RM", 0, 256), R("B0", 256, 512), A.mult, A.max)
+        lin(R("KBC"), R("B0", 256, 512), 1.0, -float(2 ** 18))
+        tc(R("SI", 48, 64), R("KB", 15, 256, 16))
+        ts(R("SI", 48, 64), R("SI", 48, 64), 15, A.bitwise_and)
+        tt(S(LB), C(1), R("SI", 48, 64), A.subtract)
+        tc(R("LST", 32, 48), wrap(LB, 16, "EMA", 0, "B0", 0))
+        tc(R("XB"), I("TX", 0, 4096, "LST", 32, 48))
         for h in range(2):
-            leave(h, "SQO", (R("GM1"), g8), False)
+            mm(hv("B6", h, 256), own(h), R("IXS"), True, True)
+        for kk in range(8):
+            squares(R("XB"), ("B4", "B5")[kk % 2], kk)
+        mm(R("B6", 0, 256), lone, row(256, 256), True, False)
+        for k in range(16):
+            for h in range(2):
+                mm(R("B6", 128 * h + k, 128 * h + 128, 16), R("SQ", 256 * k + 128 * h, 256 * k + 128 * h + 128), R("G16"), False, k == 15 and h == 1)
+        tt(R("MM", 256, 512), R("KBC"), R("B6", 0, 256), A.is_gt)
+        tt(R("MM", 0, 256), R("KBC"), R("B6", 0, 256), A.is_le)
+        scan(R("TH2", 0, 256), R("RM", 0, 256), R("MM", 256, 512), A.mult, A.add)
+        tt(R("TH2", 256, 512), R("KC", 256, 512), R("TH2", 0, 256), A.subtract)
+        ts(R("ZI"), R("TH2"), 4369.0, A.mult)
+        ts(R("ZI"), R("ZI"), 4680, A.bitwise_and)
+        for f in range(2):
+            tt(R("B4", 256 * f, 256 * f + 256), R("ZI", 256 * f, 256 * f + 256), R("B6", 256, 512), A.add)
+        tt(R("W"), R("MM"), R("B4"), A.mult)
+        shifts(R("W"), 512, "MVA", "B5", 1)
+        for j in range(4):
+            mm(hv("B6", j), hv("W", j), R("IDK"), True, True)
+        cp(R("W0", 256, 512), R("B6", 0, 256))
+        cp(R("W1", 256, 512), R("B6", 256, 512))
+        if t < 3:
+            moved(R("W2", 256, 512), R("W1", 256, 512), R("B4", 0, 256), R("EQ"))
+        cp(R("W0", 512, 768), R("ML", t, 1024, 4))
+        ts(R("SI", 64, 80), S(NN), 4369.0, A.mult)
+        ts(R("SI", 64, 80), R("SI", 64, 80), 4680, A.bitwise_and)
+        tc(R("ENX"), wide("SI", 64, 16))
+        ts(S(N16), S(NN), -1.0, A.mult, 16.0, A.add)
+        tt(R("FIT"), wide("SM", 16 * N16, 16), R("KC", 0, 256), A.is_gt)
 
-        def firsts(i, b):
+    members(0)
+    empties()
+    for t in range(4):
+        own = lambda h, b="ML": R(b, t + 512 * h, t + 512 * h + 512, 4)
+        xs, ls = R("XS%d" % (t % 2)), 16 * (t % 2)
+        la = 128 + 16 * (t % 2)
+        bas = lambda j, w=16: R("BAS", 64 * t + 16 * j, 64 * t + 16 * j + w)
+        for j in range(4):
+            cp(R("OWG", 1024 * j, 1024 * j + 1024), I("OW", 0, NO, "ACO", 64 * j, 64 * j + 64))
+        for j in range(4):
+            xa = R("XA", 1024 * j, 1024 * j + 1024)
+            tt(xa, I("X", 0, NX, "ACO", 64 * j, 64 * j + 64), R("XSE", 1024 * j, 1024 * j + 1024), A.subtract)
+            act(xa, xa, F.Square)
+        mm(R("B1"), lone, row(640, 512), True, False)
+        for b, w in (("OWG", R("GC", 16 * t, 16 * t + 16)), ("XA", R("G512"))):
+            for h in range(2):
+                for k in range(16):
+                    mm(R("B1", 256 * h + k, 256 * h + 256, 16), R(b, 2048 * h + k, 2048 * h + 2048, 16), w, False, b == "XA" and h == 1 and k == 15)
+        if t == 0:
+            owners(0)
+        scan(R("KD"), R("BM"), R("B1"), A.max, A.min)
+        sk, sl = R3("SK", 0, 2, 0, 16), R3("SL", 0, 2, 0, 16)
+        tc(sk, R("KD", 15, 512, 16))
+        ts(sl, sk, 31, A.bitwise_and)
+        ts(R("SI", 80, 96), R3("SK", 0, 2, 0, 8), 12, A.logical_shift_right, 1024, A.bitwise_and)
+        ts(S(DD), R3("SL", 0, 2, 0, 8), 32.0, A.mult)
+        tt(S(T1), R3("SL", 0, 2, 8, 16), R("SI", 80, 96), A.add)
+        tt(S(DD), S(DD), S(T1), A.add)
+        ts(R("LST", 48, 64), wrap(DD, 16, "EMB", 0, "B2", 32), 1024.0, A.min)
+        tc(R("MD"), I("ML", 0, 1280, "LST", 48, 64))
+        tc(R("OFD"), R("MD"))
+        for j in range(4):
+            cp(R("TD", 1024 * j, 1024 * j + 1024), I("X", 0, NX, "OFD", 64 * j, 64 * j + 64))
+        sign(R("INDD"), R("MD"))
+        ts(S(HAS), S(DD), 1024.0, A.is_lt)
+        tt(S(AV + 1), S(DD), bas(1), A.subtract)
+        tt(S(AV + 3), S(DD), C(3), A.subtract)
+        cp(R("EX"), wide("SM", 16 * DD, 16))
+        for h in range(2):
+            mm(hv("B0", h), hv("EX", h), R("IDF"), True, True)
+        ts(R("ZC"), R("B0", 0, 256), R("LMF", 0, 1), A.mult)
+        ts(R("ZC"), R("ZC"), 1024, A.bitwise_and)
+        tt(R("CF", 0, 256), R("ZC"), R("CN"), A.add)
+        ts(R("CF", 256, 512), R("ZC"), R("LMF", 2, 3), A.mult, R("LMF", 4, 5), A.add)
+        ts(R("CF", 512, 768), R("ZC"), R("LMF", 1, 2), A.mult, R("LMF", 3, 4), A.add)
+        for i in range(6):
+            b = ("B3", "B7")[i % 2]
             if i < 2:
                 h, gs, wd, rw = 0, range(4 * i, 4 * i + 4), 128, "RW1"
             else:
                 h, gs, wd, rw = 1, range(2 * (i - 2), 2 * (i - 2) + 2), 256, "RW2"
             for j, gg in enumerate(gs):
                 p0 = 32 * (gg // 2)
-                o = R(b, wd * j, wd * j + wd)
-                if j and p0 != 32 * (gs[j - 1] // 2):
-                    queue["p"].wait_ge(T.sem["p"], count["p"])
-                    known["p"]["p"] = count["p"]
-                mm(o, R("ONEB", 0, 128, 1, p0, p0 + 1), R("ROW", 512, 512 + wd, 1, p0, p0 + 1), True, False)
                 c = 256 + 256 * (gg % 2) + 128 * h
-                mm(o, R("CF", c, c + 128, 1, p0, p0 + 32), R("CF", 0, wd, 1, p0, p0 + 32), False, True)
-            return gs, wd, rw, h, b
-
-        def firsts2(r):
-            gs, wd, rw, h, b = r
+                mm(R(b, wd * j, wd * j + wd), R("CF", c, c + 128, 1, p0, p0 + 32), R("CF", 0, wd, 1, p0, p0 + 32), True, True,
+                   j > 0 and p0 != 32 * (gs[j - 1] // 2))
             scan(R("FS"), R(rw), R(b), A.mult, A.max)
             tc(R("SM", 16 * FM + 8 * h + gs[0], 16 * FM + 8 * h + gs[0] + len(gs)), R("FS", wd - 1, 512, wd))
-        rr = [firsts(i, ("B3", "B7")[i]) for i in range(2)]
-        scan(R("KB"), R("RM", 0, 256), R("B0", 0, 256), A.mult, A.max)
-        tc(R("SI", 48, 64), R("KB", 15, 256, 16))
-        ts(R("SI", 48, 64), R("SI", 48, 64), 15, A.bitwise_and)
-        tt(R("E1", 0, 256, 16), C(1), R("SI", 48, 64), A.subtract)
-        w = wrap(16, "B2", "B1")
-        tc(R("LST", 16, 32), w)
-        tc(R("XB"), I("TX", 0, 4096, "LST", 16, 32))
-        xb = R("XB")
-        for i in range(2):
-            firsts2(rr[i])
-            rr.append(firsts(i + 2, ("B3", "B7")[i]))
-        for i in range(2):
-            firsts2(rr[i + 2])
-            rr.append(firsts(i + 4, ("B3", "B7")[i]))
+        for h in range(2):
+            mm(hv("B0", h, 256), hv("MD", h), R("IXS"), True, True)
+        tt(R("B0", 256, 512), R("ENX"), R("B0", 256, 512), A.add)
+        tt(R("WM"), R("FIT"), R("B0", 256, 512), A.mult)
+        shifts(R("WM"), 256, "MVB", "B0", -1)
+        for h in range(2):
+            mm(hv("B0", h, 256), hv("WM", h), R("IDK"), True, True)
+        tt(R("W0", 0, 256), R("W0", 512, 768), R("B0", 256, 512), A.add)
+        if t < 3:
+            moved(R("W2", 0, 256), R("MD"), R("B6", 0, 256), R("EQ2"))
+        for h in range(2):
+            mm(R("B2", 48 + 8 * h, 56 + 8 * h), hv("INDD", h), g8, True, False)
+            mm(R("B2", 48 + 8 * h, 56 + 8 * h), own(h, "IND"), g8, False, True)
+        ts(S(T2), R("B2", 48, 64), 16.0, A.is_le)
+        tt(S(T2), S(T2), S(HAS), A.mult)
         for h in range(2):
             for k in range(16):
-                mm(R("B0", 128 * h + k, 128 * h + 128, 16), R("TD", 2048 * h + k, 2048 * h + 2048, 16), g8, True, True)
-            mm(R("B1", 8 * h, 8 * h + 8), R("INDD", 128 * h, 128 * h + 128), g8, True, False)
-            mm(R("B1", 8 * h, 8 * h + 8), own(h, "IND"), g8, False, True)
-        act(R("KA"), R("B0", 0, 256), F.Abs)
-
-        for i in range(2):
-            firsts2(rr[i + 4])
+                mm(R("B1", 128 * h + k, 128 * h + 128, 16), R("TD", 2048 * h + k, 2048 * h + 2048, 16), g8, True, True)
+        act(R("KA"), R("B1", 0, 256), F.Abs)
         for h in range(2):
-            scan(half("UD", h), half("RM", h), half("TD", h), A.mult, A.max)
-        tt(R("VM"), R("US", 15, 4096, 16), R("UD", 15, 4096, 16), A.max)
-        for kk in range(2):
-            squares("SQB", "TX", xb, ("B4", "B5")[kk], kk)
-        for h in range(2):
-            mm(R("B1", 16 + 8 * h, 24 + 8 * h), R("VM", 128 * h, 128 * h + 128), g8, True, True)
-        for kk in range(2, 8):
-            squares("SQB", "TX", xb, ("B4", "B5")[kk % 2], kk)
-        scan(R("MSD"), R("BM"), R("KA"), A.max, A.min)
-        tt(S(GR), S(SUU), R("SI", 32, 48), A.subtract)
-        tt(S(GR), S(GR), R("LIM", 16, 32), A.is_gt)
-        tt(S(FM), S(FM), C(2), A.is_equal)
-        tt(S(MS), R("SI", 32, 48), R("MSD", 15, 256, 16), A.min)
-        tt(S(FM), S(FM), S(HAS), A.mult)
-        tt(S(MS), S(MS), R("LIM", 32, 48), A.add)
-        ts(S(T1), R("B1", 0, 16), 16.0, A.is_le)
-        tt(S(T2), R("B1", 16, 32), S(MS), A.is_le)
-        tt(S(FM), S(FM), S(T1), A.mult)
-        mer = R("SB", 0, 16)
-        tt(mer, S(FM), S(T2), A.mult)
-        ts(S(NM), mer, -1.0, A.mult, 1.0, A.add)
-        tt(S(NM), S(NM), S(LIVE), A.mult)
-        want = R("SB", 16, 32)
-        tt(want, S(GR), S(NM), A.mult)
-
-        def ranks(bank, s):
-            mm(R(bank, 0, 8), R("TRI"), R("SB", s, s + 8), True, True)
-            mm(R(bank, 8, 16), R("TRI"), R("SB", s + 8, s + 16), True, False)
-            mm(R(bank, 8, 16), R("ONEB"), R("SB", s, s + 8), False, True)
-        ranks("B1", 16)
-        mm(R("B1", 32, 48), R("ONEB"), mer, True, True)
-        ts(S(T1), S(DD), float(NE), A.add)
-        tt(S(T2), S(DD), C(6 + t), A.subtract)
-        tt(S(T1), S(T1), C(3), A.subtract)
-        tt(S(T2), S(T2), mer, A.mult)
-        tt(S(T1), S(T1), mer, A.mult)
-        tt(R("E1", 512, 768, 16), S(T2), C(6 + t), A.add)
-        tc(S(RK), R("B1", 0, 16))
+            scan(half("UD", h), R("RM"), half("TD", h), A.mult, A.max)
+            tt(hv("VM", h), hv("UC", h), R("UD", 2048 * h + 15, 2048 * h + 2048, 16), A.max)
+            mm(R("B2", 64 + 8 * h, 72 + 8 * h), hv("VM", h), g8, True, True)
+        scan(R("MSD"), R("BM", 0, 256), R("KA"), A.max, A.min)
+        tt(S(T3), R("SI", 32, 48), R("MSD", 15, 256, 16), A.min)
+        tt(S(T3), S(T3), R("LIM", 32, 48), A.add)
+        tt(S(OK), S(FM), C(2), A.is_equal)
+        tt(S(OK), S(OK), S(T2), A.mult)
+        tt(S(T3), S(T3), R("B2", 64, 80), A.is_ge)
+        mer, want, nm = R("SB", 0, 16), R("SB", 16, 32), R("SB", 32, 48)
+        tt(mer, S(T3), S(OK), A.mult)
+        tt(want, S(GRL), mer, A.is_gt)
+        tt(nm, S(LIVE), mer, A.subtract)
+        mm(R("B2", 80, 112), R("TRI"), R("SB", 16, 48), True, False)
+        mm(R("B2", 88, 96), R("ONEB"), R("SB", 16, 24), False, False)
+        mm(R("B2", 104, 112), R("ONEB"), R("SB", 32, 40), False, True)
+        tt(S(TA, 64), again("SB", 0, 4), S(AV, 64), A.mult)
+        tt(S(TA, 64), S(TA, 64), bas(0, 64), A.add)
+        tc(S(RK), R("B2", 80, 96))
+        tt(S(MN), S(NV), R("B2", 80, 96), A.min)
+        tt(S(RK2), R("B2", 96, 112), S(MN), A.subtract)
         tt(S(SPL), S(RK), S(NV), A.is_lt)
         tt(S(SPL), S(SPL), want, A.mult)
-        tt(R("SB", 32, 48), S(NM), S(SPL), A.subtract)
-        ranks("B0", 32)
-        for h in range(2):
-            leave(h, "SQB", (g8, R("GM1")), True)
-        tt(S(T2), S(RK), C(3), A.subtract)
-        tt(S(RV), S(RK), C(10 + t), A.subtract)
-        tt(S(T2), S(T2), S(SPL), A.mult)
-        tt(S(RV), S(RV), S(SPL), A.mult)
-        tt(S(T1), S(T1), S(T2), A.add)
-        tt(R("E1", 256, 512, 16), S(RV), C(10 + t), A.add)
-        tt(R("E1", 0, 256, 16), S(T1), C(3), A.add)
-        ts(S(VIS), R("B0", 0, 16), 64.0, A.is_lt)
-        tt(S(T2), R("B0", 0, 16), C(4), A.subtract)
-        tt(S(VIS), S(VIS), R("SB", 32, 48), A.mult)
-        tt(S(T2), S(T2), S(VIS), A.mult)
-        tt(R("E1", 768, 1024, 16), S(T2), C(4), A.add)
-        tc(R("LST", 128, 192), wide("B2", 0, (6, 7, 4, 5, 0, 1, 2, 3)))
+        tt(S(IDL), nm, S(SPL), A.subtract)
+        ts(S(VIS), S(RK2), 64.0, A.is_lt)
+        tt(S(T4), S(RK2), C(4), A.subtract)
+        tt(S(VIS), S(VIS), S(IDL), A.mult)
+        tt(S(T4), S(T4), S(VIS), A.mult)
+        tt(S(LL + 4), S(T4), C(4), A.add)
+        tt(S(BV + 2, 32), again("SM", 16 * RK, 2), bas(2, 32), A.subtract)
+        tt(S(TB2, 64), again("SM", 16 * SPL, 4), S(BV, 64), A.mult)
+        tt(S(LL, 64), S(TA, 64), S(TB2, 64), A.add)
+        tc(R("LST", la, la + 16), wrap(LL + 4, 16, "EMW", 1024, "B2", 112))
         dst = (rank + 1 + t % (n - 1)) % n
         src = (rank - 1 - t % (n - 1)) % n
-        tc(I("VS", 0, 336, "LST", 176, 192), xs)
+        tc(I("VS", 0, 336, "LST", la, la + 16), xs)
         send(dst, "XV%d" % t, "VS", "va%d" % t, "vl%d" % t)
-        tc(R("MD"), I("ML", 0, 1280, "LST", 160, 176))
-        for h in range(2):
-            o = R("B7", 256 * h, 256 * h + 256)
-            mm(o, own(h), R3("IXA", 0, 8, 0, 32), True, False)
-            mm(o, R("MD", 128 * h, 128 * h + 128), R3("IXB", 0, 8, 0, 32), False, True)
-        ts(S(T1), mer, -2.0, A.mult, 1.0, A.add)
-        ts(R("E2", 0, 512, 32), S(SPL), -1.0, A.add, BIG, A.mult)
-        tt(S(T1), S(T1), S(SPL), A.subtract)
-        ts(S(AA), S(NN), -1.0, A.mult, 16.0, A.add)
-        ts(R("E2", 16, 512, 32), S(T1), BIG, A.mult)
-        tt(S(AA), S(AA), mer, A.mult)
-        scan(R("THB"), R("RM", 0, 512), R("E2"), A.mult, A.add)
-        tt(R("PRS"), R("B6"), R("THB"), A.is_ge)
-        ts(R("THC"), R("PRS"), -1.0, A.mult, 1.0, A.add)
-        tt(R("THC", 16, 512, 32), R("THC", 16, 512, 32), S(AA), A.add)
-        scan(R("THB"), R("RM", 0, 512), R("THC"), A.mult, A.add)
-        ts(R("ZI"), R("THB"), 4369.0, A.mult)
-        ts(R("ZI"), R("ZI"), 4680, A.bitwise_and)
-        tt(R("B3"), R("ZI"), R("B7"), A.add)
-        tt(w2(), R("B3"), R("PRS"), A.mult)
-        tc(R3("F2", 0, 16, 0, 16), R3("W", 0, 16, 16, 32))
-        for h in range(2):
-            mm(R("B0", 128 * h, 128 * h + 128), R3("F2", 8 * h, 8 * h + 8, 0, 16), R("IDK"), True, True)
-        tc(R("XE", 0, 4096, 16), I("TB", 0, NE + 1280, "LST", 144, 160))
-        tc(R("TG"), I("TB", 0, NE + 1280, "LST", 128, 144))
-        for q in range(16):
-            mm(R("B4", 0, 16), R("WQ", 128 * q, 128 * q + 128), R("TG", q, 256, 16), q == 0, q == 15)
-        if t < 3:
-            addup(R("SM", 400, 401), R("B1", 32, 48))
-        tc(R("SI", 0, 256), R("B0", 0, 256))
-        ts(R("SI", 0, 256), R("SI", 0, 256), 8191, A.bitwise_and)
-        moved(R("SI", 0, 256), "MVO")
-        settle("MVO")
-        tc(R("LST", 48, 64), R("B4", 0, 16))
-        for th, s in ((4096.0, 1), (512.0, 2), (64.0, 4)):
-            ts(R("B5"), w2(), -th, A.mult, th * th, A.add)
-            ts(R("B3"), w2(), -th, A.add, 0.0, A.max)
-            tt(R("TH"), w2(), R("B5"), A.min)
-            ts(R3("W", 15, 16, 24, 32), R("TH", 504, 512), 0.0, A.max)
-            tt(R3("W", 0, 15, 0, 32), R("TH", 0, 480), R("B3", s, 480 + s), A.max)
-            tt(R3("W", 15, 16, 0, 32 - s), R("TH", 480, 512 - s), R("B3", 480 + s, 512), A.max)
-        h3 = lambda a, b: R3("H3", 0, 16, a, b)
-        ts(R("B5"), w2(), -8.0, A.mult, 64.0, A.add)
-        ts(h3(0, 32), w2(), -8.0, A.add, 0.0, A.max)
-        tt(w2(), w2(), R("B5"), A.min)
-        tt(R3("F2", 0, 16, 0, 8), R3("W", 0, 16, 16, 24), h3(24, 32), A.max)
-        ts(R3("F2", 0, 16, 8, 16), R3("W", 0, 16, 24, 32), 0.0, A.max)
-        tt(R3("F1", 0, 16, 0, 16), R3("W", 0, 16, 0, 16), h3(8, 24), A.max)
-        for j, f in ((256, "F2"), (0, "F1")):
-            for h in range(2):
-                mm(R("B7", j + 128 * h, j + 128 * h + 128), R3(f, 8 * h, 8 * h + 8, 0, 16), R("IDK"), True, True)
-        tc(R("L2"), R("B7", 256, 512))
-        tc(R("ML", cl, 1024, 4), R("B7", 0, 256))
-        tc(I("ML", 0, 1280, "LST", 48, 64), R("L2"))
-        if t < 3:
-            act(R("IND"), ml, F.Sign)
-            tc(R("SI", 240, 241), R("SM", 400, 401))
-            ts(R("SI", 240, 241), R("SI", 240, 241), 15, A.bitwise_and)
-            tc(R("SM", 400, 401), R("SI", 240, 241))
-            ts(R("LIM", 32, 48), R("LIM", 0, 16), R("SM", 400, 401), A.add)
-        else:
-            ts(R("E1"), ml, 0.0, A.is_equal, 4097.0, A.mult)
-            tt(R("E1"), R("E1"), ml, A.add)
-            ts(R("E1"), R("E1"), -1.0, A.add)
-            dma("oy", T.ym[:, :], T.E1[:, :], R("E1")[1], [])
-            ms(R("KB"), 0.0)
-        ev = R("E1", 0, 128, 16, 0, 64) if t < 3 else R("KB", 0, 128, 16, 0, 64)
-        ew = R("E1", 0, 128, 1, 0, 64) if t < 3 else R("KB", 0, 128, 1, 0, 64)
+        tc(R("LST", 208, 224), wrap(LL + 3, 16, "EMW", 768, "B2", 176))
+        tc(R("LST", 160, 208), wrap(LL, 48, "EMW", 0, "B2", 128))
+        tc(R("TG"), I("TB", 0, NE + 1280, "LST", 208, 224))
+        tc(R("LST", 224, 240), numbers("B2", 192, "TG", 16))
+        tc(R("ML", t, 1024, 4), I("W0", 0, 768, "LST", 160, 176))
+        tc(R("L2"), I("W1", 0, 768, "LST", 160, 176))
+        tc(I("ML", 0, 1280, "LST", 224, 240), R("L2"))
+        tc(R("XE2", 0, 4096, 16), I("TB", 0, NE + 1280, "LST", 192, 208))
+        tc(I("ALT", 0, 1024, "LST", 176, 192), R("XE2", 0, 4096, 16))
         xv = "XV%d" % t
-        arrive("va%d" % t, xv)
-        for q in range(16):
-            mm(R("B2", 64, 68), R("WT", 128 * q, 128 * q + 128), R(xv, q, 64, 16), q == 0, q == 15)
-        tc(R("SI", 0, 4), R("B2", 64, 68))
-        ts(R("SI", 0, 4), R("SI", 0, 4), 4095, A.bitwise_and)
-        ts(R("LST", 192, 196), R("SI", 0, 4), 1, A.add)
+        tc(R("SJ", 0, 4), numbers("B1", 128, xv, 4, "WT"))
+        mm(R("B1", 192, 256), R("WB"), R(xv), True, True)
+        ts(R("SJ", 0, 4), R("SJ", 0, 4), 4095, A.bitwise_and)
+        ts(R("LST", 240, 244), R("SJ", 0, 4), 1, A.add)
+        tc(R("OVG"), I("OW", 0, NO, "LST", 240, 244))
+        if t < 3:
+            tc(R("MVO"), I("W2", 0, 768, "LST", 160, 176))
+            settle("MVO")
+            mm(R("B2", 208, 224), R("ONEB"), mer, True, True)
+            addup(S(E2, 1), R("B2", 208, 224))
+            tc(R("SI", 96, 97), S(E2, 1))
+            ts(R("SI", 96, 97), R("SI", 96, 97), 15, A.bitwise_and)
+            tc(S(E2, 1), R("SI", 96, 97))
+            ts(R("LIM", 32, 48), R("LIM", 0, 16), S(E2, 1), A.add)
+            sign(R("IND"), ml)
+            members(t + 1)
+            empties()
+        else:
+            ym = R("YM", 0, 1024)
+            ts(ym, ml, 0.0, A.is_equal, 4097.0, A.mult)
+            tt(ym, ym, ml, A.add)
+            ts(ym, ym, -1.0, A.add)
+            dma("oy", [(T.ym[:, :], ym[0])], ym[1], [])
+        tc(R("SJ", 64, 128), R("B1", 192, 256))
+        ts(R("SJ", 64, 128), R("SJ", 64, 128), 4095, A.bitwise_and)
+        ts(R("VF"), R("SJ", 64, 128), 1, A.add)
         tc(R("XVS", 0, 1024, 16), R(xv))
         scan(R("XVE"), R("RM", 0, 1024), R("XVS"), A.mult, A.add)
-        tc(R("OVG"), I("OW", 0, NO, "LST", 192, 196))
-        for q in range(16):
-            mm(R("B2", 64, 68), R("WQ", 128 * q, 128 * q + 128), R("OVG", q, 64, 16), q == 0, q == 15)
-        tc(R("LST", 200, 204), R("B2", 64, 68))
-        tc(R("HL"), I("ML", 0, 1280, "LST", 200, 204))
+        tc(R("LST", 244, 248), numbers("B1", 132, "OVG", 4))
+        tc(R("AVG"), I("ALT", 0, 1024, "LST", 244, 248))
+        tc(R("HL1"), I("ML", 0, 1280, "LST", 244, 248))
+        tc(R("LST", 248, 252), numbers("B1", 136, "AVG", 4))
+        tt(R("EQV"), R("HL1"), R("VF"), A.is_equal)
+        mm(R("B1", 256, 320), R("BO"), R("EQV"), True, True)
+        tc(R("HL2"), I("ML", 0, 1280, "LST", 248, 252))
+        tt(R("HL1"), R("HL1"), R("HL2"), A.subtract)
+        tt(R("HL1"), R("HL1"), R("B1", 256, 320), A.mult)
+        tt(R("HL1"), R("HL1"), R("HL2"), A.add)
+        tc(R("HL"), R("HL1"))
         tt(R("VD"), I("X", 0, NX, "HL", 0, 64), R("XVE"), A.subtract)
         act(R("SQV"), R("VD"), F.Square)
-        mm(R("B0", 0, 128, 1, 0, 64), R("ONEB", 0, 64, 1, 0, 1), row(128, 128), True, False)
+        mm(R("B1", 0, 128, 1, 0, 64), R("ONEB", 0, 64, 1, 0, 1), row(128, 128), True, False)
         for k in range(16):
-            mm(R("B0", k, 128, 16, 0, 64), R("SQV", k, 1024, 16), R("G16"), False, k == 15)
-        scan(R("KD", 0, 128, 1, 0, 64), R("BM", 0, 128, 1, 0, 64), R("B0", 0, 128, 1, 0, 64), A.max, A.min)
-        tc(R("SI", 0, 8, 1, 0, 64), R("KD", 15, 128, 16, 0, 64))
-        ts(R("SI", 0, 8, 1, 0, 64), R("SI", 0, 8, 1, 0, 64), 15, A.bitwise_and)
-        tt(ev, R("SI", 0, 8, 1, 0, 64), R("CO", 80, 88, 1, 0, 64), A.add)
-        scan(R("B3", 0, 128, 1, 0, 64), R("RM", 0, 128, 1, 0, 64), ew, A.mult, A.add)
-        tt(R("EM", 0, 128, 1, 0, 64), R("B3", 0, 128, 1, 0, 64), R("QM", 0, 128, 1, 0, 64), A.mult)
-        mm(R("B2", 64, 68), R("EM", 0, 128, 1, 0, 64), R("RB", 0, 4, 1, 0, 64), True, True)
-        tc(R("LST", 208, 212), R("B2", 64, 68))
-        tc(R("SI", 64, 128), I("VD", 0, 1024, "LST", 208, 212))
-        ts(R("SI", 64, 128), R("SI", 64, 128), 1, A.arith_shift_right)
-        tc(R("RET"), R("SI", 64, 128))
+            mm(R("B1", k, 128, 16, 0, 64), R("SQV", k, 1024, 16), R("G16"), False, k == 15)
+        scan(R("KV", 0, 128, 1, 0, 64), R("BM", 0, 128, 1, 0, 64), R("B1", 0, 128, 1, 0, 64), A.max, A.min)
+        tc(R("SJ", 8, 16, 1, 0, 64), R("KV", 15, 128, 16, 0, 64))
+        ts(R("SJ", 8, 16, 1, 0, 64), R("SJ", 8, 16, 1, 0, 64), 15, A.bitwise_and)
+        tt(R("SM", 16 * LV, 16 * LV + 8, 1, 0, 64), R("SJ", 8, 16, 1, 0, 64), R("CO", 80, 88, 1, 0, 64), A.add)
+        tt(R("EMV"), wide("SM", 16 * LV, 8), R("QM", 0, 128), A.mult)
+        mm(R("B1", 140, 144), R("EMV", 0, 128, 1, 0, 64), R("RB", 0, 4, 1, 0, 64), True, True)
+        tc(R("LST", 252, 256), R("B1", 140, 144))
+        tc(R("SJ", 64, 128), I("VD", 0, 1024, "LST", 252, 256))
+        ts(R("SJ", 64, 128), R("SJ", 64, 128), 1, A.arith_shift_right)
+        tc(R("RET"), R("SJ", 64, 128))
         send(src, "ME%d" % t, "RET", "ra%d" % t, "rl%d" % t)
-        if t < 3:
-            tc(R("OFO"), R("ML", cl + 1, 1024, 4))
-            empties()
-        arrive("ra%d" % t, "ME%d" % t)
-        tt(R("NX1"), I("ME%d" % t, 0, 336, "LST", 176, 192), xs, A.add)
-        tc(I("X", 0, NX, "LST", 0, 16), R("NX1"))
-    dma("ox", T.yx[:, :], T.X[:, 1:4097], R("X", 1, 4097)[1], [])
+        tt(R("NX1"), I("ME%d" % t, 0, 336, "LST", la, la + 16), xs, A.add)
+        tc(I("X", 0, NX, "LST", ls, ls + 16), R("NX1"))
+    dma("ox", [(T.yx[:, :], T.X[:, 1:4097])], R("X", 1, 4097)[1], [])
+
+    if "order" not in PLAN:
+        PLAN["order"] = plan(calls)
+    count = {}
+    known = {q: {} for q in queue}
+    mark = {}
+    for i, q in PLAN["order"]:
+        c = calls[i]
+        e = c["sem"] or q
+        if q == "x":
+            count[e] = -c["inc"]
+            mark[i] = (e, count[e], {e: count[e]})
+            continue
+        best = {}
+        for j, inline in c["dep"].items():
+            if not inline and best.get(mark[j][0], (0,))[0] < mark[j][1]:
+                best[mark[j][0]] = mark[j][1:]
+        for k, (v, ck) in sorted(best.items(), key=lambda x: -x[1][0]):
+            if known[q].get(k, 0) < v:
+                queue[q].wait_ge(T.sem[k], v)
+                for a, b in ck.items():
+                    known[q][a] = max(known[q].get(a, 0), b)
+        x = c["f"][q]()
+        if c["inc"] > 0:
+            x.then_inc(T.sem[e], 16 if q == "y" else 1)
+        count[e] = count.get(e, 0) + abs(c["inc"])
+        ck = dict(known[q])
+        ck[e] = count[e]
+        mark[i] = (e, count[e], ck)
     for k in ("dm", "dx", "da", "dl", "dw", "ox", "oy", "v", "s", "p", "gg"):
         g.sync.wait_ge(T.sem[k], count[k])
     for t in range(4):

@@ -3,7 +3,7 @@ AX = AxisListType.X
 
 NX = 4368
 NO = 8576
-NE = 2064
+NE = 1024
 D0 = 4352
 
 
@@ -17,9 +17,9 @@ def _sb(spec):
 
 
 SCRATCH = _sb({
-    "bfloat16": "X:4368 TB:3344 TX:4096 XE:4096 SQ:4096 XSE:4096 XA:4096 OWG:4096 RM:2048 QM:768 BM:512 ROW:1152 WQ:2048 WT:2048 "
+    "bfloat16": "X:4368 TX:4096 XE:4096 SQ:4096 XSE:4096 XA:4096 OWG:4096 RM:2048 QM:768 BM:512 ROW:1152 WQ:2048 WT:2048 "
                 "WE:2048 RW1:512 RW2:512 IND:1024 CF:768 MM:512 TH2:512 KC:512 ALT:1024 VS:336 XVE:1024 XVS:1024 VD:1024 RET:64",
-    "float32": "OW:8576 ML:1280 VAL:4096 KD:512 EMW:1280 SM:1024 W:512 MVA:528 MVB:272 W0:768 W1:768 W2:768",
+    "float32": "OW:8576 TB:2304 ML:1280 VAL:4096 KD:512 EMW:1280 SM:1024 W:512 MVA:528 MVB:272 W0:768 W1:768 W2:768",
     "int32": "AC:4368 MI:1024 LMI:2 WTI:1 SJ:128 SK:2x16 SL:2x16",
     "uint16": "OFO:256 ACO:256 OFD:256 MVO:256 MV2:256 LST:256 HL:64 SOF:80 SRP:4"})
 WIDTH = {k: v[1][1] * (v[1][2] if len(v[1]) > 2 else 1) for k, v in SCRATCH.items()}
@@ -50,56 +50,70 @@ for _k, _v, _at, _w in (("US", "OWG", 0, 4096), ("UD", "OWG", 0, 4096), ("TD", "
 SEMAPHORES = ["v", "s", "p", "gg", "dx", "da", "dm", "dl", "dw", "oy", "ox"] + ["%s%d" % (a, b) for a in ("va", "vl", "ra", "rl") for b in range(4)]
 PSUM = ["B%d" % b for b in range(8)]
 SIZE = {"float32": 4, "int32": 4, "bfloat16": 2, "uint16": 2}
-COST = {"cy": 0.9, "gat": 1.5, "sca": 3.0, "pe": 0.65, "wake": 80.0, "far": 3000.0, "dma": 3000.0, "look": 400.0}
+COST = {"cy": 0.9, "gat": 1.5, "sca": 3.0, "pe": 0.65, "wake": 80.0, "far": 3000.0, "dma": 3000.0, "look": 200.0, "cut": 8, "sf": (2, 3, 4, 5), "turns": 4, "short": 256, "b": 0.6}
 PLAN = {}
 
 
-def plan(calls):
-    n = len(calls)
-    wake = COST["wake"]
-    after = [[] for _ in calls]
-    for i, c in enumerate(calls):
-        for j in c["dep"]:
-            after[j].append(i)
-    rank = [0.0] * n
-    for i in range(n - 1, -1, -1):
-        c = calls[i]
-        rank[i] = min(c["ns"].values()) + c["lat"] + max([rank[j] + wake for j in after[i]] + [0.0])
-    left = [len(c["dep"]) for c in calls]
-    ready = [0.0] * n
-    where = [None] * n
+def issue(ns, after, rank):
+    n = len(ns)
+    left = [0] * n
+    for a in after:
+        for j, _ in a:
+            left[j] += 1
+    ready, end = [0.0] * n, [0.0] * n
     free = {q: 0.0 for q in ("v", "s", "p", "gg", "y", "x")}
     pool = {q: set() for q in free}
     order = []
 
     def enter(i):
-        for q in calls[i]["ns"]:
+        for q in ns[i]:
             pool[q].add(i)
     for i in range(n):
         if not left[i]:
             enter(i)
     while len(order) < n:
-        q = min((q for q in free if pool[q]), key=lambda q: max(free[q], min(ready[i] for i in pool[q])))
-        now = max(free[q], min(ready[i] for i in pool[q]))
-        i = max((i for i in pool[q] if ready[i] <= now + COST["look"]), key=lambda i: (rank[i], -i))
+        now, q = min((max(free[q], min(ready[i] for i in pool[q])), q) for q in free if pool[q])
+        near = [i for i in pool[q] if ready[i] <= now + COST["look"]]
+        if q == "v":
+            near = [i for i in near if len(ns[i]) == 1 or free["s"] > max(now, ready[i]) + COST["b"] * ns[i]["v"]]
+            if not near:
+                free[q] = now + 100.0
+                continue
+        i = max(near, key=lambda i: (rank[i], -i))
         if ready[i] > now:
-            fit = [j for j in pool[q] if max(now, ready[j]) + calls[j]["ns"][q] <= ready[i]]
+            fit = [j for j in near if max(now, ready[j]) + ns[j][q] <= ready[i]]
             if fit:
                 i = max(fit, key=lambda i: (rank[i], -i))
-        start = max(now, ready[i])
-        c = calls[i]
-        free[q] = start + c["ns"][q]
-        where[i] = q
-        order.append(i)
-        for k in c["ns"]:
+        free[q] = end[i] = max(now, ready[i]) + ns[i][q]
+        order.append((i, q))
+        for k in ns[i]:
             pool[k].discard(i)
-        for j in after[i]:
-            inline = c["dep"] is not None and calls[j]["dep"][i]
-            ready[j] = max(ready[j], free[q] + (0.0 if inline else c["lat"] + wake))
+        for j, gap in after[i]:
+            ready[j] = max(ready[j], end[i] + gap)
             left[j] -= 1
             if not left[j]:
                 enter(j)
-    return [(i, where[i]) for i in order]
+    return order, end
+
+
+def plan(calls):
+    ns = [c["ns"] for c in calls]
+    after, before = [[] for _ in calls], [[] for _ in calls]
+    for i, c in enumerate(calls):
+        for j, inline in c["dep"].items():
+            gap = 0.0 if inline else calls[j]["lat"] + COST["wake"]
+            after[j].append((i, gap))
+            before[i].append((j, gap))
+    rank = [0.0] * len(calls)
+    for i in range(len(calls) - 1, -1, -1):
+        rank[i] = min(ns[i].values()) + max([rank[j] + gap for j, gap in after[i]] + [calls[i]["lat"]])
+    best = issue(ns, after, rank)
+    now = best
+    for _ in range(COST["turns"]):
+        now = issue(ns, after, issue(ns, before, now[1])[1])
+        if max(now[1]) < max(best[1]):
+            best = now
+    return best[0]
 
 
 def rank_program(g, core, T, topo):
@@ -199,10 +213,14 @@ def rank_program(g, core, T, topo):
         return x[0] if isinstance(x, tuple) else x
 
     def tc(o, i):
-        vop(lambda: g.vector.tensor_copy(o[0], i[0]), o, [i])
+        floats = len(o[1]) == 1 and all(SCRATCH[x[1][0][0]][2] in ("float32", "bfloat16") for x in (o, i))
+        short = len(i[1]) == 1 and o[2] > COST["short"] and SIZE[SCRATCH[o[1][0][0]][2]] + SIZE[SCRATCH[i[1][0][0]][2]] == 4
+        other = (lambda: g.scalar.activation(o[0], i[0], F.Copy)) if floats and not short else None
+        vop(lambda: g.vector.tensor_copy(o[0], i[0]), o, [i], other=other)
+    cp = tc
 
-    def cp(o, i):
-        vop(lambda: g.vector.tensor_copy(o[0], i[0]), o, [i], other=lambda: g.scalar.activation(o[0], i[0], F.Copy))
+    def put(o, i):
+        vop(lambda: g.vector.tensor_copy(o[0], i[0]), o, [i], other=lambda: g.scalar.activation(o[0], i[0], F.Silu))
 
     def tt(o, a, b, f):
         vop(lambda: g.vector.tensor_tensor(o[0], a[0], b[0], f), o, [a, b], True)
@@ -237,6 +255,10 @@ def rank_program(g, core, T, topo):
     def act(o, i, f):
         rd, wr = sides(o, [i])
         call({"s": (lambda: g.scalar.activation(o[0], i[0], f), ns("s", o, [i]))}, rd, wr)
+
+    def over(acc, i, bias, o):
+        call({"s": (lambda: g.scalar.activation(o[0], i[0], F.Relu, bias=bias[0], accum_out=acc[0]), 20 + ns("s", o, [i]))},
+             i[1] + bias[1], o[1] + acc[1])
 
     def mm(o, l, r, a, z, fence=False):
         t = max(min(64, l[2]), r[2]) * (4 if SIZE[SCRATCH[l[1][0][0]][2]] == 4 else 1) * COST["pe"]
@@ -292,9 +314,11 @@ def rank_program(g, core, T, topo):
         tt(o, x, ids, A.add)
 
     def settle(mv):
-        for h in range(2):
-            scan(half("VAL", h), R("RM"), half("XE2", h), A.mult, A.add)
-            act(I("OW", 0, NO, mv, 128 * h, 128 * h + 128), half("VAL", h), F.Silu)
+        for j in range(4):
+            scan(R("VAL", 1024 * j, 1024 * j + 1024), R("RM", 0, 1024), R("XE2", 1024 * j, 1024 * j + 1024), A.mult, A.add)
+        w = 4096 // COST["cut"]
+        for j in range(0, 4096, w):
+            put(I("OW", 0, NO, mv, j // 16, (j + w) // 16), R("VAL", j, j + w))
 
     def owners(u):
         mv = ("MVO", "MV2")[u % 2]
@@ -415,6 +439,9 @@ def rank_program(g, core, T, topo):
     lanes(C(0), 4097, 1)
     lanes(C(1), 15, 16)
     lanes(C(2), 11 * 2 ** 18, -1)
+    ts(R("LMF", 7, 8), R("CO", 40, 41), -1.0, A.mult)
+    for i in COST["sf"]:
+        ms(R("CO", 36 + 2 * i, 38 + 2 * i), 0.0)
     lanes(C(3), 1024, 1)
     lanes(C(4), 64, 1)
     iota(C(5), [[0, 16]], 0, 16)
@@ -424,11 +451,10 @@ def rank_program(g, core, T, topo):
     iota(R("CIW", 0, 64), [[16, 64]], 0, 0)
     tc(R("SM", 6, 7), R("SJ", 96, 97))
     ts(R("CIW", 0, 64), R("CIW", 0, 64), R("SM", 6, 7), A.add)
-    ts(R("CIW", 64, 128), R("CIW", 0, 64), 1024.0, A.add)
+    ts(R("CIW", 64, 128), R("CIW", 0, 64), -1.0, A.mult, 1023.0, A.add)
     ms(R("WQ"), 1.0)
     aff(R("WQ"), R("WQ"), [[1, 16], [0, 8], [-1, 16]], A.is_equal, 0.0, 0, 0)
     bounded(R("WQ"), [[0, 16], [-16, 8], [0, 16]], 0, 1, 16)
-    ms(R("TB", 0, NE), 128.0)
     for b, s in (("RW1", 128), ("RW2", 256)):
         ms(R(b), 1.0)
         ms(R(b, 0, 512, s), 0.0)
@@ -483,13 +509,15 @@ def rank_program(g, core, T, topo):
         ts(R("NVB"), R("GS0"), S(E1, 1), A.mult)
         tt(u, R("CIW", 0, 64), u, A.subtract)
         tt(u, u, R("B7", 128, 192), A.add)
-        tt(y, R("CIW", 64, 128), R("OCB"), A.mult)
+        tt(y, R("CIW", 64, 128), u, A.add)
+        tt(y, y, R("OCB"), A.mult)
         tt(u, u, y, A.max)
         tc(R("LST", 64, 128), u)
         for h in range(2):
             mm(R("B7", 192 + 8 * h, 200 + 8 * h), R("ONEB"), R("NVB"), True, True)
-        tc(S(NV), R("B7", 192, 208))
-        tc(I("TB", 0, NE, "LST", 64, 128), R("TB", NE, NE + 1024))
+        cp(S(NV), R("B7", 192, 208))
+        for j in range(2):
+            put(I("TB", 0, NE, "LST", 64 + 32 * j, 96 + 32 * j), R("TB", NE + 512 * j, NE + 512 * j + 512))
 
     def squares(w, bank, kk):
         for j in range(2):
@@ -640,6 +668,10 @@ def rank_program(g, core, T, topo):
                 c = 256 + 256 * (gg % 2) + 128 * h
                 mm(R(b, wd * j, wd * j + wd), R("CF", c, c + 128, 1, p0, p0 + 32), R("CF", 0, wd, 1, p0, p0 + 32), True, True,
                    j > 0 and p0 != 32 * (gs[j - 1] // 2))
+            if i in COST["sf"]:
+                for j, gg in enumerate(gs):
+                    over(R("SM", 16 * FM + 8 * h + gg, 16 * FM + 8 * h + gg + 1), R(b, wd * j, wd * j + wd), R("LMF", 7, 8), R("FS", wd * j, wd * j + wd))
+                continue
             scan(R("FS"), R(rw), R(b), A.mult, A.max)
             tc(R("SM", 16 * FM + 8 * h + gs[0], 16 * FM + 8 * h + gs[0] + len(gs)), R("FS", wd - 1, 512, wd))
         for h in range(2):

@@ -17,18 +17,18 @@ def _sb(spec):
 
 
 SCRATCH = _sb({
-    "bfloat16": "X:4368 TX:4096 XE:4096 SQ:4096 XSE:4096 XA:4096 OWG:4096 RM:2048 QM:768 BM:512 ROW:1152 WQ:2048 WT:2048 "
-                "WE:2048 RW1:512 RW2:512 IND:1024 CF:768 MM:512 TH2:512 KC:512 ALT:1024 VS:336 XVE:1024 XVS:1024 VD:1024 RET:64",
-    "float32": "OW:8576 TB:2304 ML:1280 VAL:4096 KD:512 EMW:1280 SM:1024 W:512 MVA:528 MVB:272 W0:768 W1:768 W2:768",
-    "int32": "AC:4368 MI:1024 LMI:2 WTI:1 SJ:128 SK:2x16 SL:2x16",
+    "bfloat16": "X:4368 TX:4096 XE:4096 SQ:4096 XSE:4096 XA:4096 OWG:4096 RM:2048 QM:256 BM:512 ROW:1152 WQ:2048 WT:2048 "
+                "WE:2048 RW1:512 WP:768 IND:1024 CF:768 MM:512 TH2:512 ALT:1280 CT:1040 VS:336 XVE:1024 XVS:1024 VD:1024 RET:64",
+    "float32": "OW:8576 TB:2304 ML:1280 VAL:4096 KD:512 EMW:768 SM:1024 W:32x16 SH:512 MVA:528 W0:768 W1:768 W2:768",
+    "int32": "AC:4368 MI:1024 MK:1024 LMI:2 WTI:1 SJ:128 SK:2x16 SL:2x16",
     "uint16": "OFO:256 ACO:256 OFD:256 MVO:256 MV2:256 LST:256 HL:64 SOF:80 SRP:4"})
 WIDTH = {k: v[1][1] * (v[1][2] if len(v[1]) > 2 else 1) for k, v in SCRATCH.items()}
 PLACE = {k: (k, 0) for k in SCRATCH}
 for _pool, _dt, _names in (
         ("PB", "bfloat16", "ONEB:128 IDB:128 NID:128 IDV:128 BO:128 G16:8 G512:16 G64:8 GS0:8 GC:64 WB:128 TRI:128 TSB:128 XS0:256 XS1:256 "
-                           "SB:64 OCB:64 NVB:8 CN:256 XB:256 UC:256 VM:256 TG:256 INDD:256 FIT:256 NX1:256 OVG:64 AVG:64 EQV:64"),
-        ("PF", "float32", "QF:16 ONE:128 IDF:128 IDK:128 IXS:128 RB:8 DUM:256 CO:128 BAS:256 CIW:128 LMF:8 LIM:64 K1:256 KM:256 KBC:256 KV:128 "
-                          "EMA:256 EMB:256 EMV:128 EX:256 EQ:256 EQ2:256 MD:256 WM:256 ENX:256 HL1:64 HL2:64 VF:64")):
+                           "LMB:8 SB:64 OCB:64 NVB:8 CN:256 XB:256 UC:256 VM:256 INDD:256 NX1:256 OVG:64 AVG:64 EQV:64"),
+        ("PF", "float32", "QF:16 ONE:128 IDF:128 IDK:128 IXS:128 RB:8 DUM:256 CO:128 BAS:32 CIW:128 LMF:8 LIM:64 K1:256 KM:256 KBC:256 KV:128 "
+                          "EMA:256 EMB:256 EMV:128 EQ2:256 MD:256 MA:256 MW:256 GW:16 HL1:64 HL2:64 VF:64")):
     _at = 0
     for _x in _names.split():
         _k, _w = _x.split(":")
@@ -42,19 +42,20 @@ for _t in range(4):
 for _b in range(8):
     SCRATCH["B%d" % _b] = ("psum", [128, 512], "float32")
     PLACE["B%d" % _b], WIDTH["B%d" % _b] = ("B%d" % _b, 0), 512
-for _k, _v, _at, _w in (("US", "OWG", 0, 4096), ("UD", "OWG", 0, 4096), ("TD", "XA", 0, 4096), ("XE2", "XE", 0, 4096), ("QI", "AC", 16, 768),
+for _k, _v, _at, _w in (("US", "OWG", 0, 4096), ("UD", "OWG", 0, 4096), ("TD", "XA", 0, 4096), ("XE2", "XE", 0, 4096),
                         ("YM", "VAL", 0, 1024), ("FS", "KD", 0, 512), ("SQV", "XVE", 0, 1024), ("KA", "K1", 0, 256), ("MSD", "KM", 0, 256),
                         ("KB", "KM", 0, 256), ("L2", "MD", 0, 256), ("ZI", "MI", 0, 512), ("ZC", "MI", 512, 256), ("SI", "MI", 768, 256),
-                        ("ZA", "AC", 1024, 320)):
+                        ("TG", "WP", 256, 256)):
     PLACE[_k], WIDTH[_k] = (PLACE[_v][0], PLACE[_v][1] + _at), _w
-SEMAPHORES = ["v", "s", "p", "gg", "dx", "da", "dm", "dl", "dw", "oy", "ox"] + ["%s%d" % (a, b) for a in ("va", "vl", "ra", "rl") for b in range(4)]
+SEMAPHORES = ["v", "s", "p", "gg", "dx", "da", "dm", "dl", "dw", "oy", "ox"] + ["dp%d" % j for j in range(6)] + ["%s%d" % (a, b) for a in ("va", "vl", "ra", "rl") for b in range(4)]
 PSUM = ["B%d" % b for b in range(8)]
 SIZE = {"float32": 4, "int32": 4, "bfloat16": 2, "uint16": 2}
-COST = {"cy": 0.9, "gat": 1.5, "sca": 3.0, "pe": 0.65, "wake": 80.0, "far": 3000.0, "dma": 3000.0, "look": 200.0, "cut": 8, "sf": (2, 3, 4, 5), "turns": 4, "short": 256, "b": 0.6}
+COST = {"cy": 0.9, "gat": 1.5, "sca": 3.0, "pe": 0.65, "wake": 150.0, "far": 3000.0, "dma": 3000.0, "look": 200.0, "sf": (2, 3, 4, 5), "turns": 6, "short": 256,
+        "lean": (0.2, 0.3, 0.4, 0.5, 0.6)}
 PLAN = {}
 
 
-def issue(ns, after, rank):
+def issue(ns, after, rank, lean):
     n = len(ns)
     left = [0] * n
     for a in after:
@@ -75,7 +76,7 @@ def issue(ns, after, rank):
         now, q = min((max(free[q], min(ready[i] for i in pool[q])), q) for q in free if pool[q])
         near = [i for i in pool[q] if ready[i] <= now + COST["look"]]
         if q == "v":
-            near = [i for i in near if len(ns[i]) == 1 or free["s"] > max(now, ready[i]) + COST["b"] * ns[i]["v"]]
+            near = [i for i in near if len(ns[i]) == 1 or free["s"] > max(now, ready[i]) + lean * ns[i]["v"]]
             if not near:
                 free[q] = now + 100.0
                 continue
@@ -107,12 +108,13 @@ def plan(calls):
     rank = [0.0] * len(calls)
     for i in range(len(calls) - 1, -1, -1):
         rank[i] = min(ns[i].values()) + max([rank[j] + gap for j, gap in after[i]] + [calls[i]["lat"]])
-    best = issue(ns, after, rank)
-    now = best
-    for _ in range(COST["turns"]):
-        now = issue(ns, after, issue(ns, before, now[1])[1])
-        if max(now[1]) < max(best[1]):
-            best = now
+    best = None
+    for lean in COST["lean"]:
+        now = issue(ns, after, rank, lean)
+        for _ in range(COST["turns"]):
+            now = issue(ns, after, issue(ns, before, now[1], lean)[1], lean)
+            if best is None or max(now[1]) < max(best[1]):
+                best = now
     return best[0]
 
 
@@ -234,8 +236,12 @@ def rank_program(g, core, T, topo):
     def lin(o, a, mul, add):
         ts(o, a, mul, A.mult, add, A.add, lambda: g.scalar.activation(o[0], a[0], F.Identity, bias=add, scale=mul))
 
-    def relu(o, a, add):
-        ts(o, a, add, A.add, 0.0, A.max, lambda: g.scalar.activation(o[0], a[0], F.Relu, bias=add))
+    def relu(o, a, add, mul=1.0):
+        f = lambda: g.scalar.activation(o[0], a[0], F.Relu, bias=add, scale=mul)
+        if mul == 1.0:
+            ts(o, a, add, A.add, 0.0, A.max, f)
+        else:
+            call({"s": (f, ns("s", o, [a]))}, a[1], o[1])
 
     def sign(o, a):
         ts(o, a, 0.0, A.is_gt, other=lambda: g.scalar.activation(o[0], a[0], F.Sign))
@@ -286,6 +292,15 @@ def rank_program(g, core, T, topo):
         me = call({"gg": (lambda: g.remote_dma(T[ob][:, 0:64], i[0], T.sem[rs], T.sem[ls], pid, rid, mask), 100.0)}, i[1], [], ls, -len(eng), COST["far"])
         call({"x": (None, 0.0)}, [], R(ob, 0, 64)[1], rs, -len(eng), 0.0, True, more=[me])
 
+    def fill(o, c):
+        iota(o, [[0, o[2]]], c, 0)
+
+    def diag(o, zero, c):
+        aff(o, zero, [[-1, 128]], A.not_equal, c, 0, 1)
+
+    def mark(o, k, c):
+        aff(o, o, [[-16, 8]], A.not_equal, c, -k, 1)
+
     def bounded(o, pat, base, cm, width):
         aff(o, o, pat, A.is_ge, 0.0, base, cm)
         aff(o, o, [[-s, k] for s, k in pat], A.is_ge, 0.0, width - 1 - base, -cm)
@@ -308,32 +323,48 @@ def rank_program(g, core, T, topo):
             mm(R(bank, lo + 8 * h, lo + 8 * h + 8), R(em, eo + 128 * h, eo + 128 * h + 128), R("RB"), True, True)
         return R(bank, lo, lo + cols)
 
-    def moved(o, ids, e, x):
+    def moved(o, ids, e):
         none(e, ids)
-        tt(x, e, R("DUM"), A.mult)
-        tt(o, x, ids, A.add)
+        tt(e, R("DUM"), e, A.mult)
+        tt(o, ids, e, A.add)
 
-    def settle(mv):
+    def spread():
         for j in range(4):
             scan(R("VAL", 1024 * j, 1024 * j + 1024), R("RM", 0, 1024), R("XE2", 1024 * j, 1024 * j + 1024), A.mult, A.add)
-        w = 4096 // COST["cut"]
-        for j in range(0, 4096, w):
-            put(I("OW", 0, NO, mv, j // 16, (j + w) // 16), R("VAL", j, j + w))
+
+    def settle(mv, how):
+        for j in range(0, 4096, 512):
+            how(I("OW", 0, NO, mv, j // 16, j // 16 + 32), R("VAL", j, j + 512))
 
     def owners(u):
         mv = ("MVO", "MV2")[u % 2]
-        moved(R("EQ2"), R("ML", u, 1024, 4), R("B3", 0, 256), R("EQ2"))
+        moved(R("EQ2"), R("ML", u, 1024, 4), R("B3", 0, 256))
         tc(R(mv), R("EQ2"))
-        tc(R("XE2", 0, 4096, 16), R("TB", NE + u, NE + 1024, 4))
-        settle(mv)
+        if u == 1:
+            tc(R("EMA"), R("TB", NE + u, NE + 1024, 4))
+            for j in range(4):
+                cp(R("VAL", 1024 * j, 1024 * j + 1024), wide("EMA", 64 * j, 64))
+        else:
+            was = (u - 1) % 4
+            for h in range(2):
+                plane = lambda k: T.VAL[k:128:16, 2048 * h:2048 * h + 2048]
+                dma("dp%d" % (2 * was - 2 + h), [(plane(2 + u), plane(6)), (plane(2 + was), plane(2 + (u + 1) % 4))], half("VAL", h)[1], half("VAL", h)[1])
+        settle(mv, put)
 
-    def shifts(w, width, mv, bank, sg):
-        p = R(bank, 0, width)
-        for th, s in ((4096.0, 1), (512.0, 2), (64.0, 4), (8.0, 8)):
+    def shifts(b, mv, bank):
+        width = WIDTH[b]
+        w, p = R3(b, 0, width // 16, 0, 16), R(bank, 0, width)
+        for th, s in ((4096.0, 1), (512.0, 2), (64.0, 4)):
             lin(p, w, -th, th * th)
             relu(R(mv, 8, 8 + width), w, -th)
             tt(p, w, p, A.min)
-            tt(w, R(mv, 8 + sg * s, 8 + sg * s + width), p, A.max)
+            tt(w, R(mv, 8 + s, 8 + s + width), p, A.max)
+        fro, to = [R3(b, 0, width // 16, a, a + 8) for a in (8, 0)]
+        p0, p1 = R(bank, 0, width // 2), R(bank, width // 2, width)
+        ts(p0, fro, 8.0, A.is_lt)
+        ts(p1, fro, -8.0, A.add, 0.0, A.max)
+        tt(fro, fro, p0, A.mult)
+        tt(to, to, p1, A.max)
 
     def numbers(bank, lo, src, cols, wq="WQ"):
         for q in range(16):
@@ -346,8 +377,10 @@ def rank_program(g, core, T, topo):
     ts(qi, qi, 15, A.bitwise_and)
     ts(R("QF"), qi, 0, A.is_equal)
     ts(R("QM", 0, 16), qi, 0, A.is_equal)
-    for w in (16, 32, 64, 128, 256, 512):
-        tc(R("QM", w, 2 * w), R("QM", 0, min(w, 768 - w)))
+    for w in (16, 32, 64, 128):
+        tc(R("QM", w, 2 * w), R("QM", 0, w))
+    iota(R("SJ", 0, 80), [[1, 80]], 0, 0)
+    tc(R("SOF"), R("SJ", 0, 80))
     dma("dm", [(T.MI[:, :], T.ml[:, :])], [], mi[1])
     ms(R("X", 0, 16), -16.0)
     ms(R("X", 4096, NX), 0.0)
@@ -358,8 +391,9 @@ def rank_program(g, core, T, topo):
     dma("dl", [(T.LMI[:], T.lims[:, :])], [], R("LMI")[1])
     dma("dw", [(T.WTI[:], T.wt[:, :])], [], R("WTI")[1])
     iota(R("DUM"), [[16, 256]], D0, 1)
-    iota(R("OW", 0, 4112), [[0, 4112]], 128, 0)
-    ms(R("XE"), 0.0)
+    fill(R("OW", 2304, 4112), 128)
+    ms(R("OW", 0, 2304), 128.0)
+    fill(R("XE"), 0)
     ms(R("RM"), 1.0)
     ms(R("RM", 0, 2048, 16), 0.0)
     ms(one, 1.0)
@@ -373,36 +407,38 @@ def rank_program(g, core, T, topo):
     tt(R("SM", 5, 6), q_(4), q_(5), A.add)
     tt(R("SM", 4, 5), R("SM", 4, 5), R("SM", 5, 6), A.add)
     for u in range(4):
-        tt(R("SM", 8 + u, 9 + u), q_(2 + u), R("SM", 4, 5), A.subtract)
-        ts(R("SM", 8 + u, 9 + u), R("SM", 8 + u, 9 + u), 128.0, A.mult)
+        ts(R("SM", 8 + u, 9 + u), q_(2 + u), R("SM", 4, 5), A.subtract, 128.0, A.mult)
         ts(R("TB", NE + u, NE + 1280, 4), pl, R("SM", 8 + u, 9 + u), A.add)
     ml = R("ML", 0, 1024)
-    ts(ml, mi, 4096, A.is_equal, -4097, A.mult)
-    tt(ml, ml, mi, A.add)
-    ts(ml, ml, 1, A.add)
-    ms(R("ML", 1024, 1280), 0.0)
+    for h in range(2):
+        a, b = R("MI", 512 * h, 512 * h + 512), R("B%d" % h)
+        ts(b, a, 4096, A.is_equal, -4097, A.mult)
+        tt(b, a, b, A.add)
+        lin(R("ML", 512 * h, 512 * h + 512), b, 1.0, 1.0)
+    fill(R("ML", 1024, 1280), 0)
     sign(R("IND"), ml)
     for u in range(1, 4):
         owners(u)
-    aff(R("IDF"), one, [[-1, 128]], A.is_equal, 0.0, 0, 1)
-    ms(R("KD"), 1.0)
-    for o, w, p in ((0, 128, ([[-16, 8], [0, 16]], 0, 1, 16)), (128, 8, ([[-16, 8]], 0, 1, 16)), (256, 128, ([[1, 128]], -1, -1, 200))):
-        bounded(R("KD", o, o + w), *p)
-    tc(R("BO"), R("KD", 0, 128))
-    tc(R("RB"), R("KD", 128, 136))
-    tc(R("TRI"), R("KD", 256, 384))
-    ts(R("KD", 384, 512), R("KD", 256, 384), -1.0, A.add)
-    tt(R("TSB"), R("KD", 384, 512), R("KD", 0, 128), A.mult)
-    ts(R("TSB"), R("TSB"), -1.0, A.mult)
-    tc(R("ONEB"), one)
-    tc(R("IDB"), R("IDF"))
-    ts(R("NID"), R("IDF"), -1.0, A.mult)
-    ts(R("IDK"), R("IDF"), 1024.0, A.mult)
-    ts(R("IXS"), R("IDF"), 2.0 ** -10, A.mult)
-    ts(R("IDV"), R("IDF"), float(2 ** 18), A.mult)
+    for b in ("VS", "XVS", "MVA"):
+        fill(R(b), 0)
+    for b, c in (("IDF", 1.0), ("IDK", 1024.0), ("IXS", 2.0 ** -10)):
+        diag(R(b), R("MVA", 0, 128), c)
+    for b, c in (("IDB", 1.0), ("NID", -1.0), ("IDV", float(2 ** 18))):
+        diag(R(b), R("VS", 0, 128), c)
+    for b in ("ONEB", "BO", "RB"):
+        fill(R(b), 1)
+    bounded(R("BO"), [[-16, 8], [0, 16]], 0, 1, 16)
+    bounded(R("RB"), [[-16, 8]], 0, 1, 16)
+    aff(R("TRI"), R("ONEB"), [[1, 128]], A.is_gt, 0.0, 0, -1)
+    aff(R("TSB"), R("BO"), [[-1, 128]], A.is_ge, 0.0, 0, 1)
     for b, c in ((R("G16"), 16.0), (R("G64"), 65536.0), (R("G512", 0, 8), 512.0), (R("G512", 8, 16), 512.0)):
         ts(b, g8, c, A.mult)
-    ts(R("GS0"), g8, q_(0), A.mult)
+    for j in range(4):
+        aff(hv("SH", j), R("MVA", 0, 128), [[1, 128]], A.not_equal, 1.0, -2 ** j, -1)
+        bounded(hv("SH", j), [[-16, 8], [0, 16]], 0, 1, 16)
+        diag(hv("SH", j), hv("SH", j), -1.0)
+    fill(R("GS0"), 0)
+    mark(R("GS0"), 0, 1.0)
     for o, pat, base in ((0, [[0, 8], [4096, 16]], 0), (128, [[0, 8], [1, 16]], 0), (256, [[0, 16], [-1, 16]], 15), (512, [[0, 128]], -1),
                          (640, [[0, 2], [-384, 2], [0, 8]], 0)):
         w = 1
@@ -411,32 +447,25 @@ def rank_program(g, core, T, topo):
         iota(R("W1", o, o + w), pat, base, 0)
     tc(R("ROW", 0, 640), R("W1", 0, 640))
     iota(R("KD"), [[0, 32], [32, 16]], -128, 0)
-    iota(R("KC"), [[1, 2], [0, 16], [1, 16]], 0, 0)
-    iota(R("SJ", 0, 80), [[1, 80]], 0, 0)
-    tc(R("SOF"), R("SJ", 0, 80))
     iota(R("SJ", 96, 100), [[0, 4]], 0, 1)
     ts(R("SJ", 96, 100), R("SJ", 96, 100), 15, A.bitwise_and)
     tc(R("SRP"), R("SJ", 96, 100))
     tt(R("ROW", 640, 1152), wide("W1", 640, 32), R("KD"), A.add)
-    ms(R("BM"), 0.0)
+    fill(R("BM"), 0)
     ms(R("BM", 0, 512, 16), float(2 ** 25))
-    wc, wl = R("SM", 0, 1), R("SM", 1, 2)
-    ts(wl, q_(1), 4.0, A.mult)
-    for u in range(1, 4):
-        ts(R("SM", 2, 3), q_(2 + u), u / 128, A.mult)
-        tt(wl, wl, R("SM", 2, 3), A.add)
-    ts(wc, q_(0), 32.0, A.mult)
-    tt(wc, wc, wl, A.add)
-    ts(R("SM", 2, 3), q_(6), -36.0, A.mult)
-    tt(wc, wc, R("SM", 2, 3), A.add)
+    wc = R("SM", 0, 1)
+    low = [(1, 4.0)] + [(2 + u, u / 128) for u in range(1, 4)]
+    fill(R("GW"), 0)
+    fill(R("GC"), 0)
+    for k, c in low + [(0, 32.0), (6, -36.0)]:
+        mark(R("GW", 0, 8), k, c)
+    addup(wc, R("GW", 0, 8))
     for u in range(4):
-        ts(R("SM", 2, 3), q_(2 + u), float(2 ** 15), A.mult)
-        tt(R("SM", 3, 4), R("SM", 2, 3), q_(0), A.add)
-        tt(R("SM", 2, 3), R("SM", 2, 3), wl, A.max)
-        ts(R("GC", 16 * u, 16 * u + 8), g8, R("SM", 3, 4), A.mult)
-        ts(R("GC", 16 * u + 8, 16 * u + 16), g8, R("SM", 2, 3), A.mult)
+        for j, ws in enumerate(([(0, 1.0)], low)):
+            for k, c in [x for x in ws if x[0] != 2 + u] + [(2 + u, float(2 ** 15))]:
+                mark(R("GC", 16 * u + 8 * j, 16 * u + 8 * j + 8), k, c)
     lanes = lambda o, base, s: iota(o, [[128 * s, 2], [0, 8]], base, s)
-    lanes(C(0), 4097, 1)
+    lanes(C(0), 4096, 1)
     lanes(C(1), 15, 16)
     lanes(C(2), 11 * 2 ** 18, -1)
     ts(R("LMF", 7, 8), R("CO", 40, 41), -1.0, A.mult)
@@ -445,34 +474,32 @@ def rank_program(g, core, T, topo):
     lanes(C(3), 1024, 1)
     lanes(C(4), 64, 1)
     iota(C(5), [[0, 16]], 0, 16)
-    for t in range(4):
-        for j, (base, s) in enumerate(((512, 1), (t, 4), (NE + t, 4), (NE + 1024, 1))):
-            lanes(R("BAS", 64 * t + 16 * j, 64 * t + 16 * j + 16), base, s)
+    for j, base in enumerate((512, NE + 1024)):
+        lanes(R("BAS", 16 * j, 16 * j + 16), base, 1)
     iota(R("CIW", 0, 64), [[16, 64]], 0, 0)
     tc(R("SM", 6, 7), R("SJ", 96, 97))
     ts(R("CIW", 0, 64), R("CIW", 0, 64), R("SM", 6, 7), A.add)
     ts(R("CIW", 64, 128), R("CIW", 0, 64), -1.0, A.mult, 1023.0, A.add)
-    ms(R("WQ"), 1.0)
+    fill(R("WQ"), 1)
     aff(R("WQ"), R("WQ"), [[1, 16], [0, 8], [-1, 16]], A.is_equal, 0.0, 0, 0)
     bounded(R("WQ"), [[0, 16], [-16, 8], [0, 16]], 0, 1, 16)
-    for b, s in (("RW1", 128), ("RW2", 256)):
-        ms(R(b), 1.0)
-        ms(R(b, 0, 512, s), 0.0)
+    fill(R("RW1"), 1)
+    aff(R("RW1"), R("RW1"), [[0, 4], [1, 128]], A.is_gt, 0.0, 0, 0)
     for k in range(11):
-        ms(R("SM", 16 + k, 17 + k), float(2 ** (10 - k)))
-    ms(R("SM", 27, 32), 0.0)
-    tt(R("SM", 16, 32), R("SM", 16, 32), R("QM", 0, 16), A.mult)
-    addup(R("LMF", 0, 1), R("SM", 16, 32))
-    iota(R("SI", 0, 1), [[0, 1]], 0, 1)
-    ts(R("SI", 0, 1), R("SI", 0, 1), 16, A.bitwise_and)
-    ts(R("LMF", 1, 2), R("SI", 0, 1), 16.0, A.is_equal)
-    ts(R("LMF", 2, 3), R("LMF", 1, 2), -1.0, A.mult, 1.0, A.add)
+        mark(R("GW", 8, 16), k, float(2 ** (10 - k)))
+    addup(R("LMF", 0, 1), R("GW", 8, 16))
     ts(R("LMF", 5, 6), R("LMF", 0, 1), 0.0, A.is_gt, -512.0, A.mult)
-    tt(R("LMF", 6, 7), R("LMF", 5, 6), q_(15), A.add)
+    iota(mi, [[1, 1024]], 1, 0)
+    ts(mi, mi, R("LMF", 0, 1), A.mult)
+    ts(mi, mi, 1024, A.bitwise_and)
+    ts(R("CT", 1, 1025), mi, R("LMF", 5, 6), A.add)
+    tc(R("CT", 0, 1), R("LMF", 5, 6))
     for a in (0, 1):
-        tt(R("LMF", 3 + a, 4 + a), R("LMF", 1 + a, 2 + a), R("LMF", 6, 7), A.mult)
+        addup(R("LMF", 1 + a, 2 + a), R("RB", a, 8, 2))
+        tt(R("LMB", 4 + a, 5 + a), R("LMF", 1 + a, 2 + a), q_(15), A.mult)
+        tt(R("LMB", 2 + a, 3 + a), R("LMF", 1 + a, 2 + a), R("LMB", 4 + a, 5 + a), A.subtract)
     iota(R("K1"), [[-1, 256]], 0, 0)
-    ts(R("CN"), R("K1"), q_(15), A.mult, R("LMF", 5, 6), A.add)
+    ts(R("CN"), R("K1"), q_(15), A.mult)
     tc(R("SM", 12, 14), R("LMI"))
     for j in range(2):
         ts(R("VM", 128 * j, 128 * j + 128), one, R("SM", 12 + j, 13 + j), A.mult)
@@ -480,24 +507,23 @@ def rank_program(g, core, T, topo):
             mm(R("B2", 16 * j + 8 * h, 16 * j + 8 * h + 8), R("VM", 128 * j, 128 * j + 128), R("GS0"), True, True)
     tc(R("LIM", 0, 32), R("B2", 0, 32))
     tc(R("LIM", 32, 48), R("LIM", 0, 16))
-    for b in ("VS", "XVS", "MVA", "MVB", "W1"):
-        ms(R(b), 0.0)
+    fill(R("W1"), 0)
     for u in range(4):
-        ms(R("ME%d" % u, 64, 336), 0.0)
+        fill(R("ME%d" % u, 64, 336), 0)
     cp(R("W2", 512, 768), R("DUM"))
-    cp(R("ALT"), R("TB", NE, NE + 1024))
-    tc(R("SM", 14, 15), R("WTI"))
-    ts(R("WT"), R("WQ"), R("SM", 14, 15), A.mult)
-    ts(R("WB"), R("BO"), R("SM", 14, 15), A.mult)
-    ts(R("WE"), R("WQ"), q_(0), A.mult)
-    ts(R("WQ"), R("WQ"), wc, A.mult)
+    fill(R("ALT"), 128)
+    fill(R("WP", 512, 768), 128)
+    tc(R("LMB", 0, 1), R("WTI"))
+    tc(R("LMB", 1, 2), wc)
+    ts(R("WT"), R("WQ"), R("LMB", 0, 1), A.mult)
+    ts(R("WB"), R("BO"), R("LMB", 0, 1), A.mult)
+    ts(R("WE"), R("WQ"), R("QM", 0, 1), A.mult)
+    ts(R("WQ"), R("WQ"), R("LMB", 1, 2), A.mult)
     (NN, LIVE, LS, LB, SUU, GRL, N16, HAS, FM, DD, T1, T2, T3, OK, SPL, RK, NV, MN, RK2, IDL, VIS, T4, LV, E1, E2, E3) = range(2, 28)
     AV, BV, TA, TB2, LL = 32, 36, 40, 44, 48
     EU = 56
-    ms(R("SM", 16 * LV, 16 * LV + 16), 0.0)
-    ms(S(AV, 128), 0.0)
-    ms(S(AV), -512.0)
-    ms(S(BV), -256.0)
+    for a, c in ((LV, 0), (AV, -512), (BV, -256)):
+        fill(S(a), c)
 
     def empties():
         tc(R("OCB"), numbers("B7", 0, "IND", 64, "WE"))
@@ -547,11 +573,10 @@ def rank_program(g, core, T, topo):
         scan(R("KM"), R("BM", 0, 256), R("K1"), A.max, A.min)
         tc(R("SI", 0, 16), R("KM", 15, 256, 16))
         ts(R("SI", 16, 32), R("SI", 0, 16), 4095, A.bitwise_and)
-        ts(S(LS), R("SI", 16, 32), 1.0, A.add)
-        tt(S(LS), S(LS), C(0), A.subtract)
-        tt(S(LS), S(LS), S(LIVE), A.mult)
-        tt(S(LS), S(LS), C(0), A.add)
-        tc(R("LST", ls, ls + 16), wrap(LS, 16, "EMA", 0, "B0", 256))
+        tt(S(SUU), S(LIVE), C(0), A.mult)
+        tt(S(SUU), C(0), S(SUU), A.subtract)
+        tt(S(LS), R("SI", 16, 32), S(SUU), A.max)
+        ts(R("LST", ls, ls + 16), wrap(LS, 16, "EMA", 0, "B0", 256), 1.0, A.add)
         tc(xs, I("X", 0, NX, "LST", ls, ls + 16))
         ts(R("ACO"), I("AC", 0, NX, "LST", ls, ls + 16), 1, A.add)
         tc(R("XE", 0, 4096, 16), xs)
@@ -566,6 +591,10 @@ def rank_program(g, core, T, topo):
         tt(S(GRL), R("B2", 16, 32), R("SI", 32, 48), A.subtract)
         tt(S(GRL), S(GRL), R("LIM", 16, 32), A.is_gt)
         tt(S(GRL), S(GRL), S(LIVE), A.mult)
+        mm(R("B3", 0, 256), R("BO"), R("IND", t, 1024, 4), True, True)
+        tc(R("ZC"), R("B3", 0, 256))
+        for j in range(4):
+            ts(R("MK", 256 * j, 256 * j + 256), R("ZC"), j, A.logical_shift_right, 1, A.bitwise_and)
         for kk in range(8):
             squares(xs, ("B4", "B5")[kk % 2], kk)
         for h in range(2):
@@ -592,33 +621,28 @@ def rank_program(g, core, T, topo):
         tt(R("MM", 256, 512), R("KBC"), R("B6", 0, 256), A.is_gt)
         tt(R("MM", 0, 256), R("KBC"), R("B6", 0, 256), A.is_le)
         scan(R("TH2", 0, 256), R("RM", 0, 256), R("MM", 256, 512), A.mult, A.add)
-        tt(R("TH2", 256, 512), R("KC", 256, 512), R("TH2", 0, 256), A.subtract)
+        scan(R("TH2", 256, 512), R("RM", 0, 256), R("MM", 0, 256), A.mult, A.add)
         ts(R("ZI"), R("TH2"), 4369.0, A.mult)
         ts(R("ZI"), R("ZI"), 4680, A.bitwise_and)
         for f in range(2):
             tt(R("B4", 256 * f, 256 * f + 256), R("ZI", 256 * f, 256 * f + 256), R("B6", 256, 512), A.add)
-        tt(R("W"), R("MM"), R("B4"), A.mult)
-        shifts(R("W"), 512, "MVA", "B5", 1)
+        tt(R3("W", 0, 32, 0, 16), R("MM"), R("B4"), A.mult)
+        shifts("W", "MVA", "B5")
         for j in range(4):
-            mm(hv("B6", j), hv("W", j), R("IDK"), True, True)
+            mm(hv("B6", j), R3("W", 8 * j, 8 * j + 8, 0, 16), R("IDK"), True, True)
         cp(R("W0", 256, 512), R("B6", 0, 256))
         cp(R("W1", 256, 512), R("B6", 256, 512))
         if t < 3:
-            moved(R("W2", 256, 512), R("W1", 256, 512), R("B4", 0, 256), R("EQ"))
+            moved(R("W2", 256, 512), R("W1", 256, 512), R("B4", 0, 256))
         cp(R("W0", 512, 768), R("ML", t, 1024, 4))
-        ts(R("SI", 64, 80), S(NN), 4369.0, A.mult)
-        ts(R("SI", 64, 80), R("SI", 64, 80), 4680, A.bitwise_and)
-        tc(R("ENX"), wide("SI", 64, 16))
-        ts(S(N16), S(NN), -1.0, A.mult, 16.0, A.add)
-        tt(R("FIT"), wide("SM", 16 * N16, 16), R("KC", 0, 256), A.is_gt)
+        cp(R("WP", 0, 256), R("TB", NE + t, NE + 1024, 4))
 
-    members(0)
     empties()
+    members(0)
     for t in range(4):
         own = lambda h, b="ML": R(b, t + 512 * h, t + 512 * h + 512, 4)
         xs, ls = R("XS%d" % (t % 2)), 16 * (t % 2)
         la = 128 + 16 * (t % 2)
-        bas = lambda j, w=16: R("BAS", 64 * t + 16 * j, 64 * t + 16 * j + w)
         for j in range(4):
             cp(R("OWG", 1024 * j, 1024 * j + 1024), I("OW", 0, NO, "ACO", 64 * j, 64 * j + 64))
         for j in range(4):
@@ -647,22 +671,16 @@ def rank_program(g, core, T, topo):
             cp(R("TD", 1024 * j, 1024 * j + 1024), I("X", 0, NX, "OFD", 64 * j, 64 * j + 64))
         sign(R("INDD"), R("MD"))
         ts(S(HAS), S(DD), 1024.0, A.is_lt)
-        tt(S(AV + 1), S(DD), bas(1), A.subtract)
-        tt(S(AV + 3), S(DD), C(3), A.subtract)
-        cp(R("EX"), wide("SM", 16 * DD, 16))
-        for h in range(2):
-            mm(hv("B0", h), hv("EX", h), R("IDF"), True, True)
-        ts(R("ZC"), R("B0", 0, 256), R("LMF", 0, 1), A.mult)
-        ts(R("ZC"), R("ZC"), 1024, A.bitwise_and)
-        tt(R("CF", 0, 256), R("ZC"), R("CN"), A.add)
-        ts(R("CF", 256, 512), R("ZC"), R("LMF", 2, 3), A.mult, R("LMF", 4, 5), A.add)
-        ts(R("CF", 512, 768), R("ZC"), R("LMF", 1, 2), A.mult, R("LMF", 3, 4), A.add)
+        tt(S(AV + 1), S(DD), C(3), A.subtract)
+        tt(R("CF", 0, 256), I("CT", 0, 1040, "LST", 48, 64), R("CN"), A.add)
+        for a in (0, 1):
+            ts(R("CF", 256 + 256 * a, 512 + 256 * a), R("CF", 0, 256), R("LMB", 2 + a, 3 + a), A.mult, R("LMB", 4 + a, 5 + a), A.add)
         for i in range(6):
             b = ("B3", "B7")[i % 2]
             if i < 2:
                 h, gs, wd, rw = 0, range(4 * i, 4 * i + 4), 128, "RW1"
             else:
-                h, gs, wd, rw = 1, range(2 * (i - 2), 2 * (i - 2) + 2), 256, "RW2"
+                h, gs, wd, rw = 1, range(2 * (i - 2), 2 * (i - 2) + 2), 256, None
             for j, gg in enumerate(gs):
                 p0 = 32 * (gg // 2)
                 c = 256 + 256 * (gg % 2) + 128 * h
@@ -674,16 +692,17 @@ def rank_program(g, core, T, topo):
                 continue
             scan(R("FS"), R(rw), R(b), A.mult, A.max)
             tc(R("SM", 16 * FM + 8 * h + gs[0], 16 * FM + 8 * h + gs[0] + len(gs)), R("FS", wd - 1, 512, wd))
-        for h in range(2):
-            mm(hv("B0", h, 256), hv("MD", h), R("IXS"), True, True)
-        tt(R("B0", 256, 512), R("ENX"), R("B0", 256, 512), A.add)
-        tt(R("WM"), R("FIT"), R("B0", 256, 512), A.mult)
-        shifts(R("WM"), 256, "MVB", "B0", -1)
-        for h in range(2):
-            mm(hv("B0", h, 256), hv("WM", h), R("IDK"), True, True)
-        tt(R("W0", 0, 256), R("W0", 512, 768), R("B0", 256, 512), A.add)
+        w, p = R("MD"), R("B0", 0, 256)
+        for j in range(4):
+            tt(R("MA"), R("MK", 256 * j, 256 * j + 256), p if j else w, A.mult)
+            if j:
+                w = R("MW")
+                cp(w, p)
+            mm(p, R("IDF"), w, True, False)
+            mm(p, hv("SH", j), R("MA"), False, True)
+        tt(R("W0", 0, 256), R("W0", 512, 768), p, A.add)
         if t < 3:
-            moved(R("W2", 0, 256), R("MD"), R("B6", 0, 256), R("EQ2"))
+            moved(R("W2", 0, 256), R("MD"), R("B6", 0, 256))
         for h in range(2):
             mm(R("B2", 48 + 8 * h, 56 + 8 * h), hv("INDD", h), g8, True, False)
             mm(R("B2", 48 + 8 * h, 56 + 8 * h), own(h, "IND"), g8, False, True)
@@ -710,8 +729,8 @@ def rank_program(g, core, T, topo):
         mm(R("B2", 80, 112), R("TRI"), R("SB", 16, 48), True, False)
         mm(R("B2", 88, 96), R("ONEB"), R("SB", 16, 24), False, False)
         mm(R("B2", 104, 112), R("ONEB"), R("SB", 32, 40), False, True)
-        tt(S(TA, 64), again("SB", 0, 4), S(AV, 64), A.mult)
-        tt(S(TA, 64), S(TA, 64), bas(0, 64), A.add)
+        tt(S(TA, 32), again("SB", 0, 2), S(AV, 32), A.mult)
+        tt(S(TA, 32), S(TA, 32), R("BAS"), A.add)
         tc(S(RK), R("B2", 80, 96))
         tt(S(MN), S(NV), R("B2", 80, 96), A.min)
         tt(S(RK2), R("B2", 96, 112), S(MN), A.subtract)
@@ -723,23 +742,24 @@ def rank_program(g, core, T, topo):
         tt(S(VIS), S(VIS), S(IDL), A.mult)
         tt(S(T4), S(T4), S(VIS), A.mult)
         tt(S(LL + 4), S(T4), C(4), A.add)
-        tt(S(BV + 2, 32), again("SM", 16 * RK, 2), bas(2, 32), A.subtract)
-        tt(S(TB2, 64), again("SM", 16 * SPL, 4), S(BV, 64), A.mult)
-        tt(S(LL, 64), S(TA, 64), S(TB2, 64), A.add)
-        tc(R("LST", la, la + 16), wrap(LL + 4, 16, "EMW", 1024, "B2", 112))
+        tt(S(BV + 1), S(RK), R("BAS", 16, 32), A.subtract)
+        tt(S(TB2, 32), again("SM", 16 * SPL, 2), S(BV, 32), A.mult)
+        tt(S(LL, 32), S(TA, 32), S(TB2, 32), A.add)
+        tc(R("LST", la, la + 16), wrap(LL + 4, 16, "EMW", 512, "B2", 112))
         dst = (rank + 1 + t % (n - 1)) % n
         src = (rank - 1 - t % (n - 1)) % n
         tc(I("VS", 0, 336, "LST", la, la + 16), xs)
         send(dst, "XV%d" % t, "VS", "va%d" % t, "vl%d" % t)
-        tc(R("LST", 208, 224), wrap(LL + 3, 16, "EMW", 768, "B2", 176))
-        tc(R("LST", 160, 208), wrap(LL, 48, "EMW", 0, "B2", 128))
+        tc(R("LST", 208, 224), wrap(LL + 1, 16, "EMW", 256, "B2", 176))
+        tc(R("LST", 160, 176), wrap(LL, 16, "EMW", 0, "B2", 128))
         tc(R("TG"), I("TB", 0, NE + 1280, "LST", 208, 224))
         tc(R("LST", 224, 240), numbers("B2", 192, "TG", 16))
         tc(R("ML", t, 1024, 4), I("W0", 0, 768, "LST", 160, 176))
         tc(R("L2"), I("W1", 0, 768, "LST", 160, 176))
         tc(I("ML", 0, 1280, "LST", 224, 240), R("L2"))
-        tc(R("XE2", 0, 4096, 16), I("TB", 0, NE + 1280, "LST", 192, 208))
-        tc(I("ALT", 0, 1024, "LST", 176, 192), R("XE2", 0, 4096, 16))
+        tc(R("XE2", 0, 4096, 16), I("WP", 0, 768, "LST", 160, 176))
+        tc(R("ALT", t, 1024, 4), R("XE2", 0, 4096, 16))
+        tc(I("ALT", 0, 1280, "LST", 224, 240), R("WP", 0, 256))
         xv = "XV%d" % t
         tc(R("SJ", 0, 4), numbers("B1", 128, xv, 4, "WT"))
         mm(R("B1", 192, 256), R("WB"), R(xv), True, True)
@@ -748,21 +768,25 @@ def rank_program(g, core, T, topo):
         tc(R("OVG"), I("OW", 0, NO, "LST", 240, 244))
         if t < 3:
             tc(R("MVO"), I("W2", 0, 768, "LST", 160, 176))
-            settle("MVO")
+            spread()
+            settle("MVO", lambda o, i: act(o, i, F.Silu))
             mm(R("B2", 208, 224), R("ONEB"), mer, True, True)
             addup(S(E2, 1), R("B2", 208, 224))
             tc(R("SI", 96, 97), S(E2, 1))
             ts(R("SI", 96, 97), R("SI", 96, 97), 15, A.bitwise_and)
             tc(S(E2, 1), R("SI", 96, 97))
             ts(R("LIM", 32, 48), R("LIM", 0, 16), S(E2, 1), A.add)
-            sign(R("IND"), ml)
-            members(t + 1)
+            for u in range(1, 5):
+                sign(R("IND", (t + u) % 4, 1024, 4), R("ML", (t + u) % 4, 1024, 4))
             empties()
+            members(t + 1)
         else:
             ym = R("YM", 0, 1024)
-            ts(ym, ml, 0.0, A.is_equal, 4097.0, A.mult)
-            tt(ym, ym, ml, A.add)
-            ts(ym, ym, -1.0, A.add)
+            for h in range(2):
+                a, b, y = R("ML", 512 * h, 512 * h + 512), R("B%d" % (4 + h)), R("YM", 512 * h, 512 * h + 512)
+                relu(b, a, 4097.0, -4097.0)
+                lin(y, a, 1.0, -1.0)
+                tt(y, y, b, A.add)
             dma("oy", [(T.ym[:, :], ym[0])], ym[1], [])
         tc(R("SJ", 64, 128), R("B1", 192, 256))
         ts(R("SJ", 64, 128), R("SJ", 64, 128), 4095, A.bitwise_and)
@@ -770,7 +794,7 @@ def rank_program(g, core, T, topo):
         tc(R("XVS", 0, 1024, 16), R(xv))
         scan(R("XVE"), R("RM", 0, 1024), R("XVS"), A.mult, A.add)
         tc(R("LST", 244, 248), numbers("B1", 132, "OVG", 4))
-        tc(R("AVG"), I("ALT", 0, 1024, "LST", 244, 248))
+        tc(R("AVG"), I("ALT", 0, 1280, "LST", 244, 248))
         tc(R("HL1"), I("ML", 0, 1280, "LST", 244, 248))
         tc(R("LST", 248, 252), numbers("B1", 136, "AVG", 4))
         tt(R("EQV"), R("HL1"), R("VF"), A.is_equal)
@@ -804,18 +828,18 @@ def rank_program(g, core, T, topo):
         PLAN["order"] = plan(calls)
     count = {}
     known = {q: {} for q in queue}
-    mark = {}
+    seen = {}
     for i, q in PLAN["order"]:
         c = calls[i]
         e = c["sem"] or q
         if q == "x":
             count[e] = -c["inc"]
-            mark[i] = (e, count[e], {e: count[e]})
+            seen[i] = (e, count[e], {e: count[e]})
             continue
         best = {}
         for j, inline in c["dep"].items():
-            if not inline and best.get(mark[j][0], (0,))[0] < mark[j][1]:
-                best[mark[j][0]] = mark[j][1:]
+            if not inline and best.get(seen[j][0], (0,))[0] < seen[j][1]:
+                best[seen[j][0]] = seen[j][1:]
         for k, (v, ck) in sorted(best.items(), key=lambda x: -x[1][0]):
             if known[q].get(k, 0) < v:
                 queue[q].wait_ge(T.sem[k], v)
@@ -827,8 +851,8 @@ def rank_program(g, core, T, topo):
         count[e] = count.get(e, 0) + abs(c["inc"])
         ck = dict(known[q])
         ck[e] = count[e]
-        mark[i] = (e, count[e], ck)
-    for k in ("dm", "dx", "da", "dl", "dw", "ox", "oy", "v", "s", "p", "gg"):
+        seen[i] = (e, count[e], ck)
+    for k in SEMAPHORES[:17]:
         g.sync.wait_ge(T.sem[k], count[k])
     for t in range(4):
         for k in ("vl", "rl"):

@@ -1,3 +1,4 @@
+import numpy as np
 from concourse.mybir import AluOpType as A, ActivationFunctionType as F, AxisListType
 AX = AxisListType.X
 
@@ -17,17 +18,17 @@ def _sb(spec):
 
 
 SCRATCH = _sb({
-    "bfloat16": "X:4368 TX:4096 XE:4096 SQ:4096 XSE:4096 XA:4096 OWG:4096 RM:2048 QM:256 BM:512 ROW:1152 WQ:2048 WT:2048 "
-                "WE:2048 RW1:512 WP:768 IND:1024 CF:768 MM:512 TH2:512 ALT:1280 CT:1040 VS:336 XVE:1024 XVS:1024 VD:1024 RET:64",
-    "float32": "OW:8576 TB:2304 ML:1280 VAL:4096 KD:512 EMW:768 SM:1024 W:32x16 SH:512 MVA:528 W0:768 W1:768 W2:768",
-    "int32": "AC:4368 MI:1024 MK:1024 LMI:2 WTI:1 SJ:128 SK:2x16 SL:2x16",
+    "bfloat16": "X:4368 TX:4096 XE:4096 SQ:4096 XSE:4096 XA:4096 OWG:4096 RM:2048 QM:256 BM:512 ROW:1472 WQ:2048 WT:2048 "
+                "WE:2048 WP:768 IND:1024 CF:768 MM:512 TH2:256 KC:256 ALT:1280 VS:336 XVE:1024 XVS:1024 VD:1024 RET:64",
+    "float32": "OW:8576 TB:2304 ML:1280 VAL:4096 KD:512 EMW:768 SM:1024 W:16x16 WW:16x16 SH:512 MVA:128 W0:768 W1:768 W2:768",
+    "int32": "AC:4368 MI:1024 CT:1040 LMI:2 WTI:1 SJ:128 SK:2x16 SL:2x16",
     "uint16": "OFO:256 ACO:256 OFD:256 MVO:256 MV2:256 LST:256 HL:64 SOF:80 SRP:4"})
 WIDTH = {k: v[1][1] * (v[1][2] if len(v[1]) > 2 else 1) for k, v in SCRATCH.items()}
 PLACE = {k: (k, 0) for k in SCRATCH}
 for _pool, _dt, _names in (
-        ("PB", "bfloat16", "ONEB:128 IDB:128 NID:128 IDV:128 BO:128 G16:8 G512:16 G64:8 GS0:8 GC:64 WB:128 TRI:128 TSB:128 XS0:256 XS1:256 "
-                           "LMB:8 SB:64 OCB:64 NVB:8 CN:256 XB:256 UC:256 VM:256 INDD:256 NX1:256 OVG:64 AVG:64 EQV:64"),
-        ("PF", "float32", "QF:16 ONE:128 IDF:128 IDK:128 IXS:128 RB:8 DUM:256 CO:128 BAS:32 CIW:128 LMF:8 LIM:64 K1:256 KM:256 KBC:256 KV:128 "
+        ("PB", "bfloat16", "ONEB:128 IDB:128 NID:128 IDV:128 BO:128 G16:8 G1K:8 G512:16 G64:8 GS0:8 GC:64 WB:128 TRI:128 TSB:128 ID4:128 BW:512 XS0:256 XS1:256 "
+                           "LMB:8 SB:64 OCB:64 NVB:8 CN:256 XB:256 UC:256 VM:256 INDD:256 NX0:256 NX1:256 OVG:64 AVG:64 EQV:64"),
+        ("PF", "float32", "QF:16 ONE:128 IDF:128 IDK:128 IXS:128 JR:128 LR:256 RB:8 DUM:256 CO:128 BAS:32 CIW:128 LMF:8 LIM:64 K1:256 KM:256 KBC:256 KV:128 "
                           "EMA:256 EMB:256 EMV:128 EQ2:256 MD:256 MA:256 MW:256 GW:16 HL1:64 HL2:64 VF:64")):
     _at = 0
     for _x in _names.split():
@@ -50,7 +51,9 @@ for _k, _v, _at, _w in (("US", "OWG", 0, 4096), ("UD", "OWG", 0, 4096), ("TD", "
 SEMAPHORES = ["v", "s", "p", "gg", "dx", "da", "dm", "dl", "dw", "oy", "ox"] + ["dp%d" % j for j in range(6)] + ["%s%d" % (a, b) for a in ("va", "vl", "ra", "rl") for b in range(4)]
 PSUM = ["B%d" % b for b in range(8)]
 SIZE = {"float32": 4, "int32": 4, "bfloat16": 2, "uint16": 2}
-COST = {"cy": 0.9, "gat": 1.5, "sca": 3.0, "pe": 0.65, "wake": 150.0, "far": 3000.0, "dma": 3000.0, "look": 200.0, "sf": (2, 3, 4, 5), "turns": 6, "short": 256,
+COST = {"cy": 0.9, "gat": 1.5, "sca": 3.0, "pe": 0.65, "wake": 150.0, "far": 3000.0, "dma": 3000.0, "look": 200.0, "turns": 300,
+        "shake": (100.0, 300.0, 1000.0, 300.0),
+        "paces": (({"p": 0.7}, 100.0, 1.0), ({"gat": 0.8, "sca": 0.75}, 150.0, 1.0), ({"gat": 1.25, "sca": 1.65}, 120.0, 0.77)), "short": 256,
         "lean": (0.2, 0.3, 0.4, 0.5, 0.6)}
 PLAN = {}
 
@@ -108,14 +111,32 @@ def plan(calls):
     rank = [0.0] * len(calls)
     for i in range(len(calls) - 1, -1, -1):
         rank[i] = min(ns[i].values()) + max([rank[j] + gap for j, gap in after[i]] + [calls[i]["lat"]])
+
+    def length(order):
+        total = 0.0
+        for pace, wake, weight in COST["paces"]:
+            end, free = [0.0] * len(calls), {}
+            for i, q in order:
+                c = calls[i]
+                at = free.get(q, 0.0)
+                for j, inline in c["dep"].items():
+                    at = max(at, end[j] if inline else end[j] + calls[j]["lat"] + wake)
+                free[q] = end[i] = at + c["ns"][q] * pace.get(c["kind"], 1.0)
+            total += max(end) * weight
+        return total
     best = None
-    for lean in COST["lean"]:
-        now = issue(ns, after, rank, lean)
-        for _ in range(COST["turns"]):
-            now = issue(ns, after, issue(ns, before, now[1], lean)[1], lean)
-            if best is None or max(now[1]) < max(best[1]):
-                best = now
-    return best[0]
+    luck = np.random.default_rng(0)
+    for turn in range(COST["turns"]):
+        lean = COST["lean"][turn % len(COST["lean"])]
+        if turn < len(COST["lean"]):
+            end = issue(ns, after, rank, lean)[1]
+        else:
+            end = [x + float(y) for x, y in zip(best[2], luck.uniform(0.0, COST["shake"][turn % len(COST["shake"])], len(calls)))]
+        now = issue(ns, after, issue(ns, before, end, lean)[1], lean)
+        took = length(now[0])
+        if best is None or took < best[0]:
+            best = (took,) + now
+    return best[1]
 
 
 def rank_program(g, core, T, topo):
@@ -136,16 +157,16 @@ def rank_program(g, core, T, topo):
         ap = T[b][:, lo:hi:st] if full else T[b][p0:p1, lo:hi:st]
         return (ap, [(b, lo, hi, st)], -(-(hi - lo) // st))
 
-    def R3(b, a0, a1, k0, k1):
+    def R3(b, a0, a1, k0, k1, st=1):
         s = SCRATCH[b][1][2]
-        return (T[b][:, a0:a1, k0:k1], [(b, a0 * s, a1 * s, 1)], (a1 - a0) * (k1 - k0))
+        return (T[b][:, a0:a1, k0:k1:st], [(b, a0 * s, a1 * s, 1)], (a1 - a0) * -(-(k1 - k0) // st))
 
     def I(b, lo, hi, ob, o0, o1):
         b, at = PLACE[b]
         lo, hi = lo + at, hi + at
         return (T[b][:, lo:hi].indirect(T[ob][:, o0:o1]), [(b, lo, hi, 1), (ob, o0, o1, 1)], 16 * (o1 - o0))
 
-    def call(ways, reads, writes, sem=None, inc=1, lat=0.0, dma=False, fence=False, more=()):
+    def call(ways, reads, writes, sem=None, inc=1, lat=0.0, dma=False, fence=False, more=(), kind=None):
         me = len(calls)
         q = list(ways)[0] if len(ways) == 1 else None
         dep = {j: False for j in more}
@@ -177,7 +198,7 @@ def rank_program(g, core, T, topo):
                         continue
                     dep[j] = False
         calls.append({"f": {k: v[0] for k, v in ways.items()}, "ns": {k: v[1] for k, v in ways.items()}, "dep": dep, "sem": sem,
-                      "inc": inc, "lat": lat})
+                      "kind": q if kind is None else kind, "inc": inc, "lat": lat})
         for (b, lo, hi, st) in writes:
             keep = [r for r in log.get(b, []) if not (st == 1 and lo <= r[0] and r[1] <= hi)]
             log[b] = keep + [(lo, hi, st, True, q, me, dma)]
@@ -204,12 +225,15 @@ def rank_program(g, core, T, topo):
             m = ins[0][2]
         return 20 + max(m, 64) * COST["cy"]
 
+    def sort(out, ins):
+        return "sca" if len(out[1]) > 1 else "gat" if ins and len(ins[0][1]) > 1 else ""
+
     def vop(f, out, ins, two=False, other=None):
         rd, wr = sides(out, ins)
         ways = {"v": (f, ns("v", out, ins, two))}
         if other is not None:
             ways["s"] = (other, ns("s", out, ins))
-        call(ways, rd, wr)
+        call(ways, rd, wr, kind=sort(out, ins))
 
     def ap(x):
         return x[0] if isinstance(x, tuple) else x
@@ -260,7 +284,7 @@ def rank_program(g, core, T, topo):
 
     def act(o, i, f):
         rd, wr = sides(o, [i])
-        call({"s": (lambda: g.scalar.activation(o[0], i[0], f), ns("s", o, [i]))}, rd, wr)
+        call({"s": (lambda: g.scalar.activation(o[0], i[0], f), ns("s", o, [i]))}, rd, wr, kind=sort(o, [i]))
 
     def over(acc, i, bias, o):
         call({"s": (lambda: g.scalar.activation(o[0], i[0], F.Relu, bias=bias[0], accum_out=acc[0]), 20 + ns("s", o, [i]))},
@@ -285,7 +309,7 @@ def rank_program(g, core, T, topo):
         call({"y": (f, 100.0 * len(pairs))}, reads, writes, sem, 16 * len(pairs), COST["dma"] + 1000.0 * len(pairs), True)
 
     def send(dst, ob, ib, rs, ls):
-        eng = topo.engines(core, T.cores[dst])[:4]
+        eng = topo.engines(core, T.cores[dst])[:8]
         mask = sum(1 << e for e in eng)
         rid, pid, _se = topo.addr(T.cores[dst])
         i = R(ib, 0, 64)
@@ -300,6 +324,9 @@ def rank_program(g, core, T, topo):
 
     def mark(o, k, c):
         aff(o, o, [[-16, 8]], A.not_equal, c, -k, 1)
+
+    def aside(o, i):
+        aff(o, i, [[0, o[2]]], A.is_ge, 0.0, 0, 0)
 
     def bounded(o, pat, base, cm, width):
         aff(o, o, pat, A.is_ge, 0.0, base, cm)
@@ -351,21 +378,6 @@ def rank_program(g, core, T, topo):
                 dma("dp%d" % (2 * was - 2 + h), [(plane(2 + u), plane(6)), (plane(2 + was), plane(2 + (u + 1) % 4))], half("VAL", h)[1], half("VAL", h)[1])
         settle(mv, put)
 
-    def shifts(b, mv, bank):
-        width = WIDTH[b]
-        w, p = R3(b, 0, width // 16, 0, 16), R(bank, 0, width)
-        for th, s in ((4096.0, 1), (512.0, 2), (64.0, 4)):
-            lin(p, w, -th, th * th)
-            relu(R(mv, 8, 8 + width), w, -th)
-            tt(p, w, p, A.min)
-            tt(w, R(mv, 8 + s, 8 + s + width), p, A.max)
-        fro, to = [R3(b, 0, width // 16, a, a + 8) for a in (8, 0)]
-        p0, p1 = R(bank, 0, width // 2), R(bank, width // 2, width)
-        ts(p0, fro, 8.0, A.is_lt)
-        ts(p1, fro, -8.0, A.add, 0.0, A.max)
-        tt(fro, fro, p0, A.mult)
-        tt(to, to, p1, A.max)
-
     def numbers(bank, lo, src, cols, wq="WQ"):
         for q in range(16):
             mm(R(bank, lo, lo + cols), R(wq, 128 * q, 128 * q + 128), R(src, q, 16 * cols, 16), q == 0, q == 15)
@@ -391,8 +403,9 @@ def rank_program(g, core, T, topo):
     dma("dl", [(T.LMI[:], T.lims[:, :])], [], R("LMI")[1])
     dma("dw", [(T.WTI[:], T.wt[:, :])], [], R("WTI")[1])
     iota(R("DUM"), [[16, 256]], D0, 1)
-    fill(R("OW", 2304, 4112), 128)
-    ms(R("OW", 0, 2304), 128.0)
+    ms(R("OW", 0, 528), 128.0)
+    for w in (512, 1024, 2048):
+        act(R("OW", 16 + w, 16 + 2 * w), R("OW", 16, 16 + w), F.Copy)
     fill(R("XE"), 0)
     ms(R("RM"), 1.0)
     ms(R("RM", 0, 2048, 16), 0.0)
@@ -421,9 +434,9 @@ def rank_program(g, core, T, topo):
         owners(u)
     for b in ("VS", "XVS", "MVA"):
         fill(R(b), 0)
-    for b, c in (("IDF", 1.0), ("IDK", 1024.0), ("IXS", 2.0 ** -10)):
+    for b, c in (("IDF", 1.0), ("IDK", 2048.0), ("IXS", 2.0 ** -11)):
         diag(R(b), R("MVA", 0, 128), c)
-    for b, c in (("IDB", 1.0), ("NID", -1.0), ("IDV", float(2 ** 18))):
+    for b, c in (("IDB", 1.0), ("NID", -1.0), ("ID4", 4.0), ("IDV", float(2 ** 18))):
         diag(R(b), R("VS", 0, 128), c)
     for b in ("ONEB", "BO", "RB"):
         fill(R(b), 1)
@@ -431,26 +444,32 @@ def rank_program(g, core, T, topo):
     bounded(R("RB"), [[-16, 8]], 0, 1, 16)
     aff(R("TRI"), R("ONEB"), [[1, 128]], A.is_gt, 0.0, 0, -1)
     aff(R("TSB"), R("BO"), [[-1, 128]], A.is_ge, 0.0, 0, 1)
-    for b, c in ((R("G16"), 16.0), (R("G64"), 65536.0), (R("G512", 0, 8), 512.0), (R("G512", 8, 16), 512.0)):
+    for b, c in ((R("G16"), 16.0), (R("G1K"), 1024.0), (R("G64"), 65536.0), (R("G512", 0, 8), 512.0), (R("G512", 8, 16), 512.0)):
         ts(b, g8, c, A.mult)
     for j in range(4):
         aff(hv("SH", j), R("MVA", 0, 128), [[1, 128]], A.not_equal, 1.0, -2 ** j, -1)
         bounded(hv("SH", j), [[-16, 8], [0, 16]], 0, 1, 16)
         diag(hv("SH", j), hv("SH", j), -1.0)
+    aff(R("JR"), R("MVA"), [[-16, 8], [1, 16]], A.not_equal, 1.0, -15, 1)
+    iota(R("KC"), [[0, 16], [-1, 16]], 16, 0)
+    iota(R("ZI", 0, 128), [[0, 8], [4369, 16]], 0, 0)
+    for j, bits in enumerate((4608, 72)):
+        ts(R("ZI", 128, 256), R("ZI", 0, 128), bits, A.bitwise_and)
+        ts(R("ROW", 1152 + 128 * j, 1280 + 128 * j), R("ZI", 128, 256), -2048.0, A.mult)
     fill(R("GS0"), 0)
     mark(R("GS0"), 0, 1.0)
-    for o, pat, base in ((0, [[0, 8], [4096, 16]], 0), (128, [[0, 8], [1, 16]], 0), (256, [[0, 16], [-1, 16]], 15), (512, [[0, 128]], -1),
-                         (640, [[0, 2], [-384, 2], [0, 8]], 0)):
-        w = 1
-        for x in pat:
-            w *= x[1]
-        iota(R("W1", o, o + w), pat, base, 0)
-    tc(R("ROW", 0, 640), R("W1", 0, 640))
-    iota(R("KD"), [[0, 32], [32, 16]], -128, 0)
+    for o, w, pat, base in ((0, 128, [[0, 8], [4096, 16]], 0), (128, 128, [[0, 8], [1, 16]], 0), (256, 256, [[0, 16], [-1, 16]], 15),
+                            (512, 128, [[0, 128]], -1), (640, 256, [[-384, 2], [0, 8], [32, 16]], -128),
+                            (896, 256, [[-384, 2], [0, 8], [32, 16]], -128)):
+        iota(R("ROW", o, o + w), pat, base, 0)
     iota(R("SJ", 96, 100), [[0, 4]], 0, 1)
     ts(R("SJ", 96, 100), R("SJ", 96, 100), 15, A.bitwise_and)
     tc(R("SRP"), R("SJ", 96, 100))
-    tt(R("ROW", 640, 1152), wide("W1", 640, 32), R("KD"), A.add)
+    ts(R("SJ", 97, 98), R("SJ", 96, 97), 1, A.add)
+    for j in range(4):
+        ts(R("SJ", 100, 102), R("SJ", 96, 98), j, A.logical_shift_right, 1, A.bitwise_and)
+        tt(R("LMB", 6, 7), R("SJ", 101, 102), R("SJ", 100, 101), A.subtract)
+        ts(hv("BW", j), R("BO"), R("LMB", 6, 7), A.mult)
     fill(R("BM"), 0)
     ms(R("BM", 0, 512, 16), float(2 ** 25))
     wc = R("SM", 0, 1)
@@ -468,12 +487,10 @@ def rank_program(g, core, T, topo):
     lanes(C(0), 4096, 1)
     lanes(C(1), 15, 16)
     lanes(C(2), 11 * 2 ** 18, -1)
-    ts(R("LMF", 7, 8), R("CO", 40, 41), -1.0, A.mult)
-    for i in COST["sf"]:
-        ms(R("CO", 36 + 2 * i, 38 + 2 * i), 0.0)
+    ts(R("LMF", 6, 8), R("CO", 32, 48, 8), -1.0, A.mult)
     lanes(C(3), 1024, 1)
     lanes(C(4), 64, 1)
-    iota(C(5), [[0, 16]], 0, 16)
+    iota(R("ROW", 1408, 1472), [[16, 64]], 0, 0)
     for j, base in enumerate((512, NE + 1024)):
         lanes(R("BAS", 16 * j, 16 * j + 16), base, 1)
     iota(R("CIW", 0, 64), [[16, 64]], 0, 0)
@@ -483,23 +500,19 @@ def rank_program(g, core, T, topo):
     fill(R("WQ"), 1)
     aff(R("WQ"), R("WQ"), [[1, 16], [0, 8], [-1, 16]], A.is_equal, 0.0, 0, 0)
     bounded(R("WQ"), [[0, 16], [-16, 8], [0, 16]], 0, 1, 16)
-    fill(R("RW1"), 1)
-    aff(R("RW1"), R("RW1"), [[0, 4], [1, 128]], A.is_gt, 0.0, 0, 0)
     for k in range(11):
         mark(R("GW", 8, 16), k, float(2 ** (10 - k)))
     addup(R("LMF", 0, 1), R("GW", 8, 16))
     ts(R("LMF", 5, 6), R("LMF", 0, 1), 0.0, A.is_gt, -512.0, A.mult)
-    iota(mi, [[1, 1024]], 1, 0)
-    ts(mi, mi, R("LMF", 0, 1), A.mult)
-    ts(mi, mi, 1024, A.bitwise_and)
-    ts(R("CT", 1, 1025), mi, R("LMF", 5, 6), A.add)
-    tc(R("CT", 0, 1), R("LMF", 5, 6))
+    iota(R("CT"), [[1, 1040]], 0, 0)
+    ts(R("CT"), R("CT"), R("LMF", 0, 1), A.mult)
+    ts(R("CT"), R("CT"), 1024, A.bitwise_and)
     for a in (0, 1):
         addup(R("LMF", 1 + a, 2 + a), R("RB", a, 8, 2))
         tt(R("LMB", 4 + a, 5 + a), R("LMF", 1 + a, 2 + a), q_(15), A.mult)
         tt(R("LMB", 2 + a, 3 + a), R("LMF", 1 + a, 2 + a), R("LMB", 4 + a, 5 + a), A.subtract)
     iota(R("K1"), [[-1, 256]], 0, 0)
-    ts(R("CN"), R("K1"), q_(15), A.mult)
+    ts(R("CN"), R("K1"), q_(15), A.mult, R("LMF", 5, 6), A.add)
     tc(R("SM", 12, 14), R("LMI"))
     for j in range(2):
         ts(R("VM", 128 * j, 128 * j + 128), one, R("SM", 12 + j, 13 + j), A.mult)
@@ -509,7 +522,7 @@ def rank_program(g, core, T, topo):
     tc(R("LIM", 32, 48), R("LIM", 0, 16))
     fill(R("W1"), 0)
     for u in range(4):
-        fill(R("ME%d" % u, 64, 336), 0)
+        fill(R("ME%d" % u, 64, 336), 192)
     cp(R("W2", 512, 768), R("DUM"))
     fill(R("ALT"), 128)
     fill(R("WP", 512, 768), 128)
@@ -522,7 +535,7 @@ def rank_program(g, core, T, topo):
     (NN, LIVE, LS, LB, SUU, GRL, N16, HAS, FM, DD, T1, T2, T3, OK, SPL, RK, NV, MN, RK2, IDL, VIS, T4, LV, E1, E2, E3) = range(2, 28)
     AV, BV, TA, TB2, LL = 32, 36, 40, 44, 48
     EU = 56
-    for a, c in ((LV, 0), (AV, -512), (BV, -256)):
+    for a, c in ((AV, -512), (BV, -256)):
         fill(S(a), c)
 
     def empties():
@@ -585,16 +598,12 @@ def rank_program(g, core, T, topo):
         ts(R("SI", 32, 48), R("SI", 0, 16), 16, A.logical_shift_right)
         for h in range(2):
             scan(half("US", h), R("RM"), half("TX", h), A.mult, A.max)
-        tc(R("UC"), R("US", 15, 4096, 16))
+        aside(R("UC"), R("US", 15, 4096, 16))
         for h in range(2):
             mm(R("B2", 16 + 8 * h, 24 + 8 * h), hv("UC", h), g8, True, True)
         tt(S(GRL), R("B2", 16, 32), R("SI", 32, 48), A.subtract)
         tt(S(GRL), S(GRL), R("LIM", 16, 32), A.is_gt)
         tt(S(GRL), S(GRL), S(LIVE), A.mult)
-        mm(R("B3", 0, 256), R("BO"), R("IND", t, 1024, 4), True, True)
-        tc(R("ZC"), R("B3", 0, 256))
-        for j in range(4):
-            ts(R("MK", 256 * j, 256 * j + 256), R("ZC"), j, A.logical_shift_right, 1, A.bitwise_and)
         for kk in range(8):
             squares(xs, ("B4", "B5")[kk % 2], kk)
         for h in range(2):
@@ -610,8 +619,6 @@ def rank_program(g, core, T, topo):
         tt(S(LB), C(1), R("SI", 48, 64), A.subtract)
         tc(R("LST", 32, 48), wrap(LB, 16, "EMA", 0, "B0", 0))
         tc(R("XB"), I("TX", 0, 4096, "LST", 32, 48))
-        for h in range(2):
-            mm(hv("B6", h, 256), own(h), R("IXS"), True, True)
         for kk in range(8):
             squares(R("XB"), ("B4", "B5")[kk % 2], kk)
         mm(R("B6", 0, 256), lone, row(256, 256), True, False)
@@ -619,23 +626,34 @@ def rank_program(g, core, T, topo):
             for h in range(2):
                 mm(R("B6", 128 * h + k, 128 * h + 128, 16), R("SQ", 256 * k + 128 * h, 256 * k + 128 * h + 128), R("G16"), False, k == 15 and h == 1)
         tt(R("MM", 256, 512), R("KBC"), R("B6", 0, 256), A.is_gt)
-        tt(R("MM", 0, 256), R("KBC"), R("B6", 0, 256), A.is_le)
-        scan(R("TH2", 0, 256), R("RM", 0, 256), R("MM", 256, 512), A.mult, A.add)
-        scan(R("TH2", 256, 512), R("RM", 0, 256), R("MM", 0, 256), A.mult, A.add)
-        ts(R("ZI"), R("TH2"), 4369.0, A.mult)
-        ts(R("ZI"), R("ZI"), 4680, A.bitwise_and)
-        for f in range(2):
-            tt(R("B4", 256 * f, 256 * f + 256), R("ZI", 256 * f, 256 * f + 256), R("B6", 256, 512), A.add)
-        tt(R3("W", 0, 32, 0, 16), R("MM"), R("B4"), A.mult)
-        shifts("W", "MVA", "B5")
-        for j in range(4):
-            mm(hv("B6", j), R3("W", 8 * j, 8 * j + 8, 0, 16), R("IDK"), True, True)
-        cp(R("W0", 256, 512), R("B6", 0, 256))
-        cp(R("W1", 256, 512), R("B6", 256, 512))
+        ts(R("MM", 0, 256), R("MM", 256, 512), -1.0, A.mult, 1.0, A.add)
+        mm(R("B6", 256, 512), R("ID4"), R("MM", 256, 512), True, False)
+        for h in range(2):
+            mm(hv("B6", h, 256), own(h), R("IXS"), False, h == 1)
+        zi = R("ZI", 0, 256)
+        scan(R("TH2"), R("RM", 0, 256), R("MM", 0, 256), A.mult, A.add)
+        tt(R("B4", 0, 256), R("MM", 256, 512), R("KC"), A.mult)
+        tt(R("TH2"), R("TH2"), R("B4", 0, 256), A.add)
+        ts(zi, R("TH2"), -1.0, A.add, 4369.0, A.mult)
+        ts(zi, zi, 4680, A.bitwise_and)
+        tt(R3("W", 0, 16, 0, 16), zi, R("B6", 256, 512), A.add)
+        for a, b in (("W", "WW"), ("WW", "W")) * 2:
+            for k, f in ((0, A.min), (8, A.max)):
+                tt(R3(b, 0, 16, k, k + 8), R3(a, 0, 16, 0, 16, 2), R3(a, 0, 16, 1, 16, 2), f)
+        p = R("B5", 0, 256)
+        for h in range(2):
+            mm(hv("B5", h), row(1152, 128), lone, True, False)
+            mm(hv("B5", h), row(1280, 128), lone, False, False)
+            mm(hv("B5", h), R3("W", 8 * h, 8 * h + 8, 0, 16), R("IDK"), False, True)
+        relu(R("LR"), p, -8192.0)
+        mm(R("B4", 256, 512), R("JR"), R("LR"), True, True)
+        cp(R("W1", 256, 512), R("B4", 256, 512))
+        ts(R("KBC"), p, 8192.0, A.is_lt)
+        tt(R("W0", 256, 512), R("KBC"), p, A.mult)
         if t < 3:
-            moved(R("W2", 256, 512), R("W1", 256, 512), R("B4", 0, 256))
-        cp(R("W0", 512, 768), R("ML", t, 1024, 4))
-        cp(R("WP", 0, 256), R("TB", NE + t, NE + 1024, 4))
+            moved(R("W2", 256, 512), R("LR"), R("B6", 0, 256))
+        aside(R("W0", 512, 768), R("ML", t, 1024, 4))
+        aside(R("WP", 0, 256), R("TB", NE + t, NE + 1024, 4))
 
     empties()
     members(0)
@@ -678,49 +696,45 @@ def rank_program(g, core, T, topo):
         for i in range(6):
             b = ("B3", "B7")[i % 2]
             if i < 2:
-                h, gs, wd, rw = 0, range(4 * i, 4 * i + 4), 128, "RW1"
+                h, gs, wd = 0, range(4 * i, 4 * i + 4), 128
             else:
-                h, gs, wd, rw = 1, range(2 * (i - 2), 2 * (i - 2) + 2), 256, None
+                h, gs, wd = 1, range(2 * (i - 2), 2 * (i - 2) + 2), 256
             for j, gg in enumerate(gs):
                 p0 = 32 * (gg // 2)
                 c = 256 + 256 * (gg % 2) + 128 * h
                 mm(R(b, wd * j, wd * j + wd), R("CF", c, c + 128, 1, p0, p0 + 32), R("CF", 0, wd, 1, p0, p0 + 32), True, True,
                    j > 0 and p0 != 32 * (gs[j - 1] // 2))
-            if i in COST["sf"]:
-                for j, gg in enumerate(gs):
-                    over(R("SM", 16 * FM + 8 * h + gg, 16 * FM + 8 * h + gg + 1), R(b, wd * j, wd * j + wd), R("LMF", 7, 8), R("FS", wd * j, wd * j + wd))
-                continue
-            scan(R("FS"), R(rw), R(b), A.mult, A.max)
-            tc(R("SM", 16 * FM + 8 * h + gs[0], 16 * FM + 8 * h + gs[0] + len(gs)), R("FS", wd - 1, 512, wd))
+            for j, gg in enumerate(gs):
+                over(R("SM", 16 * FM + 8 * h + gg, 16 * FM + 8 * h + gg + 1), R(b, wd * j, wd * j + wd), R("LMF", 6 + h, 7 + h), R("FS", wd * j, wd * j + wd))
         w, p = R("MD"), R("B0", 0, 256)
         for j in range(4):
-            tt(R("MA"), R("MK", 256 * j, 256 * j + 256), p if j else w, A.mult)
+            mm(R("B0", 256, 512), hv("BW", j), R("IND", t, 1024, 4), True, True)
             if j:
                 w = R("MW")
                 cp(w, p)
+            tt(R("MA"), w, R("B0", 256, 512), A.mult)
             mm(p, R("IDF"), w, True, False)
             mm(p, hv("SH", j), R("MA"), False, True)
         tt(R("W0", 0, 256), R("W0", 512, 768), p, A.add)
         if t < 3:
-            moved(R("W2", 0, 256), R("MD"), R("B6", 0, 256))
+            moved(R("W2", 0, 256), R("MD"), R("B2", 256, 512))
         for h in range(2):
             mm(R("B2", 48 + 8 * h, 56 + 8 * h), hv("INDD", h), g8, True, False)
             mm(R("B2", 48 + 8 * h, 56 + 8 * h), own(h, "IND"), g8, False, True)
         ts(S(T2), R("B2", 48, 64), 16.0, A.is_le)
         tt(S(T2), S(T2), S(HAS), A.mult)
         for h in range(2):
-            for k in range(16):
+            for k in range(15):
                 mm(R("B1", 128 * h + k, 128 * h + 128, 16), R("TD", 2048 * h + k, 2048 * h + 2048, 16), g8, True, True)
         act(R("KA"), R("B1", 0, 256), F.Abs)
         for h in range(2):
+            tc(R("TD", 2048 * h + 15, 2048 * h + 2048, 16), hv("UC", h))
             scan(half("UD", h), R("RM"), half("TD", h), A.mult, A.max)
-            tt(hv("VM", h), hv("UC", h), R("UD", 2048 * h + 15, 2048 * h + 2048, 16), A.max)
-            mm(R("B2", 64 + 8 * h, 72 + 8 * h), hv("VM", h), g8, True, True)
+            mm(R("B2", 64 + 8 * h, 72 + 8 * h), R("UD", 2048 * h + 15, 2048 * h + 2048, 16), g8, True, True)
         scan(R("MSD"), R("BM", 0, 256), R("KA"), A.max, A.min)
-        tt(S(T3), R("SI", 32, 48), R("MSD", 15, 256, 16), A.min)
+        tt(S(T3), R("SI", 32, 48), R("MSD", 14, 256, 16), A.min)
         tt(S(T3), S(T3), R("LIM", 32, 48), A.add)
-        tt(S(OK), S(FM), C(2), A.is_equal)
-        tt(S(OK), S(OK), S(T2), A.mult)
+        tt(S(OK), S(T2), S(FM), A.is_gt)
         tt(S(T3), S(T3), R("B2", 64, 80), A.is_ge)
         mer, want, nm = R("SB", 0, 16), R("SB", 16, 32), R("SB", 32, 48)
         tt(mer, S(T3), S(OK), A.mult)
@@ -731,10 +745,9 @@ def rank_program(g, core, T, topo):
         mm(R("B2", 104, 112), R("ONEB"), R("SB", 32, 40), False, True)
         tt(S(TA, 32), again("SB", 0, 2), S(AV, 32), A.mult)
         tt(S(TA, 32), S(TA, 32), R("BAS"), A.add)
-        tc(S(RK), R("B2", 80, 96))
         tt(S(MN), S(NV), R("B2", 80, 96), A.min)
         tt(S(RK2), R("B2", 96, 112), S(MN), A.subtract)
-        tt(S(SPL), S(RK), S(NV), A.is_lt)
+        tt(S(SPL), S(NV), R("B2", 80, 96), A.is_gt)
         tt(S(SPL), S(SPL), want, A.mult)
         tt(S(IDL), nm, S(SPL), A.subtract)
         ts(S(VIS), S(RK2), 64.0, A.is_lt)
@@ -742,7 +755,7 @@ def rank_program(g, core, T, topo):
         tt(S(VIS), S(VIS), S(IDL), A.mult)
         tt(S(T4), S(T4), S(VIS), A.mult)
         tt(S(LL + 4), S(T4), C(4), A.add)
-        tt(S(BV + 1), S(RK), R("BAS", 16, 32), A.subtract)
+        tt(S(BV + 1), R("B2", 80, 96), R("BAS", 16, 32), A.subtract)
         tt(S(TB2, 32), again("SM", 16 * SPL, 2), S(BV, 32), A.mult)
         tt(S(LL, 32), S(TA, 32), S(TB2, 32), A.add)
         tc(R("LST", la, la + 16), wrap(LL + 4, 16, "EMW", 512, "B2", 112))
@@ -758,7 +771,7 @@ def rank_program(g, core, T, topo):
         tc(R("L2"), I("W1", 0, 768, "LST", 160, 176))
         tc(I("ML", 0, 1280, "LST", 224, 240), R("L2"))
         tc(R("XE2", 0, 4096, 16), I("WP", 0, 768, "LST", 160, 176))
-        tc(R("ALT", t, 1024, 4), R("XE2", 0, 4096, 16))
+        aside(R("ALT", t, 1024, 4), R("XE2", 0, 4096, 16))
         tc(I("ALT", 0, 1280, "LST", 224, 240), R("WP", 0, 256))
         xv = "XV%d" % t
         tc(R("SJ", 0, 4), numbers("B1", 128, xv, 4, "WT"))
@@ -791,7 +804,7 @@ def rank_program(g, core, T, topo):
         tc(R("SJ", 64, 128), R("B1", 192, 256))
         ts(R("SJ", 64, 128), R("SJ", 64, 128), 4095, A.bitwise_and)
         ts(R("VF"), R("SJ", 64, 128), 1, A.add)
-        tc(R("XVS", 0, 1024, 16), R(xv))
+        aside(R("XVS", 0, 1024, 16), R(xv))
         scan(R("XVE"), R("RM", 0, 1024), R("XVS"), A.mult, A.add)
         tc(R("LST", 244, 248), numbers("B1", 132, "OVG", 4))
         tc(R("AVG"), I("ALT", 0, 1280, "LST", 244, 248))
@@ -804,23 +817,24 @@ def rank_program(g, core, T, topo):
         tt(R("HL1"), R("HL1"), R("B1", 256, 320), A.mult)
         tt(R("HL1"), R("HL1"), R("HL2"), A.add)
         tc(R("HL"), R("HL1"))
-        tt(R("VD"), I("X", 0, NX, "HL", 0, 64), R("XVE"), A.subtract)
-        act(R("SQV"), R("VD"), F.Square)
+        for h in range(2):
+            vd = R("VD", 512 * h, 512 * h + 512)
+            tt(vd, I("X", 0, NX, "HL", 32 * h, 32 * h + 32), R("XVE", 512 * h, 512 * h + 512), A.subtract)
+            act(R("SQV", 512 * h, 512 * h + 512), vd, F.Square)
         mm(R("B1", 0, 128, 1, 0, 64), R("ONEB", 0, 64, 1, 0, 1), row(128, 128), True, False)
+        mm(R("B1", 0, 128, 1, 0, 64), row(1408, 64), lone, False, False)
         for k in range(16):
-            mm(R("B1", k, 128, 16, 0, 64), R("SQV", k, 1024, 16), R("G16"), False, k == 15)
+            mm(R("B1", k, 128, 16, 0, 64), R("SQV", k, 1024, 16), R("G1K"), False, k == 15)
         scan(R("KV", 0, 128, 1, 0, 64), R("BM", 0, 128, 1, 0, 64), R("B1", 0, 128, 1, 0, 64), A.max, A.min)
         tc(R("SJ", 8, 16, 1, 0, 64), R("KV", 15, 128, 16, 0, 64))
-        ts(R("SJ", 8, 16, 1, 0, 64), R("SJ", 8, 16, 1, 0, 64), 15, A.bitwise_and)
-        tt(R("SM", 16 * LV, 16 * LV + 8, 1, 0, 64), R("SJ", 8, 16, 1, 0, 64), R("CO", 80, 88, 1, 0, 64), A.add)
-        tt(R("EMV"), wide("SM", 16 * LV, 8), R("QM", 0, 128), A.mult)
+        ts(R("SJ", 8, 16, 1, 0, 64), R("SJ", 8, 16, 1, 0, 64), 1023, A.bitwise_and)
+        tt(R("EMV"), wide("SJ", 8, 8), R("QM", 0, 128), A.mult)
         mm(R("B1", 140, 144), R("EMV", 0, 128, 1, 0, 64), R("RB", 0, 4, 1, 0, 64), True, True)
         tc(R("LST", 252, 256), R("B1", 140, 144))
-        tc(R("SJ", 64, 128), I("VD", 0, 1024, "LST", 252, 256))
-        ts(R("SJ", 64, 128), R("SJ", 64, 128), 1, A.arith_shift_right)
-        tc(R("RET"), R("SJ", 64, 128))
+        ts(R("RET"), I("VD", 0, 1024, "LST", 252, 256), 0.5, A.mult, 191.75, A.add)
         send(src, "ME%d" % t, "RET", "ra%d" % t, "rl%d" % t)
-        tt(R("NX1"), I("ME%d" % t, 0, 336, "LST", la, la + 16), xs, A.add)
+        ts(R("NX0"), xs, -192.0, A.add)
+        tt(R("NX1"), I("ME%d" % t, 0, 336, "LST", la, la + 16), R("NX0"), A.add)
         tc(I("X", 0, NX, "LST", ls, ls + 16), R("NX1"))
     dma("ox", [(T.yx[:, :], T.X[:, 1:4097])], R("X", 1, 4097)[1], [])
 

@@ -18,11 +18,11 @@ def _sb(spec):
 
 
 SCRATCH = _sb({
-    "bfloat16": "X:4368 TX:4096 XE:4096 SQ:4096 XSE:4096 XA:4096 OWG:4096 RM:2048 QM:256 BM:512 ROW:1472 WQ:2048 WT:2048 "
-                "WE:2048 WP:768 IND:1024 CF:768 MM:512 TH2:256 KC:256 ALT:1280 VS:336 XVE:1024 XVS:1024 VD:1024 RET:64",
-    "float32": "OW:8576 TB:2304 ML:1280 VAL:4096 KD:512 EMW:768 SM:1024 W:16x16 WW:16x16 SH:512 MVA:128 W0:768 W1:768 W2:768",
+    "bfloat16": "X:4368 TX:4096 XE:4096 SQ:4096 XSE:4096 XA:4096 OWG:4096 RM:1024 QM:256 BM:512 ROW:1472 WQ:2048 WT:2048 "
+                "WE:2048 WP:768 IND:1024 CF:768 MM:512 TH2:256 KC:256 VS:336 XVE:1024 XVS:1024 VD:1024 RET:64",
+    "float32": "OW:8576 TB:2304 ML:1280 VAL:4096 KD:512 EMW:768 SM:784 W:16x16 WW:16x16 SH:512 ALT:1280 PCF:256 MVA:128 W0:768 W1:768 W2:768",
     "int32": "AC:4368 MI:1024 CT:1040 LMI:2 WTI:1 SJ:128 SK:2x16 SL:2x16",
-    "uint16": "OFO:256 ACO:256 OFD:256 MVO:256 MV2:256 LST:256 HL:64 SOF:80 SRP:4"})
+    "uint16": "OFO:256 ACO:256 OFD:256 MVO:256 LST:256 HL:64 SOF:80 SRP:4"})
 WIDTH = {k: v[1][1] * (v[1][2] if len(v[1]) > 2 else 1) for k, v in SCRATCH.items()}
 PLACE = {k: (k, 0) for k in SCRATCH}
 for _pool, _dt, _names in (
@@ -48,13 +48,12 @@ for _k, _v, _at, _w in (("US", "OWG", 0, 4096), ("UD", "OWG", 0, 4096), ("TD", "
                         ("KB", "KM", 0, 256), ("L2", "MD", 0, 256), ("ZI", "MI", 0, 512), ("ZC", "MI", 512, 256), ("SI", "MI", 768, 256),
                         ("TG", "WP", 256, 256)):
     PLACE[_k], WIDTH[_k] = (PLACE[_v][0], PLACE[_v][1] + _at), _w
-SEMAPHORES = ["v", "s", "p", "gg", "dx", "da", "dm", "dl", "dw", "oy", "ox"] + ["dp%d" % j for j in range(6)] + ["%s%d" % (a, b) for a in ("va", "vl", "ra", "rl") for b in range(4)]
+SEMAPHORES = ["v", "s", "p", "gg", "dx", "da", "dm0", "dm1", "dl", "dw", "dz", "dr", "oy", "ox"] + ["dp%d" % j for j in range(4)] + ["%s%d" % (a, b) for a in ("va", "vl", "ra", "rl") for b in range(4)]
 PSUM = ["B%d" % b for b in range(8)]
 SIZE = {"float32": 4, "int32": 4, "bfloat16": 2, "uint16": 2}
-COST = {"cy": 0.9, "gat": 1.5, "sca": 3.0, "pe": 0.65, "wake": 150.0, "far": 3000.0, "dma": 3000.0, "look": 200.0, "turns": 300,
-        "shake": (100.0, 300.0, 1000.0, 300.0),
-        "paces": (({"p": 0.7}, 100.0, 1.0), ({"gat": 0.8, "sca": 0.75}, 150.0, 1.0), ({"gat": 1.25, "sca": 1.65}, 120.0, 0.77)), "short": 256,
-        "lean": (0.2, 0.3, 0.4, 0.5, 0.6)}
+COST = {"cy": 0.9, "gat": 1.5, "sca": 3.0, "pe": 0.65, "wake": 150.0, "far": 3000.0, "dma": 3000.0, "look": 200.0, "turns": 100,
+        "shake": (100.0, 300.0, 1000.0, 300.0), "seed": 1, "mend": 3000, "swap": 8000, "short": 256, "lean": (0.0, 0.15, 0.3, 0.45, 0.6),
+        "paces": (({"p": 0.7}, 100.0, 1.0, 1.0), ({"gat": 0.8, "sca": 0.75}, 150.0, 1.3, 1.0), ({"gat": 1.25, "sca": 1.65}, 120.0, 0.8, 0.77))}
 PLAN = {}
 
 
@@ -67,16 +66,18 @@ def issue(ns, after, rank, lean):
     ready, end = [0.0] * n, [0.0] * n
     free = {q: 0.0 for q in ("v", "s", "p", "gg", "y", "x")}
     pool = {q: set() for q in free}
+    first = {}
     order = []
 
     def enter(i):
         for q in ns[i]:
             pool[q].add(i)
+            first[q] = min(first.get(q, 1e18), ready[i])
     for i in range(n):
         if not left[i]:
             enter(i)
     while len(order) < n:
-        now, q = min((max(free[q], min(ready[i] for i in pool[q])), q) for q in free if pool[q])
+        now, q = min((max(free[q], at), q) for q, at in first.items())
         near = [i for i in pool[q] if ready[i] <= now + COST["look"]]
         if q == "v":
             near = [i for i in near if len(ns[i]) == 1 or free["s"] > max(now, ready[i]) + lean * ns[i]["v"]]
@@ -92,6 +93,10 @@ def issue(ns, after, rank, lean):
         order.append((i, q))
         for k in ns[i]:
             pool[k].discard(i)
+            if pool[k]:
+                first[k] = min(ready[j] for j in pool[k])
+            else:
+                del first[k]
         for j, gap in after[i]:
             ready[j] = max(ready[j], end[i] + gap)
             left[j] -= 1
@@ -101,42 +106,107 @@ def issue(ns, after, rank, lean):
 
 
 def plan(calls):
+    n = len(calls)
     ns = [c["ns"] for c in calls]
     after, before = [[] for _ in calls], [[] for _ in calls]
+    known, need = [], []
+    for c in calls:
+        seen = 0
+        for j in c["dep"]:
+            seen |= known[j]
+        need.append({j: x for j, x in c["dep"].items() if not seen >> j & 1 or calls[j]["lat"] > 100.0})
+        known.append(seen | sum(1 << j for j in c["dep"]))
     for i, c in enumerate(calls):
-        for j, inline in c["dep"].items():
+        for j, inline in need[i].items():
             gap = 0.0 if inline else calls[j]["lat"] + COST["wake"]
             after[j].append((i, gap))
             before[i].append((j, gap))
-    rank = [0.0] * len(calls)
-    for i in range(len(calls) - 1, -1, -1):
+    rank = [0.0] * n
+    for i in range(n - 1, -1, -1):
         rank[i] = min(ns[i].values()) + max([rank[j] + gap for j, gap in after[i]] + [calls[i]["lat"]])
+    paces = []
+    for pace, wake, far, weight in COST["paces"]:
+        paces.append(([pace.get(c["kind"], 1.0) for c in calls], weight,
+                      [[(j, 0.0 if inline else calls[j]["lat"] * far + wake) for j, inline in d.items()] for d in need]))
 
     def length(order):
-        total = 0.0
-        for pace, wake, weight in COST["paces"]:
-            end, free = [0.0] * len(calls), {}
+        total, behind = 0.0, []
+        for pace, weight, deps in paces:
+            end, why, last = [0.0] * n, [None] * n, {}
             for i, q in order:
-                c = calls[i]
-                at = free.get(q, 0.0)
-                for j, inline in c["dep"].items():
-                    at = max(at, end[j] if inline else end[j] + calls[j]["lat"] + wake)
-                free[q] = end[i] = at + c["ns"][q] * pace.get(c["kind"], 1.0)
-            total += max(end) * weight
-        return total
+                k = last.get(q)
+                at = 0.0 if k is None else end[k]
+                for j, gap in deps[i]:
+                    if end[j] + gap > at:
+                        at, k = end[j] + gap, -1 - j
+                why[i], last[q] = k, i
+                end[i] = at + ns[i][q] * pace[i]
+            i = end.index(max(end))
+            total += end[i] * weight
+            while why[i] is not None:
+                if why[i] >= 0:
+                    behind.append((why[i], i))
+                i = why[i] if why[i] >= 0 else -1 - why[i]
+        return total, behind
     best = None
-    luck = np.random.default_rng(0)
+    luck = np.random.default_rng(COST["seed"])
     for turn in range(COST["turns"]):
         lean = COST["lean"][turn % len(COST["lean"])]
         if turn < len(COST["lean"]):
             end = issue(ns, after, rank, lean)[1]
         else:
-            end = [x + float(y) for x, y in zip(best[2], luck.uniform(0.0, COST["shake"][turn % len(COST["shake"])], len(calls)))]
+            end = [x + float(y) for x, y in zip(best[2], luck.uniform(0.0, COST["shake"][turn % len(COST["shake"])], n))]
         now = issue(ns, after, issue(ns, before, end, lean)[1], lean)
         took = length(now[0])
-        if best is None or took < best[0]:
+        if best is None or took[0] < best[0][0]:
             best = (took,) + now
-    return best[1]
+    took, order, end = best
+    way = [None] * n
+    for i, q in order:
+        way[i] = {q: ns[i][q]}
+        rank[i] = ns[i][q] - end[i]
+    for turn in range(COST["mend"]):
+        a, b = took[1][int(luck.integers(len(took[1])))]
+        rank2, way2, how = list(rank), list(way), int(luck.integers(4))
+        if how < 2 and len(ns[(a, b)[how]]) > 1:
+            i = (a, b)[how]
+            way2[i] = {q: x for q, x in ns[i].items() if q not in way[i]}
+        else:
+            i, up = (b, 1.0) if how % 2 else (a, -1.0)
+            rank2[i] = rank[a + b - i] + up * float(luck.choice(COST["shake"]))
+            todo = [i]
+            while todo:
+                i = todo.pop()
+                for j, _ in before[i] if up > 0 else after[i]:
+                    if up * (rank2[i] - rank2[j]) > 0:
+                        rank2[j] = rank2[i] + up
+                        todo.append(j)
+        order2 = issue(way2, after, rank2, 0.0)[0]
+        took2 = length(order2)
+        if took2[0] <= took[0]:
+            took, order, rank, way = took2, order2, rank2, way2
+    for turn in range(COST["swap"]):
+        a, b = took[1][int(luck.integers(len(took[1])))]
+        how = int(luck.integers(4))
+        at = {i: k for k, (i, q) in enumerate(order)}
+        order2 = list(order)
+        if how < 2 and len(ns[(a, b)[how]]) > 1:
+            k = at[(a, b)[how]]
+            order2[k] = (order[k][0], "s" if order[k][1] == "v" else "v")
+        else:
+            part = order[at[a]:at[b] + 1]
+            go = {b if how % 2 else a}
+            for i, q in part[::-1] if how % 2 else part:
+                if i in go:
+                    go.update(j for j, _ in (before[i] if how % 2 else after[i]))
+            if (a if how % 2 else b) in go:
+                continue
+            ahead = [x for x in part if (x[0] in go) == bool(how % 2)]
+            order2[at[a]:at[b] + 1] = ahead + [x for x in part if (x[0] in go) != bool(how % 2)]
+        took2 = length(order2)
+        if took2[0] <= took[0]:
+            took, order = took2, order2
+    return order
 
 
 def rank_program(g, core, T, topo):
@@ -260,6 +330,9 @@ def rank_program(g, core, T, topo):
     def lin(o, a, mul, add):
         ts(o, a, mul, A.mult, add, A.add, lambda: g.scalar.activation(o[0], a[0], F.Identity, bias=add, scale=mul))
 
+    def cols(o, a, mul, add):
+        ts(o, a, mul, A.mult, add, A.add, lambda: g.scalar.activation(o[0], a[0], F.Identity, bias=ap(add), scale=ap(mul)))
+
     def relu(o, a, add, mul=1.0):
         f = lambda: g.scalar.activation(o[0], a[0], F.Relu, bias=add, scale=mul)
         if mul == 1.0:
@@ -306,7 +379,7 @@ def rank_program(g, core, T, topo):
             for o, i in pairs[:-1]:
                 g.sync.dma_start(o, i).then_inc(T.sem[sem], 16)
             return g.sync.dma_start(*pairs[-1])
-        call({"y": (f, 100.0 * len(pairs))}, reads, writes, sem, 16 * len(pairs), COST["dma"] + 1000.0 * len(pairs), True)
+        call({"y": (f, 100.0 * len(pairs))}, reads, writes, sem, 16 * len(pairs), COST["dma"] + 600.0 * len(pairs), True)
 
     def send(dst, ob, ib, rs, ls):
         eng = topo.engines(core, T.cores[dst])[:8]
@@ -340,6 +413,7 @@ def rank_program(g, core, T, topo):
     lone = R("ONEB", 0, 128, 1, 0, 1)
     one = R("ONE")
     half = lambda b, h: R(b, 2048 * h, 2048 * h + 2048)
+    part = lambda b, j: R(b, 1024 * j, 1024 * j + 1024)
     hv = lambda b, h, o=0: R(b, o + 128 * h, o + 128 * h + 128)
     wide = lambda b, lo, w: I(b, lo, lo + w, "SOF", 0, w)
     again = lambda b, lo, k: I(b, lo, lo + 16, "SRP", 0, k)
@@ -350,23 +424,24 @@ def rank_program(g, core, T, topo):
             mm(R(bank, lo + 8 * h, lo + 8 * h + 8), R(em, eo + 128 * h, eo + 128 * h + 128), R("RB"), True, True)
         return R(bank, lo, lo + cols)
 
-    def moved(o, ids, e):
+    def moved(o, ids, e, a=0, z=256):
         none(e, ids)
-        tt(e, R("DUM"), e, A.mult)
+        tt(e, R("DUM", a, z), e, A.mult)
         tt(o, ids, e, A.add)
 
     def spread():
         for j in range(4):
             scan(R("VAL", 1024 * j, 1024 * j + 1024), R("RM", 0, 1024), R("XE2", 1024 * j, 1024 * j + 1024), A.mult, A.add)
 
-    def settle(mv, how):
-        for j in range(0, 4096, 512):
+    def settle(mv, how, a=0, z=4096):
+        for j in range(a, z, 512):
             how(I("OW", 0, NO, mv, j // 16, j // 16 + 32), R("VAL", j, j + 512))
 
     def owners(u):
-        mv = ("MVO", "MV2")[u % 2]
-        moved(R("EQ2"), R("ML", u, 1024, 4), R("B3", 0, 256))
-        tc(R(mv), R("EQ2"))
+        mv = ("MVO", "OFD")[u % 2]
+        for a, z in ((0, 128), (128, 256)) if u == 1 else ((0, 256),):
+            moved(R("EQ2", a, z), R("ML", u + 4 * a, 4 * z, 4), R("B3", a, z), a, z)
+            tc(R(mv, a, z), R("EQ2", a, z))
         if u == 1:
             tc(R("EMA"), R("TB", NE + u, NE + 1024, 4))
             for j in range(4):
@@ -393,7 +468,8 @@ def rank_program(g, core, T, topo):
         tc(R("QM", w, 2 * w), R("QM", 0, w))
     iota(R("SJ", 0, 80), [[1, 80]], 0, 0)
     tc(R("SOF"), R("SJ", 0, 80))
-    dma("dm", [(T.MI[:, :], T.ml[:, :])], [], mi[1])
+    for h in range(2):
+        dma("dm%d" % h, [(T.MI[:, 512 * h:512 * h + 512], T.ml[:, 512 * h:512 * h + 512])], [], R("MI", 512 * h, 512 * h + 512)[1])
     ms(R("X", 0, 16), -16.0)
     ms(R("X", 4096, NX), 0.0)
     ms(R("AC", 0, 8), -1)
@@ -406,22 +482,24 @@ def rank_program(g, core, T, topo):
     ms(R("OW", 0, 528), 128.0)
     for w in (512, 1024, 2048):
         act(R("OW", 16 + w, 16 + 2 * w), R("OW", 16, 16 + w), F.Copy)
-    fill(R("XE"), 0)
-    ms(R("RM"), 1.0)
-    ms(R("RM", 0, 2048, 16), 0.0)
+    fill(R("XE", 0, 512), 0)
+    dma("dz", [(T.XE[:, w:w + 512], T.XE[:, 0:512]) for w in range(512, 4096, 512)], R("XE", 0, 512)[1], R("XE", 512, 4096)[1])
+    ms(R("RM", 0, 256), 1.0)
+    ms(R("RM", 0, 256, 16), 0.0)
+    dma("dr", [(T.RM[:, w:w + 256], T.RM[:, 0:256]) for w in range(256, 1024, 256)], R("RM", 0, 256)[1], R("RM", 256, 1024)[1])
     ms(one, 1.0)
     pl, cj = R("W0", 0, 320), R("W0", 320, 640)
     iota(pl, [[1, 40], [0, 8]], 0, 0)
     iota(cj, [[0, 40], [1, 8]], 0, 0)
-    ts(cj, cj, q_(1), A.mult, 128.0, A.add)
-    ts(pl, pl, q_(0), A.mult)
+    cols(cj, cj, q_(1), 128.0)
+    cols(pl, pl, q_(0), 0.0)
     tt(pl, pl, cj, A.add)
     tt(R("SM", 4, 5), q_(2), q_(3), A.add)
     tt(R("SM", 5, 6), q_(4), q_(5), A.add)
     tt(R("SM", 4, 5), R("SM", 4, 5), R("SM", 5, 6), A.add)
     for u in range(4):
         ts(R("SM", 8 + u, 9 + u), q_(2 + u), R("SM", 4, 5), A.subtract, 128.0, A.mult)
-        ts(R("TB", NE + u, NE + 1280, 4), pl, R("SM", 8 + u, 9 + u), A.add)
+        cols(R("TB", NE + u, NE + 1280, 4), pl, 1.0, R("SM", 8 + u, 9 + u))
     ml = R("ML", 0, 1024)
     for h in range(2):
         a, b = R("MI", 512 * h, 512 * h + 512), R("B%d" % h)
@@ -497,8 +575,7 @@ def rank_program(g, core, T, topo):
     tc(R("SM", 6, 7), R("SJ", 96, 97))
     ts(R("CIW", 0, 64), R("CIW", 0, 64), R("SM", 6, 7), A.add)
     ts(R("CIW", 64, 128), R("CIW", 0, 64), -1.0, A.mult, 1023.0, A.add)
-    fill(R("WQ"), 1)
-    aff(R("WQ"), R("WQ"), [[1, 16], [0, 8], [-1, 16]], A.is_equal, 0.0, 0, 0)
+    aff(R("WQ"), R("XE", 2048, 4096), [[1, 16], [0, 8], [-1, 16]], A.not_equal, 1.0, 0, 0)
     bounded(R("WQ"), [[0, 16], [-16, 8], [0, 16]], 0, 1, 16)
     for k in range(11):
         mark(R("GW", 8, 16), k, float(2 ** (10 - k)))
@@ -512,7 +589,7 @@ def rank_program(g, core, T, topo):
         tt(R("LMB", 4 + a, 5 + a), R("LMF", 1 + a, 2 + a), q_(15), A.mult)
         tt(R("LMB", 2 + a, 3 + a), R("LMF", 1 + a, 2 + a), R("LMB", 4 + a, 5 + a), A.subtract)
     iota(R("K1"), [[-1, 256]], 0, 0)
-    ts(R("CN"), R("K1"), q_(15), A.mult, R("LMF", 5, 6), A.add)
+    cols(R("CN"), R("K1"), q_(15), R("LMF", 5, 6))
     tc(R("SM", 12, 14), R("LMI"))
     for j in range(2):
         ts(R("VM", 128 * j, 128 * j + 128), one, R("SM", 12 + j, 13 + j), A.mult)
@@ -523,18 +600,16 @@ def rank_program(g, core, T, topo):
     fill(R("W1"), 0)
     for u in range(4):
         fill(R("ME%d" % u, 64, 336), 192)
-    cp(R("W2", 512, 768), R("DUM"))
     fill(R("ALT"), 128)
-    fill(R("WP", 512, 768), 128)
     tc(R("LMB", 0, 1), R("WTI"))
     tc(R("LMB", 1, 2), wc)
     ts(R("WT"), R("WQ"), R("LMB", 0, 1), A.mult)
     ts(R("WB"), R("BO"), R("LMB", 0, 1), A.mult)
-    ts(R("WE"), R("WQ"), R("QM", 0, 1), A.mult)
+    aff(R("WE"), R("WQ"), [[0, 16], [-16, 8], [0, 16]], A.is_equal, 0.0, 0, 1)
     ts(R("WQ"), R("WQ"), R("LMB", 1, 2), A.mult)
     (NN, LIVE, LS, LB, SUU, GRL, N16, HAS, FM, DD, T1, T2, T3, OK, SPL, RK, NV, MN, RK2, IDL, VIS, T4, LV, E1, E2, E3) = range(2, 28)
-    AV, BV, TA, TB2, LL = 32, 36, 40, 44, 48
-    EU = 56
+    AV, BV, TA, TB2, LL = 28, 30, 32, 34, 36
+    EU = 41
     for a, c in ((AV, -512), (BV, -256)):
         fill(S(a), c)
 
@@ -569,8 +644,8 @@ def rank_program(g, core, T, topo):
         own = lambda h, b="ML": R(b, t + 512 * h, t + 512 * h + 512, 4)
         xs, ls = R("XS%d" % (t % 2)), 16 * (t % 2)
         tc(R("OFO"), R("ML", t, 1024, 4))
-        for j in range(4):
-            cp(R("TX", 1024 * j, 1024 * j + 1024), I("X", 0, NX, "OFO", 64 * j, 64 * j + 64))
+        for j in range(8):
+            cp(R("TX", 512 * j, 512 * j + 512), I("X", 0, NX, "OFO", 32 * j, 32 * j + 32))
         for h in range(2):
             o = hv("B0", h)
             mm(o, own(h), R("IDF"), True, False)
@@ -593,17 +668,16 @@ def rank_program(g, core, T, topo):
         tc(xs, I("X", 0, NX, "LST", ls, ls + 16))
         ts(R("ACO"), I("AC", 0, NX, "LST", ls, ls + 16), 1, A.add)
         tc(R("XE", 0, 4096, 16), xs)
-        for h in range(2):
-            scan(half("XSE", h), R("RM"), half("XE", h), A.mult, A.add)
+        for j in range(4):
+            scan(part("XSE", j), R("RM"), part("XE", j), A.mult, A.add)
         ts(R("SI", 32, 48), R("SI", 0, 16), 16, A.logical_shift_right)
-        for h in range(2):
-            scan(half("US", h), R("RM"), half("TX", h), A.mult, A.max)
+        for j in range(4):
+            scan(part("US", j), R("RM"), part("TX", j), A.mult, A.max)
         aside(R("UC"), R("US", 15, 4096, 16))
         for h in range(2):
             mm(R("B2", 16 + 8 * h, 24 + 8 * h), hv("UC", h), g8, True, True)
         tt(S(GRL), R("B2", 16, 32), R("SI", 32, 48), A.subtract)
         tt(S(GRL), S(GRL), R("LIM", 16, 32), A.is_gt)
-        tt(S(GRL), S(GRL), S(LIVE), A.mult)
         for kk in range(8):
             squares(xs, ("B4", "B5")[kk % 2], kk)
         for h in range(2):
@@ -626,12 +700,16 @@ def rank_program(g, core, T, topo):
             for h in range(2):
                 mm(R("B6", 128 * h + k, 128 * h + 128, 16), R("SQ", 256 * k + 128 * h, 256 * k + 128 * h + 128), R("G16"), False, k == 15 and h == 1)
         tt(R("MM", 256, 512), R("KBC"), R("B6", 0, 256), A.is_gt)
-        ts(R("MM", 0, 256), R("MM", 256, 512), -1.0, A.mult, 1.0, A.add)
+        lin(R("MM", 0, 256), R("MM", 256, 512), -1.0, 1.0)
         mm(R("B6", 256, 512), R("ID4"), R("MM", 256, 512), True, False)
         for h in range(2):
             mm(hv("B6", h, 256), own(h), R("IXS"), False, h == 1)
         zi = R("ZI", 0, 256)
         scan(R("TH2"), R("RM", 0, 256), R("MM", 0, 256), A.mult, A.add)
+        if t == 0:
+            ts(S(SUU), R("TH2", 15, 256, 16), 15.0, A.min, -15.0, A.add)
+            tt(S(SUU), S(SUU), C(1), A.add)
+            tc(R("LST", 176, 192), wrap(SUU, 16, "EMA", 0, "B2", 224))
         tt(R("B4", 0, 256), R("MM", 256, 512), R("KC"), A.mult)
         tt(R("TH2"), R("TH2"), R("B4", 0, 256), A.add)
         ts(zi, R("TH2"), -1.0, A.add, 4369.0, A.mult)
@@ -648,12 +726,18 @@ def rank_program(g, core, T, topo):
         relu(R("LR"), p, -8192.0)
         mm(R("B4", 256, 512), R("JR"), R("LR"), True, True)
         cp(R("W1", 256, 512), R("B4", 256, 512))
-        ts(R("KBC"), p, 8192.0, A.is_lt)
+        none(R("KBC"), R("LR"))
         tt(R("W0", 256, 512), R("KBC"), p, A.mult)
-        if t < 3:
+        if t == 0:
+            tt(R("W2", 256, 512), R("W0", 256, 512), R("LR"), A.add)
+            aside(R("W2", 512, 768), R("ML", t, 1024, 4))
+            aside(R("WP", 512, 768), R("TB", NE + t, NE + 1024, 4))
+        elif t < 3:
             moved(R("W2", 256, 512), R("LR"), R("B6", 0, 256))
         aside(R("W0", 512, 768), R("ML", t, 1024, 4))
         aside(R("WP", 0, 256), R("TB", NE + t, NE + 1024, 4))
+        if t:
+            aside(R("PCF"), R("TB", NE + t, NE + 1024, 4))
 
     empties()
     members(0)
@@ -661,19 +745,17 @@ def rank_program(g, core, T, topo):
         own = lambda h, b="ML": R(b, t + 512 * h, t + 512 * h + 512, 4)
         xs, ls = R("XS%d" % (t % 2)), 16 * (t % 2)
         la = 128 + 16 * (t % 2)
-        for j in range(4):
-            cp(R("OWG", 1024 * j, 1024 * j + 1024), I("OW", 0, NO, "ACO", 64 * j, 64 * j + 64))
-        for j in range(4):
-            xa = R("XA", 1024 * j, 1024 * j + 1024)
-            tt(xa, I("X", 0, NX, "ACO", 64 * j, 64 * j + 64), R("XSE", 1024 * j, 1024 * j + 1024), A.subtract)
+        for j in range(8):
+            cp(R("OWG", 512 * j, 512 * j + 512), I("OW", 0, NO, "ACO", 32 * j, 32 * j + 32))
+        for j in range(8):
+            xa = R("XA", 512 * j, 512 * j + 512)
+            tt(xa, I("X", 0, NX, "ACO", 32 * j, 32 * j + 32), R("XSE", 512 * j, 512 * j + 512), A.subtract)
             act(xa, xa, F.Square)
         mm(R("B1"), lone, row(640, 512), True, False)
         for b, w in (("OWG", R("GC", 16 * t, 16 * t + 16)), ("XA", R("G512"))):
             for h in range(2):
                 for k in range(16):
                     mm(R("B1", 256 * h + k, 256 * h + 256, 16), R(b, 2048 * h + k, 2048 * h + 2048, 16), w, False, b == "XA" and h == 1 and k == 15)
-        if t == 0:
-            owners(0)
         scan(R("KD"), R("BM"), R("B1"), A.max, A.min)
         sk, sl = R3("SK", 0, 2, 0, 16), R3("SL", 0, 2, 0, 16)
         tc(sk, R("KD", 15, 512, 16))
@@ -685,8 +767,8 @@ def rank_program(g, core, T, topo):
         ts(R("LST", 48, 64), wrap(DD, 16, "EMB", 0, "B2", 32), 1024.0, A.min)
         tc(R("MD"), I("ML", 0, 1280, "LST", 48, 64))
         tc(R("OFD"), R("MD"))
-        for j in range(4):
-            cp(R("TD", 1024 * j, 1024 * j + 1024), I("X", 0, NX, "OFD", 64 * j, 64 * j + 64))
+        for j in range(8):
+            cp(R("TD", 512 * j, 512 * j + 512), I("X", 0, NX, "OFD", 32 * j, 32 * j + 32))
         sign(R("INDD"), R("MD"))
         ts(S(HAS), S(DD), 1024.0, A.is_lt)
         tt(S(AV + 1), S(DD), C(3), A.subtract)
@@ -716,7 +798,9 @@ def rank_program(g, core, T, topo):
             mm(p, R("IDF"), w, True, False)
             mm(p, hv("SH", j), R("MA"), False, True)
         tt(R("W0", 0, 256), R("W0", 512, 768), p, A.add)
-        if t < 3:
+        if t == 0:
+            tt(R("W2", 0, 256), R("W0", 512, 768), p, A.add)
+        elif t < 3:
             moved(R("W2", 0, 256), R("MD"), R("B2", 256, 512))
         for h in range(2):
             mm(R("B2", 48 + 8 * h, 56 + 8 * h), hv("INDD", h), g8, True, False)
@@ -729,7 +813,8 @@ def rank_program(g, core, T, topo):
         act(R("KA"), R("B1", 0, 256), F.Abs)
         for h in range(2):
             tc(R("TD", 2048 * h + 15, 2048 * h + 2048, 16), hv("UC", h))
-            scan(half("UD", h), R("RM"), half("TD", h), A.mult, A.max)
+            for j in (2 * h, 2 * h + 1):
+                scan(part("UD", j), R("RM"), part("TD", j), A.mult, A.max)
             mm(R("B2", 64 + 8 * h, 72 + 8 * h), R("UD", 2048 * h + 15, 2048 * h + 2048, 16), g8, True, True)
         scan(R("MSD"), R("BM", 0, 256), R("KA"), A.max, A.min)
         tt(S(T3), R("SI", 32, 48), R("MSD", 14, 256, 16), A.min)
@@ -770,19 +855,38 @@ def rank_program(g, core, T, topo):
         tc(R("ML", t, 1024, 4), I("W0", 0, 768, "LST", 160, 176))
         tc(R("L2"), I("W1", 0, 768, "LST", 160, 176))
         tc(I("ML", 0, 1280, "LST", 224, 240), R("L2"))
-        tc(R("XE2", 0, 4096, 16), I("WP", 0, 768, "LST", 160, 176))
-        aside(R("ALT", t, 1024, 4), R("XE2", 0, 4096, 16))
-        tc(I("ALT", 0, 1280, "LST", 224, 240), R("WP", 0, 256))
+        early = t > 0
+        if early:
+            tc(R("XE2", 0, 4096, 16), I("WP", 0, 768, "LST", 160, 176))
+            aside(R("ALT", t, 1024, 4), R("XE2", 0, 4096, 16))
+            put(I("ALT", 0, 1280, "LST", 224, 240), R("PCF"))
+        else:
+            tc(R("XE2", 0, 4096, 16), R("WP", 0, 256))
+            tt(R("VM"), I("WP", 0, 768, "LST", 160, 176), R("XE2", 0, 4096, 16), A.subtract)
+            tc(I("XE2", 0, 4096, "LST", 176, 192), R("VM"))
         xv = "XV%d" % t
         tc(R("SJ", 0, 4), numbers("B1", 128, xv, 4, "WT"))
-        mm(R("B1", 192, 256), R("WB"), R(xv), True, True)
+        if early:
+            mm(R("B1", 192, 256), R("WB"), R(xv), True, True)
         ts(R("SJ", 0, 4), R("SJ", 0, 4), 4095, A.bitwise_and)
         ts(R("LST", 240, 244), R("SJ", 0, 4), 1, A.add)
-        tc(R("OVG"), I("OW", 0, NO, "LST", 240, 244))
+        if t == 3:
+            tc(R("OVG"), I("OW", 0, NO, "LST", 240, 244))
         if t < 3:
-            tc(R("MVO"), I("W2", 0, 768, "LST", 160, 176))
+            if early:
+                tc(R("MVO"), I("W2", 0, 768, "LST", 160, 176))
+            else:
+                tc(R("EQ2"), I("W2", 0, 768, "LST", 160, 176))
+                moved(R("EQ2"), R("EQ2"), R("B6", 0, 256))
+                tc(R("MVO"), R("EQ2"))
+                aside(R("W2", 512, 768), R("DUM"))
             spread()
-            settle("MVO", lambda o, i: act(o, i, F.Silu))
+            if not early:
+                tc(I("XE2", 0, 4096, "LST", 176, 192), R("W1", 0, 256))
+            at = 512 if early else 4096
+            settle("MVO", lambda o, i: act(o, i, F.Silu), 0, at)
+            tc(R("OVG"), I("OW", 0, NO, "LST", 240, 244))
+            settle("MVO", lambda o, i: act(o, i, F.Silu), at, 4096)
             mm(R("B2", 208, 224), R("ONEB"), mer, True, True)
             addup(S(E2, 1), R("B2", 208, 224))
             tc(R("SI", 96, 97), S(E2, 1))
@@ -801,22 +905,26 @@ def rank_program(g, core, T, topo):
                 lin(y, a, 1.0, -1.0)
                 tt(y, y, b, A.add)
             dma("oy", [(T.ym[:, :], ym[0])], ym[1], [])
-        tc(R("SJ", 64, 128), R("B1", 192, 256))
-        ts(R("SJ", 64, 128), R("SJ", 64, 128), 4095, A.bitwise_and)
-        ts(R("VF"), R("SJ", 64, 128), 1, A.add)
+        if early:
+            tc(R("SJ", 64, 128), R("B1", 192, 256))
+            ts(R("SJ", 64, 128), R("SJ", 64, 128), 4095, A.bitwise_and)
+            ts(R("VF"), R("SJ", 64, 128), 1, A.add)
         aside(R("XVS", 0, 1024, 16), R(xv))
         scan(R("XVE"), R("RM", 0, 1024), R("XVS"), A.mult, A.add)
         tc(R("LST", 244, 248), numbers("B1", 132, "OVG", 4))
-        tc(R("AVG"), I("ALT", 0, 1280, "LST", 244, 248))
-        tc(R("HL1"), I("ML", 0, 1280, "LST", 244, 248))
-        tc(R("LST", 248, 252), numbers("B1", 136, "AVG", 4))
-        tt(R("EQV"), R("HL1"), R("VF"), A.is_equal)
-        mm(R("B1", 256, 320), R("BO"), R("EQV"), True, True)
-        tc(R("HL2"), I("ML", 0, 1280, "LST", 248, 252))
-        tt(R("HL1"), R("HL1"), R("HL2"), A.subtract)
-        tt(R("HL1"), R("HL1"), R("B1", 256, 320), A.mult)
-        tt(R("HL1"), R("HL1"), R("HL2"), A.add)
-        tc(R("HL"), R("HL1"))
+        if early:
+            tc(R("AVG"), I("ALT", 0, 1280, "LST", 244, 248))
+            tc(R("HL1"), I("ML", 0, 1280, "LST", 244, 248))
+            tc(R("LST", 248, 252), numbers("B1", 136, "AVG", 4))
+            tt(R("EQV"), R("HL1"), R("VF"), A.is_equal)
+            mm(R("B1", 256, 320), R("BO"), R("EQV"), True, True)
+            tc(R("HL2"), I("ML", 0, 1280, "LST", 248, 252))
+            tt(R("HL1"), R("HL1"), R("HL2"), A.subtract)
+            tt(R("HL1"), R("HL1"), R("B1", 256, 320), A.mult)
+            tt(R("HL1"), R("HL1"), R("HL2"), A.add)
+            tc(R("HL"), R("HL1"))
+        else:
+            tc(R("HL"), I("ML", 0, 1280, "LST", 244, 248))
         for h in range(2):
             vd = R("VD", 512 * h, 512 * h + 512)
             tt(vd, I("X", 0, NX, "HL", 32 * h, 32 * h + 32), R("XVE", 512 * h, 512 * h + 512), A.subtract)
@@ -833,7 +941,7 @@ def rank_program(g, core, T, topo):
         tc(R("LST", 252, 256), R("B1", 140, 144))
         ts(R("RET"), I("VD", 0, 1024, "LST", 252, 256), 0.5, A.mult, 191.75, A.add)
         send(src, "ME%d" % t, "RET", "ra%d" % t, "rl%d" % t)
-        ts(R("NX0"), xs, -192.0, A.add)
+        lin(R("NX0"), xs, 1.0, -192.0)
         tt(R("NX1"), I("ME%d" % t, 0, 336, "LST", la, la + 16), R("NX0"), A.add)
         tc(I("X", 0, NX, "LST", ls, ls + 16), R("NX1"))
     dma("ox", [(T.yx[:, :], T.X[:, 1:4097])], R("X", 1, 4097)[1], [])
@@ -866,7 +974,7 @@ def rank_program(g, core, T, topo):
         ck = dict(known[q])
         ck[e] = count[e]
         seen[i] = (e, count[e], ck)
-    for k in SEMAPHORES[:17]:
+    for k in SEMAPHORES[:18]:
         g.sync.wait_ge(T.sem[k], count[k])
     for t in range(4):
         for k in ("vl", "rl"):

import numpy as np
from concourse.mybir import AluOpType as A, ActivationFunctionType as F, AxisListType
AX = AxisListType.X

NX = 4368
NO = 8576
NE = 1024
D0 = 4352


def _sb(spec):
    d = {}
    for dtype, names in spec.items():
        for x in names.split():
            k, w = x.split(":")
            d[k] = ("sbuf", [128] + [int(v) for v in w.split("x")], dtype)
    return d


SCRATCH = _sb({
    "bfloat16": "X:4368 TX:4096 XE:4096 SQ:4096 XSE:4096 XA:4096 OWG:4096 RM:1024 QM:256 BM:512 ROW:1472 WQ:2048 WT:2048 "
                "WE:2048 WP:768 IND:1024 CF:768 MM:512 TH2:256 KC:256 VS:336 XVE:1024 XVS:1024 VD:1024 RET:64",
    "float32": "OW:8576 TB:2304 ML:1280 VAL:4096 KD:512 EMW:768 SM:784 W:16x16 WW:16x16 SH:512 ALT:1280 PCF:256 MVA:128 W0:768 W1:768 W2:768",
    "int32": "AC:4368 MI:1024 CT:1040 LMI:2 WTI:1 SJ:128 SK:2x16 SL:2x16",
    "uint16": "OFO:256 ACO:256 OFD:256 MVO:256 LST:256 HL:64 SOF:80 SRP:4"})
WIDTH = {k: v[1][1] * (v[1][2] if len(v[1]) > 2 else 1) for k, v in SCRATCH.items()}
PLACE = {k: (k, 0) for k in SCRATCH}
for _pool, _dt, _names in (
        ("PB", "bfloat16", "ONEB:128 IDB:128 NID:128 IDV:128 BO:128 G16:8 G1K:8 G512:16 G64:8 GS0:8 GC:64 WB:128 TRI:128 TSB:128 ID4:128 BW:512 XS0:256 XS1:256 "
                           "LMB:8 SB:64 OCB:64 NVB:8 CN:256 XB:256 UC:256 VM:256 INDD:256 NX0:256 NX1:256 OVG:64 AVG:64 EQV:64"),
        ("PF", "float32", "QF:16 ONE:128 IDF:128 IDK:128 IXS:128 JR:128 LR:256 RB:8 DUM:256 CO:128 BAS:32 CIW:128 LMF:8 LIM:64 K1:256 KM:256 KBC:256 KV:128 "
                          "EMA:256 EMB:256 EMV:128 EQ2:256 MD:256 MA:256 MW:256 GW:16 HL1:64 HL2:64 VF:64")):
    _at = 0
    for _x in _names.split():
        _k, _w = _x.split(":")
        PLACE[_k], WIDTH[_k] = (_pool, _at), int(_w)
        _at += -(-int(_w) // 16) * 16
    SCRATCH[_pool] = ("sbuf", [128, _at], _dt)
for _t in range(4):
    for _k, _w in (("XV%d" % _t, 64), ("ME%d" % _t, 336)):
        SCRATCH[_k] = ("sbuf", [128, _w], "bfloat16")
        PLACE[_k], WIDTH[_k] = (_k, 0), _w
for _b in range(8):
    SCRATCH["B%d" % _b] = ("psum", [128, 512], "float32")
    PLACE["B%d" % _b], WIDTH["B%d" % _b] = ("B%d" % _b, 0), 512
for _k, _v, _at, _w in (("US", "OWG", 0, 4096), ("UD", "OWG", 0, 4096), ("TD", "XA", 0, 4096), ("XE2", "XE", 0, 4096),
                        ("YM", "VAL", 0, 1024), ("FS", "KD", 0, 512), ("SQV", "XVE", 0, 1024), ("KA", "K1", 0, 256), ("MSD", "KM", 0, 256),
                        ("KB", "KM", 0, 256), ("L2", "MD", 0, 256), ("ZI", "MI", 0, 512), ("ZC", "MI", 512, 256), ("SI", "MI", 768, 256),
                        ("TG", "WP", 256, 256)):
    PLACE[_k], WIDTH[_k] = (PLACE[_v][0], PLACE[_v][1] + _at), _w
SEMAPHORES = ["v", "s", "p", "gg", "dx", "da", "dm0", "dm1", "dl", "dw", "dz", "dr", "oy", "ox"] + ["dp%d" % j for j in range(4)] + ["%s%d" % (a, b) for a in ("va", "vl", "ra", "rl") for b in range(4)]
PSUM = ["B%d" % b for b in range(8)]
SIZE = {"float32": 4, "int32": 4, "bfloat16": 2, "uint16": 2}
COST = {"cy": 0.9, "gat": 1.5, "sca": 3.0, "pe": 0.65, "wake": 150.0, "far": 3000.0, "dma": 3000.0, "look": 200.0, "turns": 100,
        "shake": (100.0, 300.0, 1000.0, 300.0), "seed": 1, "mend": 3000, "swap": 8000, "short": 256, "lean": (0.0, 0.15, 0.3, 0.45, 0.6),
        "paces": (({"p": 0.7}, 100.0, 1.0, 1.0), ({"gat": 0.8, "sca": 0.75}, 150.0, 1.3, 1.0), ({"gat": 1.25, "sca": 1.65}, 120.0, 0.8, 0.77))}
PLAN = {}


def issue(ns, after, rank, lean):
    n = len(ns)
    left = [0] * n
    for a in after:
        for j, _ in a:
            left[j] += 1
    ready, end = [0.0] * n, [0.0] * n
    free = {q: 0.0 for q in ("v", "s", "p", "gg", "y", "x")}
    pool = {q: set() for q in free}
    first = {}
    order = []

    def enter(i):
        for q in ns[i]:
            pool[q].add(i)
            first[q] = min(first.get(q, 1e18), ready[i])
    for i in range(n):
        if not left[i]:
            enter(i)
    while len(order) < n:
        now, q = min((max(free[q], at), q) for q, at in first.items())
        near = [i for i in pool[q] if ready[i] <= now + COST["look"]]
        if q == "v":
            near = [i for i in near if len(ns[i]) == 1 or free["s"] > max(now, ready[i]) + lean * ns[i]["v"]]
            if not near:
                free[q] = now + 100.0
                continue
        i = max(near, key=lambda i: (rank[i], -i))
        if ready[i] > now:
            fit = [j for j in near if max(now, ready[j]) + ns[j][q] <= ready[i]]
            if fit:
                i = max(fit, key=lambda i: (rank[i], -i))
        free[q] = end[i] = max(now, ready[i]) + ns[i][q]
        order.append((i, q))
        for k in ns[i]:
            pool[k].discard(i)
            if pool[k]:
                first[k] = min(ready[j] for j in pool[k])
            else:
                del first[k]
        for j, gap in after[i]:
            ready[j] = max(ready[j], end[i] + gap)
            left[j] -= 1
            if not left[j]:
                enter(j)
    return order, end


def plan(calls):
    n = len(calls)
    ns = [c["ns"] for c in calls]
    after, before = [[] for _ in calls], [[] for _ in calls]
    known, need = [], []
    for c in calls:
        seen = 0
        for j in c["dep"]:
            seen |= known[j]
        need.append({j: x for j, x in c["dep"].items() if not seen >> j & 1 or calls[j]["lat"] > 100.0})
        known.append(seen | sum(1 << j for j in c["dep"]))
    for i, c in enumerate(calls):
        for j, inline in need[i].items():
            gap = 0.0 if inline else calls[j]["lat"] + COST["wake"]
            after[j].append((i, gap))
            before[i].append((j, gap))
    rank = [0.0] * n
    for i in range(n - 1, -1, -1):
        rank[i] = min(ns[i].values()) + max([rank[j] + gap for j, gap in after[i]] + [calls[i]["lat"]])
    paces = []
    for pace, wake, far, weight in COST["paces"]:
        paces.append(([pace.get(c["kind"], 1.0) for c in calls], weight,
                      [[(j, 0.0 if inline else calls[j]["lat"] * far + wake) for j, inline in d.items()] for d in need]))

    def length(order):
        total, behind = 0.0, []
        for pace, weight, deps in paces:
            end, why, last = [0.0] * n, [None] * n, {}
            for i, q in order:
                k = last.get(q)
                at = 0.0 if k is None else end[k]
                for j, gap in deps[i]:
                    if end[j] + gap > at:
                        at, k = end[j] + gap, -1 - j
                why[i], last[q] = k, i
                end[i] = at + ns[i][q] * pace[i]
            i = end.index(max(end))
            total += end[i] * weight
            while why[i] is not None:
                if why[i] >= 0:
                    behind.append((why[i], i))
                i = why[i] if why[i] >= 0 else -1 - why[i]
        return total, behind
    best = None
    luck = np.random.default_rng(COST["seed"])
    for turn in range(COST["turns"]):
        lean = COST["lean"][turn % len(COST["lean"])]
        if turn < len(COST["lean"]):
            end = issue(ns, after, rank, lean)[1]
        else:
            end = [x + float(y) for x, y in zip(best[2], luck.uniform(0.0, COST["shake"][turn % len(COST["shake"])], n))]
        now = issue(ns, after, issue(ns, before, end, lean)[1], lean)
        took = length(now[0])
        if best is None or took[0] < best[0][0]:
            best = (took,) + now
    took, order, end = best
    way = [None] * n
    for i, q in order:
        way[i] = {q: ns[i][q]}
        rank[i] = ns[i][q] - end[i]
    for turn in range(COST["mend"]):
        a, b = took[1][int(luck.integers(len(took[1])))]
        rank2, way2, how = list(rank), list(way), int(luck.integers(4))
        if how < 2 and len(ns[(a, b)[how]]) > 1:
            i = (a, b)[how]
            way2[i] = {q: x for q, x in ns[i].items() if q not in way[i]}
        else:
            i, up = (b, 1.0) if how % 2 else (a, -1.0)
            rank2[i] = rank[a + b - i] + up * float(luck.choice(COST["shake"]))
            todo = [i]
            while todo:
                i = todo.pop()
                for j, _ in before[i] if up > 0 else after[i]:
                    if up * (rank2[i] - rank2[j]) > 0:
                        rank2[j] = rank2[i] + up
                        todo.append(j)
        order2 = issue(way2, after, rank2, 0.0)[0]
        took2 = length(order2)
        if took2[0] <= took[0]:
            took, order, rank, way = took2, order2, rank2, way2
    for turn in range(COST["swap"]):
        a, b = took[1][int(luck.integers(len(took[1])))]
        how = int(luck.integers(4))
        at = {i: k for k, (i, q) in enumerate(order)}
        order2 = list(order)
        if how < 2 and len(ns[(a, b)[how]]) > 1:
            k = at[(a, b)[how]]
            order2[k] = (order[k][0], "s" if order[k][1] == "v" else "v")
        else:
            part = order[at[a]:at[b] + 1]
            go = {b if how % 2 else a}
            for i, q in part[::-1] if how % 2 else part:
                if i in go:
                    go.update(j for j, _ in (before[i] if how % 2 else after[i]))
            if (a if how % 2 else b) in go:
                continue
            ahead = [x for x in part if (x[0] in go) == bool(how % 2)]
            order2[at[a]:at[b] + 1] = ahead + [x for x in part if (x[0] in go) != bool(how % 2)]
        took2 = length(order2)
        if took2[0] <= took[0]:
            took, order = took2, order2
    return order


def rank_program(g, core, T, topo):
    rank = T.rank_of(core)
    if rank is None:
        return
    n = len(T.cores)
    queue = {"v": g.vector, "s": g.scalar, "p": g.tensor, "gg": g, "y": g.sync}
    calls = []
    log = {}
    turn = {}

    def R(b, lo=0, hi=None, st=1, p0=0, p1=128):
        hi = WIDTH[b] if hi is None else min(hi, WIDTH[b])
        b, at = PLACE[b]
        lo, hi = lo + at, hi + at
        full = p0 == 0 and p1 == 128
        ap = T[b][:, lo:hi:st] if full else T[b][p0:p1, lo:hi:st]
        return (ap, [(b, lo, hi, st)], -(-(hi - lo) // st))

    def R3(b, a0, a1, k0, k1, st=1):
        s = SCRATCH[b][1][2]
        return (T[b][:, a0:a1, k0:k1:st], [(b, a0 * s, a1 * s, 1)], (a1 - a0) * -(-(k1 - k0) // st))

    def I(b, lo, hi, ob, o0, o1):
        b, at = PLACE[b]
        lo, hi = lo + at, hi + at
        return (T[b][:, lo:hi].indirect(T[ob][:, o0:o1]), [(b, lo, hi, 1), (ob, o0, o1, 1)], 16 * (o1 - o0))

    def call(ways, reads, writes, sem=None, inc=1, lat=0.0, dma=False, fence=False, more=(), kind=None):
        me = len(calls)
        q = list(ways)[0] if len(ways) == 1 else None
        dep = {j: False for j in more}
        for b in set(x[0] for x in reads + writes if x[0] in PSUM):
            holder, before, now = turn.get(b, (None, [], []))
            if q is None or q != holder:
                before, now = now, []
                log[b] = []
            if q == "p" and now:
                dep[now[-1]] = not fence
                now = []
            else:
                dep.update({j: False for j in before})
            turn[b] = (q, before, now + [me])
        for regs, w in ((reads, False), (writes, True)):
            for (b, lo, hi, st) in regs:
                if q == "p" and b in PSUM:
                    continue
                if dma and w:
                    al = 16 // SIZE[SCRATCH[b][2]]
                    lo, hi, st = lo // al * al, -(-hi // al) * al, 1
                for (l2, h2, s2, w2, e, j, d2) in log.get(b, []):
                    if not (w or w2):
                        continue
                    if d2 and w2 and w:
                        al = 16 // SIZE[SCRATCH[b][2]]
                        l2, h2, s2 = l2 // al * al, -(-h2 // al) * al, 1
                    if lo >= h2 or l2 >= hi or (st == s2 and st > 1 and (lo - l2) % st):
                        continue
                    dep[j] = False
        calls.append({"f": {k: v[0] for k, v in ways.items()}, "ns": {k: v[1] for k, v in ways.items()}, "dep": dep, "sem": sem,
                      "kind": q if kind is None else kind, "inc": inc, "lat": lat})
        for (b, lo, hi, st) in writes:
            keep = [r for r in log.get(b, []) if not (st == 1 and lo <= r[0] and r[1] <= hi)]
            log[b] = keep + [(lo, hi, st, True, q, me, dma)]
        for (b, lo, hi, st) in reads:
            log.setdefault(b, []).append((lo, hi, st, False, q, me, dma))
        return me

    def sides(out, ins):
        rd = [x for i in ins if isinstance(i, tuple) for x in i[1]]
        return rd + out[1][1:], out[1][:1]

    def ns(q, out, ins, two=False):
        m = out[2]
        if len(out[1]) > 1:
            return 60 + m * COST["sca"] * COST["cy"]
        if ins and len(ins[0][1]) > 1:
            return 60 + m * COST["gat"] * COST["cy"]
        bufs = [x[1][0][0] for x in [out] + ins if isinstance(x, tuple)]
        if two:
            m *= 1 if any(b in PSUM for b in bufs[1:]) else 2
        elif q == "v" and all(SIZE[SCRATCH[b][2]] == 2 for b in bufs):
            m *= 0.5
        if q == "v" and not two and len(ins) == 1 and ins[0][2] > m * 2:
            m = ins[0][2]
        return 20 + max(m, 64) * COST["cy"]

    def sort(out, ins):
        return "sca" if len(out[1]) > 1 else "gat" if ins and len(ins[0][1]) > 1 else ""

    def vop(f, out, ins, two=False, other=None):
        rd, wr = sides(out, ins)
        ways = {"v": (f, ns("v", out, ins, two))}
        if other is not None:
            ways["s"] = (other, ns("s", out, ins))
        call(ways, rd, wr, kind=sort(out, ins))

    def ap(x):
        return x[0] if isinstance(x, tuple) else x

    def tc(o, i):
        floats = len(o[1]) == 1 and all(SCRATCH[x[1][0][0]][2] in ("float32", "bfloat16") for x in (o, i))
        short = len(i[1]) == 1 and o[2] > COST["short"] and SIZE[SCRATCH[o[1][0][0]][2]] + SIZE[SCRATCH[i[1][0][0]][2]] == 4
        other = (lambda: g.scalar.activation(o[0], i[0], F.Copy)) if floats and not short else None
        vop(lambda: g.vector.tensor_copy(o[0], i[0]), o, [i], other=other)
    cp = tc

    def put(o, i):
        vop(lambda: g.vector.tensor_copy(o[0], i[0]), o, [i], other=lambda: g.scalar.activation(o[0], i[0], F.Silu))

    def tt(o, a, b, f):
        vop(lambda: g.vector.tensor_tensor(o[0], a[0], b[0], f), o, [a, b], True)

    def ts(o, a, s1, f1, s2=None, f2=None, other=None):
        if f2 is None:
            vop(lambda: g.vector.tensor_scalar(o[0], a[0], ap(s1), None, f1), o, [a, s1], other=other)
        else:
            vop(lambda: g.vector.tensor_scalar(o[0], a[0], ap(s1), ap(s2), f1, f2), o, [a, s1, s2], other=other)

    def lin(o, a, mul, add):
        ts(o, a, mul, A.mult, add, A.add, lambda: g.scalar.activation(o[0], a[0], F.Identity, bias=add, scale=mul))

    def cols(o, a, mul, add):
        ts(o, a, mul, A.mult, add, A.add, lambda: g.scalar.activation(o[0], a[0], F.Identity, bias=ap(add), scale=ap(mul)))

    def relu(o, a, add, mul=1.0):
        f = lambda: g.scalar.activation(o[0], a[0], F.Relu, bias=add, scale=mul)
        if mul == 1.0:
            ts(o, a, add, A.add, 0.0, A.max, f)
        else:
            call({"s": (f, ns("s", o, [a]))}, a[1], o[1])

    def sign(o, a):
        ts(o, a, 0.0, A.is_gt, other=lambda: g.scalar.activation(o[0], a[0], F.Sign))

    def none(o, a):
        ts(o, a, 0.0, A.is_equal, other=lambda: g.scalar.activation(o[0], a[0], F.Relu, bias=1.0, scale=-1.0))

    def ms(o, c):
        vop(lambda: g.vector.memset(o[0], c), o, [])

    def scan(o, d0, d1, f0, f1):
        vop(lambda: g.vector.tensor_tensor_scan(o[0], d0[0], d1[0], 0.0, f0, f1), o, [d0, d1])

    def addup(o, i):
        vop(lambda: g.vector.tensor_reduce(o[0], i[0], AX, A.add), o, [i])

    def act(o, i, f):
        rd, wr = sides(o, [i])
        call({"s": (lambda: g.scalar.activation(o[0], i[0], f), ns("s", o, [i]))}, rd, wr, kind=sort(o, [i]))

    def over(acc, i, bias, o):
        call({"s": (lambda: g.scalar.activation(o[0], i[0], F.Relu, bias=bias[0], accum_out=acc[0]), 20 + ns("s", o, [i]))},
             i[1] + bias[1], o[1] + acc[1])

    def mm(o, l, r, a, z, fence=False):
        t = max(min(64, l[2]), r[2]) * (4 if SIZE[SCRATCH[l[1][0][0]][2]] == 4 else 1) * COST["pe"]
        call({"p": (lambda: g.tensor.matmul(o[0], l[0], r[0], a, z), t)}, l[1] + r[1], o[1], lat=100.0, fence=fence)

    def aff(o, i, pat, cmp, fill, base, cm):
        call({"gg": (lambda: g.affine_select(o[0], i[0], pat, cmp, fill, base, cm), 170 + 2 * o[2] * COST["cy"])}, i[1], o[1])

    def iota(o, pat, base, cm):
        fl = SCRATCH[o[1][0][0]][2] != "int32"
        call({"gg": (lambda: g.iota(o[0], pat, base, cm, allow_small_or_imprecise_dtypes=fl), 130 + 2 * o[2] * COST["cy"])}, [], o[1])

    def dma(sem, pairs, reads, writes):
        def f():
            for o, i in pairs[:-1]:
                g.sync.dma_start(o, i).then_inc(T.sem[sem], 16)
            return g.sync.dma_start(*pairs[-1])
        call({"y": (f, 100.0 * len(pairs))}, reads, writes, sem, 16 * len(pairs), COST["dma"] + 600.0 * len(pairs), True)

    def send(dst, ob, ib, rs, ls):
        eng = topo.engines(core, T.cores[dst])[:8]
        mask = sum(1 << e for e in eng)
        rid, pid, _se = topo.addr(T.cores[dst])
        i = R(ib, 0, 64)
        me = call({"gg": (lambda: g.remote_dma(T[ob][:, 0:64], i[0], T.sem[rs], T.sem[ls], pid, rid, mask), 100.0)}, i[1], [], ls, -len(eng), COST["far"])
        call({"x": (None, 0.0)}, [], R(ob, 0, 64)[1], rs, -len(eng), 0.0, True, more=[me])

    def fill(o, c):
        iota(o, [[0, o[2]]], c, 0)

    def diag(o, zero, c):
        aff(o, zero, [[-1, 128]], A.not_equal, c, 0, 1)

    def mark(o, k, c):
        aff(o, o, [[-16, 8]], A.not_equal, c, -k, 1)

    def aside(o, i):
        aff(o, i, [[0, o[2]]], A.is_ge, 0.0, 0, 0)

    def bounded(o, pat, base, cm, width):
        aff(o, o, pat, A.is_ge, 0.0, base, cm)
        aff(o, o, [[-s, k] for s, k in pat], A.is_ge, 0.0, width - 1 - base, -cm)

    q_ = lambda k: R("QF", k, k + 1)
    C = lambda a: R("CO", 16 * a, 16 * a + 16)
    S = lambda a, w=16: R("SM", 16 * a, 16 * a + w)
    g8 = R("BO", 0, 128, 16)
    row = lambda a, w: R("ROW", a, a + w, 1, 0, 1)
    lone = R("ONEB", 0, 128, 1, 0, 1)
    one = R("ONE")
    half = lambda b, h: R(b, 2048 * h, 2048 * h + 2048)
    part = lambda b, j: R(b, 1024 * j, 1024 * j + 1024)
    hv = lambda b, h, o=0: R(b, o + 128 * h, o + 128 * h + 128)
    wide = lambda b, lo, w: I(b, lo, lo + w, "SOF", 0, w)
    again = lambda b, lo, k: I(b, lo, lo + 16, "SRP", 0, k)

    def wrap(a, cols, em, eo, bank, lo):
        tt(R(em, eo, eo + 16 * cols), wide("SM", 16 * a, cols), R("QM", 0, 16 * cols), A.mult)
        for h in range(cols // 8):
            mm(R(bank, lo + 8 * h, lo + 8 * h + 8), R(em, eo + 128 * h, eo + 128 * h + 128), R("RB"), True, True)
        return R(bank, lo, lo + cols)

    def moved(o, ids, e, a=0, z=256):
        none(e, ids)
        tt(e, R("DUM", a, z), e, A.mult)
        tt(o, ids, e, A.add)

    def spread():
        for j in range(4):
            scan(R("VAL", 1024 * j, 1024 * j + 1024), R("RM", 0, 1024), R("XE2", 1024 * j, 1024 * j + 1024), A.mult, A.add)

    def settle(mv, how, a=0, z=4096):
        for j in range(a, z, 512):
            how(I("OW", 0, NO, mv, j // 16, j // 16 + 32), R("VAL", j, j + 512))

    def owners(u):
        mv = ("MVO", "OFD")[u % 2]
        for a, z in ((0, 128), (128, 256)) if u == 1 else ((0, 256),):
            moved(R("EQ2", a, z), R("ML", u + 4 * a, 4 * z, 4), R("B3", a, z), a, z)
            tc(R(mv, a, z), R("EQ2", a, z))
        if u == 1:
            tc(R("EMA"), R("TB", NE + u, NE + 1024, 4))
            for j in range(4):
                cp(R("VAL", 1024 * j, 1024 * j + 1024), wide("EMA", 64 * j, 64))
        else:
            was = (u - 1) % 4
            for h in range(2):
                plane = lambda k: T.VAL[k:128:16, 2048 * h:2048 * h + 2048]
                dma("dp%d" % (2 * was - 2 + h), [(plane(2 + u), plane(6)), (plane(2 + was), plane(2 + (u + 1) % 4))], half("VAL", h)[1], half("VAL", h)[1])
        settle(mv, put)

    def numbers(bank, lo, src, cols, wq="WQ"):
        for q in range(16):
            mm(R(bank, lo, lo + cols), R(wq, 128 * q, 128 * q + 128), R(src, q, 16 * cols, 16), q == 0, q == 15)
        return R(bank, lo, lo + cols)

    mi = R("MI")
    qi = R("SJ", 112, 128)
    iota(qi, [[-1, 16]], 1024, 1)
    ts(qi, qi, 15, A.bitwise_and)
    ts(R("QF"), qi, 0, A.is_equal)
    ts(R("QM", 0, 16), qi, 0, A.is_equal)
    for w in (16, 32, 64, 128):
        tc(R("QM", w, 2 * w), R("QM", 0, w))
    iota(R("SJ", 0, 80), [[1, 80]], 0, 0)
    tc(R("SOF"), R("SJ", 0, 80))
    for h in range(2):
        dma("dm%d" % h, [(T.MI[:, 512 * h:512 * h + 512], T.ml[:, 512 * h:512 * h + 512])], [], R("MI", 512 * h, 512 * h + 512)[1])
    ms(R("X", 0, 16), -16.0)
    ms(R("X", 4096, NX), 0.0)
    ms(R("AC", 0, 8), -1)
    ms(R("AC", 4096, NX), -1)
    dma("dx", [(T.X[:, 1:4097], T.x0[:, :])], [], R("X", 1, 4097)[1])
    dma("da", [(T.AC[:, 1 + 1024 * j:1025 + 1024 * j], T.ac[:, :]) for j in range(4)], [], R("AC", 1, 4097)[1])
    dma("dl", [(T.LMI[:], T.lims[:, :])], [], R("LMI")[1])
    dma("dw", [(T.WTI[:], T.wt[:, :])], [], R("WTI")[1])
    iota(R("DUM"), [[16, 256]], D0, 1)
    ms(R("OW", 0, 528), 128.0)
    for w in (512, 1024, 2048):
        act(R("OW", 16 + w, 16 + 2 * w), R("OW", 16, 16 + w), F.Copy)
    fill(R("XE", 0, 512), 0)
    dma("dz", [(T.XE[:, w:w + 512], T.XE[:, 0:512]) for w in range(512, 4096, 512)], R("XE", 0, 512)[1], R("XE", 512, 4096)[1])
    ms(R("RM", 0, 256), 1.0)
    ms(R("RM", 0, 256, 16), 0.0)
    dma("dr", [(T.RM[:, w:w + 256], T.RM[:, 0:256]) for w in range(256, 1024, 256)], R("RM", 0, 256)[1], R("RM", 256, 1024)[1])
    ms(one, 1.0)
    pl, cj = R("W0", 0, 320), R("W0", 320, 640)
    iota(pl, [[1, 40], [0, 8]], 0, 0)
    iota(cj, [[0, 40], [1, 8]], 0, 0)
    cols(cj, cj, q_(1), 128.0)
    cols(pl, pl, q_(0), 0.0)
    tt(pl, pl, cj, A.add)
    tt(R("SM", 4, 5), q_(2), q_(3), A.add)
    tt(R("SM", 5, 6), q_(4), q_(5), A.add)
    tt(R("SM", 4, 5), R("SM", 4, 5), R("SM", 5, 6), A.add)
    for u in range(4):
        ts(R("SM", 8 + u, 9 + u), q_(2 + u), R("SM", 4, 5), A.subtract, 128.0, A.mult)
        cols(R("TB", NE + u, NE + 1280, 4), pl, 1.0, R("SM", 8 + u, 9 + u))
    ml = R("ML", 0, 1024)
    for h in range(2):
        a, b = R("MI", 512 * h, 512 * h + 512), R("B%d" % h)
        ts(b, a, 4096, A.is_equal, -4097, A.mult)
        tt(b, a, b, A.add)
        lin(R("ML", 512 * h, 512 * h + 512), b, 1.0, 1.0)
    fill(R("ML", 1024, 1280), 0)
    sign(R("IND"), ml)
    for u in range(1, 4):
        owners(u)
    for b in ("VS", "XVS", "MVA"):
        fill(R(b), 0)
    for b, c in (("IDF", 1.0), ("IDK", 2048.0), ("IXS", 2.0 ** -11)):
        diag(R(b), R("MVA", 0, 128), c)
    for b, c in (("IDB", 1.0), ("NID", -1.0), ("ID4", 4.0), ("IDV", float(2 ** 18))):
        diag(R(b), R("VS", 0, 128), c)
    for b in ("ONEB", "BO", "RB"):
        fill(R(b), 1)
    bounded(R("BO"), [[-16, 8], [0, 16]], 0, 1, 16)
    bounded(R("RB"), [[-16, 8]], 0, 1, 16)
    aff(R("TRI"), R("ONEB"), [[1, 128]], A.is_gt, 0.0, 0, -1)
    aff(R("TSB"), R("BO"), [[-1, 128]], A.is_ge, 0.0, 0, 1)
    for b, c in ((R("G16"), 16.0), (R("G1K"), 1024.0), (R("G64"), 65536.0), (R("G512", 0, 8), 512.0), (R("G512", 8, 16), 512.0)):
        ts(b, g8, c, A.mult)
    for j in range(4):
        aff(hv("SH", j), R("MVA", 0, 128), [[1, 128]], A.not_equal, 1.0, -2 ** j, -1)
        bounded(hv("SH", j), [[-16, 8], [0, 16]], 0, 1, 16)
        diag(hv("SH", j), hv("SH", j), -1.0)
    aff(R("JR"), R("MVA"), [[-16, 8], [1, 16]], A.not_equal, 1.0, -15, 1)
    iota(R("KC"), [[0, 16], [-1, 16]], 16, 0)
    iota(R("ZI", 0, 128), [[0, 8], [4369, 16]], 0, 0)
    for j, bits in enumerate((4608, 72)):
        ts(R("ZI", 128, 256), R("ZI", 0, 128), bits, A.bitwise_and)
        ts(R("ROW", 1152 + 128 * j, 1280 + 128 * j), R("ZI", 128, 256), -2048.0, A.mult)
    fill(R("GS0"), 0)
    mark(R("GS0"), 0, 1.0)
    for o, w, pat, base in ((0, 128, [[0, 8], [4096, 16]], 0), (128, 128, [[0, 8], [1, 16]], 0), (256, 256, [[0, 16], [-1, 16]], 15),
                            (512, 128, [[0, 128]], -1), (640, 256, [[-384, 2], [0, 8], [32, 16]], -128),
                            (896, 256, [[-384, 2], [0, 8], [32, 16]], -128)):
        iota(R("ROW", o, o + w), pat, base, 0)
    iota(R("SJ", 96, 100), [[0, 4]], 0, 1)
    ts(R("SJ", 96, 100), R("SJ", 96, 100), 15, A.bitwise_and)
    tc(R("SRP"), R("SJ", 96, 100))
    ts(R("SJ", 97, 98), R("SJ", 96, 97), 1, A.add)
    for j in range(4):
        ts(R("SJ", 100, 102), R("SJ", 96, 98), j, A.logical_shift_right, 1, A.bitwise_and)
        tt(R("LMB", 6, 7), R("SJ", 101, 102), R("SJ", 100, 101), A.subtract)
        ts(hv("BW", j), R("BO"), R("LMB", 6, 7), A.mult)
    fill(R("BM"), 0)
    ms(R("BM", 0, 512, 16), float(2 ** 25))
    wc = R("SM", 0, 1)
    low = [(1, 4.0)] + [(2 + u, u / 128) for u in range(1, 4)]
    fill(R("GW"), 0)
    fill(R("GC"), 0)
    for k, c in low + [(0, 32.0), (6, -36.0)]:
        mark(R("GW", 0, 8), k, c)
    addup(wc, R("GW", 0, 8))
    for u in range(4):
        for j, ws in enumerate(([(0, 1.0)], low)):
            for k, c in [x for x in ws if x[0] != 2 + u] + [(2 + u, float(2 ** 15))]:
                mark(R("GC", 16 * u + 8 * j, 16 * u + 8 * j + 8), k, c)
    lanes = lambda o, base, s: iota(o, [[128 * s, 2], [0, 8]], base, s)
    lanes(C(0), 4096, 1)
    lanes(C(1), 15, 16)
    lanes(C(2), 11 * 2 ** 18, -1)
    ts(R("LMF", 6, 8), R("CO", 32, 48, 8), -1.0, A.mult)
    lanes(C(3), 1024, 1)
    lanes(C(4), 64, 1)
    iota(R("ROW", 1408, 1472), [[16, 64]], 0, 0)
    for j, base in enumerate((512, NE + 1024)):
        lanes(R("BAS", 16 * j, 16 * j + 16), base, 1)
    iota(R("CIW", 0, 64), [[16, 64]], 0, 0)
    tc(R("SM", 6, 7), R("SJ", 96, 97))
    ts(R("CIW", 0, 64), R("CIW", 0, 64), R("SM", 6, 7), A.add)
    ts(R("CIW", 64, 128), R("CIW", 0, 64), -1.0, A.mult, 1023.0, A.add)
    aff(R("WQ"), R("XE", 2048, 4096), [[1, 16], [0, 8], [-1, 16]], A.not_equal, 1.0, 0, 0)
    bounded(R("WQ"), [[0, 16], [-16, 8], [0, 16]], 0, 1, 16)
    for k in range(11):
        mark(R("GW", 8, 16), k, float(2 ** (10 - k)))
    addup(R("LMF", 0, 1), R("GW", 8, 16))
    ts(R("LMF", 5, 6), R("LMF", 0, 1), 0.0, A.is_gt, -512.0, A.mult)
    iota(R("CT"), [[1, 1040]], 0, 0)
    ts(R("CT"), R("CT"), R("LMF", 0, 1), A.mult)
    ts(R("CT"), R("CT"), 1024, A.bitwise_and)
    for a in (0, 1):
        addup(R("LMF", 1 + a, 2 + a), R("RB", a, 8, 2))
        tt(R("LMB", 4 + a, 5 + a), R("LMF", 1 + a, 2 + a), q_(15), A.mult)
        tt(R("LMB", 2 + a, 3 + a), R("LMF", 1 + a, 2 + a), R("LMB", 4 + a, 5 + a), A.subtract)
    iota(R("K1"), [[-1, 256]], 0, 0)
    cols(R("CN"), R("K1"), q_(15), R("LMF", 5, 6))
    tc(R("SM", 12, 14), R("LMI"))
    for j in range(2):
        ts(R("VM", 128 * j, 128 * j + 128), one, R("SM", 12 + j, 13 + j), A.mult)
        for h in range(2):
            mm(R("B2", 16 * j + 8 * h, 16 * j + 8 * h + 8), R("VM", 128 * j, 128 * j + 128), R("GS0"), True, True)
    tc(R("LIM", 0, 32), R("B2", 0, 32))
    tc(R("LIM", 32, 48), R("LIM", 0, 16))
    fill(R("W1"), 0)
    for u in range(4):
        fill(R("ME%d" % u, 64, 336), 192)
    fill(R("ALT"), 128)
    tc(R("LMB", 0, 1), R("WTI"))
    tc(R("LMB", 1, 2), wc)
    ts(R("WT"), R("WQ"), R("LMB", 0, 1), A.mult)
    ts(R("WB"), R("BO"), R("LMB", 0, 1), A.mult)
    aff(R("WE"), R("WQ"), [[0, 16], [-16, 8], [0, 16]], A.is_equal, 0.0, 0, 1)
    ts(R("WQ"), R("WQ"), R("LMB", 1, 2), A.mult)
    (NN, LIVE, LS, LB, SUU, GRL, N16, HAS, FM, DD, T1, T2, T3, OK, SPL, RK, NV, MN, RK2, IDL, VIS, T4, LV, E1, E2, E3) = range(2, 28)
    AV, BV, TA, TB2, LL = 28, 30, 32, 34, 36
    EU = 41
    for a, c in ((AV, -512), (BV, -256)):
        fill(S(a), c)

    def empties():
        tc(R("OCB"), numbers("B7", 0, "IND", 64, "WE"))
        mm(R("B7", 64, 128), R("BO"), R("OCB"), True, True)
        mm(R("B7", 128, 192), R("TSB"), R("OCB"), True, True)
        u, y = S(EU, 64), S(EU + 4, 64)
        scan(u, R("ONE", 0, 64), R("B7", 64, 128), A.mult, A.add)
        ts(S(E1, 1), R("SM", 16 * EU + 63, 16 * EU + 64), -1.0, A.mult, 1024.0, A.add)
        ts(R("NVB"), R("GS0"), S(E1, 1), A.mult)
        tt(u, R("CIW", 0, 64), u, A.subtract)
        tt(u, u, R("B7", 128, 192), A.add)
        tt(y, R("CIW", 64, 128), u, A.add)
        tt(y, y, R("OCB"), A.mult)
        tt(u, u, y, A.max)
        tc(R("LST", 64, 128), u)
        for h in range(2):
            mm(R("B7", 192 + 8 * h, 200 + 8 * h), R("ONEB"), R("NVB"), True, True)
        cp(S(NV), R("B7", 192, 208))
        for j in range(2):
            put(I("TB", 0, NE, "LST", 64 + 32 * j, 96 + 32 * j), R("TB", NE + 512 * j, NE + 512 * j + 512))

    def squares(w, bank, kk):
        for j in range(2):
            o = R(bank, 256 * j, 256 * j + 256)
            mm(o, R("IDB"), R("TX", 2 * kk + j, 4096, 16), True, False)
            mm(o, R("NID"), w, False, True)
        act(R("SQ", 512 * kk, 512 * kk + 512), R(bank), F.Square)

    def members(t):
        own = lambda h, b="ML": R(b, t + 512 * h, t + 512 * h + 512, 4)
        xs, ls = R("XS%d" % (t % 2)), 16 * (t % 2)
        tc(R("OFO"), R("ML", t, 1024, 4))
        for j in range(8):
            cp(R("TX", 512 * j, 512 * j + 512), I("X", 0, NX, "OFO", 32 * j, 32 * j + 32))
        for h in range(2):
            o = hv("B0", h)
            mm(o, own(h), R("IDF"), True, False)
            mm(o, lone, row(0, 128), False, False)
            mm(o, lone, row(512, 128), False, False)
            for k in range(16):
                mm(R("B0", 128 * h + k, 128 * h + 128, 16), R("TX", 2048 * h + k, 2048 * h + 2048, 16), R("G64"), False, k == 15)
        act(R("K1"), R("B0", 0, 256), F.Abs)
        for h in range(2):
            mm(R("B2", 8 * h, 8 * h + 8), own(h, "IND"), g8, True, True)
        tc(S(NN), R("B2", 0, 16))
        ts(S(LIVE), S(NN), 0.0, A.is_gt)
        scan(R("KM"), R("BM", 0, 256), R("K1"), A.max, A.min)
        tc(R("SI", 0, 16), R("KM", 15, 256, 16))
        ts(R("SI", 16, 32), R("SI", 0, 16), 4095, A.bitwise_and)
        tt(S(SUU), S(LIVE), C(0), A.mult)
        tt(S(SUU), C(0), S(SUU), A.subtract)
        tt(S(LS), R("SI", 16, 32), S(SUU), A.max)
        ts(R("LST", ls, ls + 16), wrap(LS, 16, "EMA", 0, "B0", 256), 1.0, A.add)
        tc(xs, I("X", 0, NX, "LST", ls, ls + 16))
        ts(R("ACO"), I("AC", 0, NX, "LST", ls, ls + 16), 1, A.add)
        tc(R("XE", 0, 4096, 16), xs)
        for j in range(4):
            scan(part("XSE", j), R("RM"), part("XE", j), A.mult, A.add)
        ts(R("SI", 32, 48), R("SI", 0, 16), 16, A.logical_shift_right)
        for j in range(4):
            scan(part("US", j), R("RM"), part("TX", j), A.mult, A.max)
        aside(R("UC"), R("US", 15, 4096, 16))
        for h in range(2):
            mm(R("B2", 16 + 8 * h, 24 + 8 * h), hv("UC", h), g8, True, True)
        tt(S(GRL), R("B2", 16, 32), R("SI", 32, 48), A.subtract)
        tt(S(GRL), S(GRL), R("LIM", 16, 32), A.is_gt)
        for kk in range(8):
            squares(xs, ("B4", "B5")[kk % 2], kk)
        for h in range(2):
            o = hv("B0", h, 256)
            mm(o, own(h, "IND"), R("IDV"), True, False)
            mm(o, lone, row(256, 128), False, False)
            for k in range(16):
                mm(R("B0", 256 + 128 * h + k, 384 + 128 * h, 16), R("SQ", 256 * k + 128 * h, 256 * k + 128 * h + 128), R("G16"), False, k == 15)
        scan(R("KB"), R("RM", 0, 256), R("B0", 256, 512), A.mult, A.max)
        lin(R("KBC"), R("B0", 256, 512), 1.0, -float(2 ** 18))
        tc(R("SI", 48, 64), R("KB", 15, 256, 16))
        ts(R("SI", 48, 64), R("SI", 48, 64), 15, A.bitwise_and)
        tt(S(LB), C(1), R("SI", 48, 64), A.subtract)
        tc(R("LST", 32, 48), wrap(LB, 16, "EMA", 0, "B0", 0))
        tc(R("XB"), I("TX", 0, 4096, "LST", 32, 48))
        for kk in range(8):
            squares(R("XB"), ("B4", "B5")[kk % 2], kk)
        mm(R("B6", 0, 256), lone, row(256, 256), True, False)
        for k in range(16):
            for h in range(2):
                mm(R("B6", 128 * h + k, 128 * h + 128, 16), R("SQ", 256 * k + 128 * h, 256 * k + 128 * h + 128), R("G16"), False, k == 15 and h == 1)
        tt(R("MM", 256, 512), R("KBC"), R("B6", 0, 256), A.is_gt)
        lin(R("MM", 0, 256), R("MM", 256, 512), -1.0, 1.0)
        mm(R("B6", 256, 512), R("ID4"), R("MM", 256, 512), True, False)
        for h in range(2):
            mm(hv("B6", h, 256), own(h), R("IXS"), False, h == 1)
        zi = R("ZI", 0, 256)
        scan(R("TH2"), R("RM", 0, 256), R("MM", 0, 256), A.mult, A.add)
        if t == 0:
            ts(S(SUU), R("TH2", 15, 256, 16), 15.0, A.min, -15.0, A.add)
            tt(S(SUU), S(SUU), C(1), A.add)
            tc(R("LST", 176, 192), wrap(SUU, 16, "EMA", 0, "B2", 224))
        tt(R("B4", 0, 256), R("MM", 256, 512), R("KC"), A.mult)
        tt(R("TH2"), R("TH2"), R("B4", 0, 256), A.add)
        ts(zi, R("TH2"), -1.0, A.add, 4369.0, A.mult)
        ts(zi, zi, 4680, A.bitwise_and)
        tt(R3("W", 0, 16, 0, 16), zi, R("B6", 256, 512), A.add)
        for a, b in (("W", "WW"), ("WW", "W")) * 2:
            for k, f in ((0, A.min), (8, A.max)):
                tt(R3(b, 0, 16, k, k + 8), R3(a, 0, 16, 0, 16, 2), R3(a, 0, 16, 1, 16, 2), f)
        p = R("B5", 0, 256)
        for h in range(2):
            mm(hv("B5", h), row(1152, 128), lone, True, False)
            mm(hv("B5", h), row(1280, 128), lone, False, False)
            mm(hv("B5", h), R3("W", 8 * h, 8 * h + 8, 0, 16), R("IDK"), False, True)
        relu(R("LR"), p, -8192.0)
        mm(R("B4", 256, 512), R("JR"), R("LR"), True, True)
        cp(R("W1", 256, 512), R("B4", 256, 512))
        none(R("KBC"), R("LR"))
        tt(R("W0", 256, 512), R("KBC"), p, A.mult)
        if t == 0:
            tt(R("W2", 256, 512), R("W0", 256, 512), R("LR"), A.add)
            aside(R("W2", 512, 768), R("ML", t, 1024, 4))
            aside(R("WP", 512, 768), R("TB", NE + t, NE + 1024, 4))
        elif t < 3:
            moved(R("W2", 256, 512), R("LR"), R("B6", 0, 256))
        aside(R("W0", 512, 768), R("ML", t, 1024, 4))
        aside(R("WP", 0, 256), R("TB", NE + t, NE + 1024, 4))
        if t:
            aside(R("PCF"), R("TB", NE + t, NE + 1024, 4))

    empties()
    members(0)
    for t in range(4):
        own = lambda h, b="ML": R(b, t + 512 * h, t + 512 * h + 512, 4)
        xs, ls = R("XS%d" % (t % 2)), 16 * (t % 2)
        la = 128 + 16 * (t % 2)
        for j in range(8):
            cp(R("OWG", 512 * j, 512 * j + 512), I("OW", 0, NO, "ACO", 32 * j, 32 * j + 32))
        for j in range(8):
            xa = R("XA", 512 * j, 512 * j + 512)
            tt(xa, I("X", 0, NX, "ACO", 32 * j, 32 * j + 32), R("XSE", 512 * j, 512 * j + 512), A.subtract)
            act(xa, xa, F.Square)
        mm(R("B1"), lone, row(640, 512), True, False)
        for b, w in (("OWG", R("GC", 16 * t, 16 * t + 16)), ("XA", R("G512"))):
            for h in range(2):
                for k in range(16):
                    mm(R("B1", 256 * h + k, 256 * h + 256, 16), R(b, 2048 * h + k, 2048 * h + 2048, 16), w, False, b == "XA" and h == 1 and k == 15)
        scan(R("KD"), R("BM"), R("B1"), A.max, A.min)
        sk, sl = R3("SK", 0, 2, 0, 16), R3("SL", 0, 2, 0, 16)
        tc(sk, R("KD", 15, 512, 16))
        ts(sl, sk, 31, A.bitwise_and)
        ts(R("SI", 80, 96), R3("SK", 0, 2, 0, 8), 12, A.logical_shift_right, 1024, A.bitwise_and)
        ts(S(DD), R3("SL", 0, 2, 0, 8), 32.0, A.mult)
        tt(S(T1), R3("SL", 0, 2, 8, 16), R("SI", 80, 96), A.add)
        tt(S(DD), S(DD), S(T1), A.add)
        ts(R("LST", 48, 64), wrap(DD, 16, "EMB", 0, "B2", 32), 1024.0, A.min)
        tc(R("MD"), I("ML", 0, 1280, "LST", 48, 64))
        tc(R("OFD"), R("MD"))
        for j in range(8):
            cp(R("TD", 512 * j, 512 * j + 512), I("X", 0, NX, "OFD", 32 * j, 32 * j + 32))
        sign(R("INDD"), R("MD"))
        ts(S(HAS), S(DD), 1024.0, A.is_lt)
        tt(S(AV + 1), S(DD), C(3), A.subtract)
        tt(R("CF", 0, 256), I("CT", 0, 1040, "LST", 48, 64), R("CN"), A.add)
        for a in (0, 1):
            ts(R("CF", 256 + 256 * a, 512 + 256 * a), R("CF", 0, 256), R("LMB", 2 + a, 3 + a), A.mult, R("LMB", 4 + a, 5 + a), A.add)
        for i in range(6):
            b = ("B3", "B7")[i % 2]
            if i < 2:
                h, gs, wd = 0, range(4 * i, 4 * i + 4), 128
            else:
                h, gs, wd = 1, range(2 * (i - 2), 2 * (i - 2) + 2), 256
            for j, gg in enumerate(gs):
                p0 = 32 * (gg // 2)
                c = 256 + 256 * (gg % 2) + 128 * h
                mm(R(b, wd * j, wd * j + wd), R("CF", c, c + 128, 1, p0, p0 + 32), R("CF", 0, wd, 1, p0, p0 + 32), True, True,
                   j > 0 and p0 != 32 * (gs[j - 1] // 2))
            for j, gg in enumerate(gs):
                over(R("SM", 16 * FM + 8 * h + gg, 16 * FM + 8 * h + gg + 1), R(b, wd * j, wd * j + wd), R("LMF", 6 + h, 7 + h), R("FS", wd * j, wd * j + wd))
        w, p = R("MD"), R("B0", 0, 256)
        for j in range(4):
            mm(R("B0", 256, 512), hv("BW", j), R("IND", t, 1024, 4), True, True)
            if j:
                w = R("MW")
                cp(w, p)
            tt(R("MA"), w, R("B0", 256, 512), A.mult)
            mm(p, R("IDF"), w, True, False)
            mm(p, hv("SH", j), R("MA"), False, True)
        tt(R("W0", 0, 256), R("W0", 512, 768), p, A.add)
        if t == 0:
            tt(R("W2", 0, 256), R("W0", 512, 768), p, A.add)
        elif t < 3:
            moved(R("W2", 0, 256), R("MD"), R("B2", 256, 512))
        for h in range(2):
            mm(R("B2", 48 + 8 * h, 56 + 8 * h), hv("INDD", h), g8, True, False)
            mm(R("B2", 48 + 8 * h, 56 + 8 * h), own(h, "IND"), g8, False, True)
        ts(S(T2), R("B2", 48, 64), 16.0, A.is_le)
        tt(S(T2), S(T2), S(HAS), A.mult)
        for h in range(2):
            for k in range(15):
                mm(R("B1", 128 * h + k, 128 * h + 128, 16), R("TD", 2048 * h + k, 2048 * h + 2048, 16), g8, True, True)
        act(R("KA"), R("B1", 0, 256), F.Abs)
        for h in range(2):
            tc(R("TD", 2048 * h + 15, 2048 * h + 2048, 16), hv("UC", h))
            for j in (2 * h, 2 * h + 1):
                scan(part("UD", j), R("RM"), part("TD", j), A.mult, A.max)
            mm(R("B2", 64 + 8 * h, 72 + 8 * h), R("UD", 2048 * h + 15, 2048 * h + 2048, 16), g8, True, True)
        scan(R("MSD"), R("BM", 0, 256), R("KA"), A.max, A.min)
        tt(S(T3), R("SI", 32, 48), R("MSD", 14, 256, 16), A.min)
        tt(S(T3), S(T3), R("LIM", 32, 48), A.add)
        tt(S(OK), S(T2), S(FM), A.is_gt)
        tt(S(T3), S(T3), R("B2", 64, 80), A.is_ge)
        mer, want, nm = R("SB", 0, 16), R("SB", 16, 32), R("SB", 32, 48)
        tt(mer, S(T3), S(OK), A.mult)
        tt(want, S(GRL), mer, A.is_gt)
        tt(nm, S(LIVE), mer, A.subtract)
        mm(R("B2", 80, 112), R("TRI"), R("SB", 16, 48), True, False)
        mm(R("B2", 88, 96), R("ONEB"), R("SB", 16, 24), False, False)
        mm(R("B2", 104, 112), R("ONEB"), R("SB", 32, 40), False, True)
        tt(S(TA, 32), again("SB", 0, 2), S(AV, 32), A.mult)
        tt(S(TA, 32), S(TA, 32), R("BAS"), A.add)
        tt(S(MN), S(NV), R("B2", 80, 96), A.min)
        tt(S(RK2), R("B2", 96, 112), S(MN), A.subtract)
        tt(S(SPL), S(NV), R("B2", 80, 96), A.is_gt)
        tt(S(SPL), S(SPL), want, A.mult)
        tt(S(IDL), nm, S(SPL), A.subtract)
        ts(S(VIS), S(RK2), 64.0, A.is_lt)
        tt(S(T4), S(RK2), C(4), A.subtract)
        tt(S(VIS), S(VIS), S(IDL), A.mult)
        tt(S(T4), S(T4), S(VIS), A.mult)
        tt(S(LL + 4), S(T4), C(4), A.add)
        tt(S(BV + 1), R("B2", 80, 96), R("BAS", 16, 32), A.subtract)
        tt(S(TB2, 32), again("SM", 16 * SPL, 2), S(BV, 32), A.mult)
        tt(S(LL, 32), S(TA, 32), S(TB2, 32), A.add)
        tc(R("LST", la, la + 16), wrap(LL + 4, 16, "EMW", 512, "B2", 112))
        dst = (rank + 1 + t % (n - 1)) % n
        src = (rank - 1 - t % (n - 1)) % n
        tc(I("VS", 0, 336, "LST", la, la + 16), xs)
        send(dst, "XV%d" % t, "VS", "va%d" % t, "vl%d" % t)
        tc(R("LST", 208, 224), wrap(LL + 1, 16, "EMW", 256, "B2", 176))
        tc(R("LST", 160, 176), wrap(LL, 16, "EMW", 0, "B2", 128))
        tc(R("TG"), I("TB", 0, NE + 1280, "LST", 208, 224))
        tc(R("LST", 224, 240), numbers("B2", 192, "TG", 16))
        tc(R("ML", t, 1024, 4), I("W0", 0, 768, "LST", 160, 176))
        tc(R("L2"), I("W1", 0, 768, "LST", 160, 176))
        tc(I("ML", 0, 1280, "LST", 224, 240), R("L2"))
        early = t > 0
        if early:
            tc(R("XE2", 0, 4096, 16), I("WP", 0, 768, "LST", 160, 176))
            aside(R("ALT", t, 1024, 4), R("XE2", 0, 4096, 16))
            put(I("ALT", 0, 1280, "LST", 224, 240), R("PCF"))
        else:
            tc(R("XE2", 0, 4096, 16), R("WP", 0, 256))
            tt(R("VM"), I("WP", 0, 768, "LST", 160, 176), R("XE2", 0, 4096, 16), A.subtract)
            tc(I("XE2", 0, 4096, "LST", 176, 192), R("VM"))
        xv = "XV%d" % t
        tc(R("SJ", 0, 4), numbers("B1", 128, xv, 4, "WT"))
        if early:
            mm(R("B1", 192, 256), R("WB"), R(xv), True, True)
        ts(R("SJ", 0, 4), R("SJ", 0, 4), 4095, A.bitwise_and)
        ts(R("LST", 240, 244), R("SJ", 0, 4), 1, A.add)
        if t == 3:
            tc(R("OVG"), I("OW", 0, NO, "LST", 240, 244))
        if t < 3:
            if early:
                tc(R("MVO"), I("W2", 0, 768, "LST", 160, 176))
            else:
                tc(R("EQ2"), I("W2", 0, 768, "LST", 160, 176))
                moved(R("EQ2"), R("EQ2"), R("B6", 0, 256))
                tc(R("MVO"), R("EQ2"))
                aside(R("W2", 512, 768), R("DUM"))
            spread()
            if not early:
                tc(I("XE2", 0, 4096, "LST", 176, 192), R("W1", 0, 256))
            at = 512 if early else 4096
            settle("MVO", lambda o, i: act(o, i, F.Silu), 0, at)
            tc(R("OVG"), I("OW", 0, NO, "LST", 240, 244))
            settle("MVO", lambda o, i: act(o, i, F.Silu), at, 4096)
            mm(R("B2", 208, 224), R("ONEB"), mer, True, True)
            addup(S(E2, 1), R("B2", 208, 224))
            tc(R("SI", 96, 97), S(E2, 1))
            ts(R("SI", 96, 97), R("SI", 96, 97), 15, A.bitwise_and)
            tc(S(E2, 1), R("SI", 96, 97))
            ts(R("LIM", 32, 48), R("LIM", 0, 16), S(E2, 1), A.add)
            for u in range(1, 5):
                sign(R("IND", (t + u) % 4, 1024, 4), R("ML", (t + u) % 4, 1024, 4))
            empties()
            members(t + 1)
        else:
            ym = R("YM", 0, 1024)
            for h in range(2):
                a, b, y = R("ML", 512 * h, 512 * h + 512), R("B%d" % (4 + h)), R("YM", 512 * h, 512 * h + 512)
                relu(b, a, 4097.0, -4097.0)
                lin(y, a, 1.0, -1.0)
                tt(y, y, b, A.add)
            dma("oy", [(T.ym[:, :], ym[0])], ym[1], [])
        if early:
            tc(R("SJ", 64, 128), R("B1", 192, 256))
            ts(R("SJ", 64, 128), R("SJ", 64, 128), 4095, A.bitwise_and)
            ts(R("VF"), R("SJ", 64, 128), 1, A.add)
        aside(R("XVS", 0, 1024, 16), R(xv))
        scan(R("XVE"), R("RM", 0, 1024), R("XVS"), A.mult, A.add)
        tc(R("LST", 244, 248), numbers("B1", 132, "OVG", 4))
        if early:
            tc(R("AVG"), I("ALT", 0, 1280, "LST", 244, 248))
            tc(R("HL1"), I("ML", 0, 1280, "LST", 244, 248))
            tc(R("LST", 248, 252), numbers("B1", 136, "AVG", 4))
            tt(R("EQV"), R("HL1"), R("VF"), A.is_equal)
            mm(R("B1", 256, 320), R("BO"), R("EQV"), True, True)
            tc(R("HL2"), I("ML", 0, 1280, "LST", 248, 252))
            tt(R("HL1"), R("HL1"), R("HL2"), A.subtract)
            tt(R("HL1"), R("HL1"), R("B1", 256, 320), A.mult)
            tt(R("HL1"), R("HL1"), R("HL2"), A.add)
            tc(R("HL"), R("HL1"))
        else:
            tc(R("HL"), I("ML", 0, 1280, "LST", 244, 248))
        for h in range(2):
            vd = R("VD", 512 * h, 512 * h + 512)
            tt(vd, I("X", 0, NX, "HL", 32 * h, 32 * h + 32), R("XVE", 512 * h, 512 * h + 512), A.subtract)
            act(R("SQV", 512 * h, 512 * h + 512), vd, F.Square)
        mm(R("B1", 0, 128, 1, 0, 64), R("ONEB", 0, 64, 1, 0, 1), row(128, 128), True, False)
        mm(R("B1", 0, 128, 1, 0, 64), row(1408, 64), lone, False, False)
        for k in range(16):
            mm(R("B1", k, 128, 16, 0, 64), R("SQV", k, 1024, 16), R("G1K"), False, k == 15)
        scan(R("KV", 0, 128, 1, 0, 64), R("BM", 0, 128, 1, 0, 64), R("B1", 0, 128, 1, 0, 64), A.max, A.min)
        tc(R("SJ", 8, 16, 1, 0, 64), R("KV", 15, 128, 16, 0, 64))
        ts(R("SJ", 8, 16, 1, 0, 64), R("SJ", 8, 16, 1, 0, 64), 1023, A.bitwise_and)
        tt(R("EMV"), wide("SJ", 8, 8), R("QM", 0, 128), A.mult)
        mm(R("B1", 140, 144), R("EMV", 0, 128, 1, 0, 64), R("RB", 0, 4, 1, 0, 64), True, True)
        tc(R("LST", 252, 256), R("B1", 140, 144))
        ts(R("RET"), I("VD", 0, 1024, "LST", 252, 256), 0.5, A.mult, 191.75, A.add)
        send(src, "ME%d" % t, "RET", "ra%d" % t, "rl%d" % t)
        lin(R("NX0"), xs, 1.0, -192.0)
        tt(R("NX1"), I("ME%d" % t, 0, 336, "LST", la, la + 16), R("NX0"), A.add)
        tc(I("X", 0, NX, "LST", ls, ls + 16), R("NX1"))
    dma("ox", [(T.yx[:, :], T.X[:, 1:4097])], R("X", 1, 4097)[1], [])

    if "order" not in PLAN:
        PLAN["order"] = plan(calls)
    count = {}
    known = {q: {} for q in queue}
    seen = {}
    for i, q in PLAN["order"]:
        c = calls[i]
        e = c["sem"] or q
        if q == "x":
            count[e] = -c["inc"]
            seen[i] = (e, count[e], {e: count[e]})
            continue
        best = {}
        for j, inline in c["dep"].items():
            if not inline and best.get(seen[j][0], (0,))[0] < seen[j][1]:
                best[seen[j][0]] = seen[j][1:]
        for k, (v, ck) in sorted(best.items(), key=lambda x: -x[1][0]):
            if known[q].get(k, 0) < v:
                queue[q].wait_ge(T.sem[k], v)
                for a, b in ck.items():
                    known[q][a] = max(known[q].get(a, 0), b)
        x = c["f"][q]()
        if c["inc"] > 0:
            x.then_inc(T.sem[e], 16 if q == "y" else 1)
        count[e] = count.get(e, 0) + abs(c["inc"])
        ck = dict(known[q])
        ck[e] = count[e]
        seen[i] = (e, count[e], ck)
    for k in SEMAPHORES[:18]:
        g.sync.wait_ge(T.sem[k], count[k])
    for t in range(4):
        for k in ("vl", "rl"):
            g.wait_ge(T.sem["%s%d" % (k, t)], count["%s%d" % (k, t)])
